import numpy as np
import ml_dtypes


def mxq(x, axis, fmt="e4m3"):
    dtype, down = {"e4m3": (ml_dtypes.float8_e4m3fn, 7), "e5m2": (ml_dtypes.float8_e5m2, 14)}[fmt]
    v = np.moveaxis(np.asarray(x, np.float32).astype(ml_dtypes.bfloat16).astype(np.float64), axis, -1)
    blocks = v.reshape(v.shape[:-1] + (-1, 32))
    amax = np.abs(blocks).max(-1, keepdims=True)
    byte = np.maximum(np.where(amax > 0, np.frexp(amax)[1] - 1 + 127, 0) - down, 1)
    scale = np.exp2(byte - 127.0)
    codes = (blocks / scale).astype(np.float32).astype(dtype).astype(np.float64)
    return np.moveaxis((codes * scale).reshape(v.shape), -1, axis)


WIDE = False


def mx_kscale(k):
    if not WIDE:
        return np.ones(k)
    levels = np.array([10, -10, 5, -5, 0])
    if k % 512:
        return np.exp2(np.random.permutation(np.resize(levels, k // 32))).repeat(32)
    a = np.empty((k // 512, 16))
    for p in range(k // 512):
        a[p, :8] = np.random.permutation(np.resize(levels, 8))
        for g in range(8):
            far = levels[np.abs(levels - a[p, g]) >= 10]
            a[p, g + 8] = far[np.random.randint(len(far))]
    return np.exp2(a.ravel()).repeat(32)


def f64(x):
    return np.asarray(x).astype(np.float64)


def striped(idx):
    return np.tile(np.asarray(idx).reshape(-1, 16).T, (8, 1)).astype(np.uint16)


def unstriped(offs):
    return offs[:16].T.reshape(-1).astype(np.int64)


E2M1 = np.array([0.0, 0.5, 1.0, 1.5, 2.0, 3.0, 4.0, 6.0, -0.0, -0.5, -1.0, -1.5, -2.0, -3.0, -4.0, -6.0])


def pack_weight(w, fmt):
    k, n = w.shape
    w = f64(np.asarray(w, np.float32).astype(ml_dtypes.bfloat16)).reshape(k // 32, 32, n)
    amax = np.abs(w).max(1)
    if fmt == "e4m3":
        byte = np.frexp(amax)[1] - 1 + 127 - 7
    else:
        mant, ex = np.frexp(amax / 6.0)
        byte = np.where(mant > 0.5, ex, ex - 1) + 127
    byte = np.clip(np.where(amax > 0, byte, 1), 1, 254)
    scaled = (w * np.exp2(127.0 - byte)[:, None, :]).reshape(k, n).astype(np.float32)
    by_word = np.ascontiguousarray(scaled.reshape(k // 512, 128, 4, n).transpose(0, 1, 3, 2))
    if fmt == "e4m3":
        words = by_word.astype(ml_dtypes.float8_e4m3fn).view(np.uint8)
    else:
        c = by_word.astype(ml_dtypes.float4_e2m1fn).view(np.uint8) & 0xF
        words = (c[..., 0::2] | (c[..., 1::2] << 4)).reshape(k // 512, 128, 2 * n)
    return np.ascontiguousarray(words), np.ascontiguousarray(byte.astype(np.uint8).reshape(k // 512, 16, n))


def unpack_weight(words, scales, fmt):
    g, _, n = scales.shape
    words = np.ascontiguousarray(words).reshape(g, 128, n, -1)
    if fmt == "e4m3":
        vals = words.view(ml_dtypes.float8_e4m3fn).astype(np.float64)
    else:
        nib = np.empty((g, 128, n, 4), np.uint8)
        nib[..., 0::2] = words & 0xF
        nib[..., 1::2] = words >> 4
        vals = E2M1[nib]
    vals = vals * np.repeat(np.exp2(scales.astype(np.float64) - 127.0), 8, axis=1)[..., None]
    return vals.transpose(0, 1, 3, 2).reshape(g * 512, n)


def sigmoid(v):
    return 1.0 / (1.0 + np.exp(-v))


def bf(x):
    return np.asarray(x, np.float32).astype(ml_dtypes.bfloat16)


def planes(Y):
    r, m = Y.shape
    b = f64(bf(Y)).reshape(r // 32, 32, m)
    amax = np.abs(b).max(1)
    byte = np.clip(np.where(amax > 0, np.frexp(amax)[1] - 1 + 127 - 7, 1), 1, 254)
    codes = (b * np.exp2(127.0 - byte)[:, None, :]).reshape(r, m).astype(np.float32).astype(ml_dtypes.float8_e4m3fn).view(np.uint8)
    words = codes.reshape(r // 512, 128, 4, m).transpose(0, 1, 3, 2)
    return np.ascontiguousarray(words), np.ascontiguousarray(byte.astype(np.uint8).reshape(r // 512, 16, m))


D, T, I, Q, E, K = 512, 2048, 512, 256, 512, 512


def setup_inputs():
    n = np.random.standard_normal
    idx = np.random.permutation(T)[:I]
    fd = mx_kscale(D)
    fi = mx_kscale(I)
    fk = mx_kscale(K)
    ti = np.ones(T)
    ti[idx] = fi
    keysp = pack_weight(n((D, T)) / fd[:, None], "e2m1")
    return {
        "query": (n((D, Q)) * 0.4 / np.sqrt(D) * fd[:, None]).astype(np.float32),
        "keys_words": keysp[0],
        "keys_scales": keysp[1],
        "size": (np.random.uniform(0.5, 2.0, (1, I)) * fi).astype(np.float32),
        "vals": (n((E, T)) / ti).astype(np.float32),
        "inp": (n((K, Q)) * fk[:, None]).astype(np.float32),
        "wg": (n((K, E)) * 1 / np.sqrt(K) / fk[:, None]).astype(np.float32),
        "offs": striped(idx),
    }


def reference(query, keys_words, keys_scales, size, vals, inp, wg, offs):
    idx = unstriped(offs)
    keysu = unpack_weight(keys_words, keys_scales, "e2m1")
    queryq = mxq(f64(query), 0, "e4m3")
    keysidxg = keysu[:, idx]
    a = queryq.T @ keysidxg
    p = np.exp(a - np.max(a, axis=1, keepdims=True))
    w = p * f64(size) / np.sum(p, axis=1, keepdims=True)
    wt = w.T
    vt = f64(vals)[:, idx].T
    vtq = mxq(vt, 0, "e4m3")
    wtq = mxq(wt, 0, "e4m3")
    o = vtq.T @ wtq
    wgq = mxq(f64(wg), 0, "e4m3")
    inpq = mxq(f64(inp), 0, "e4m3")
    z = wgq.T @ inpq
    y = o * sigmoid(z)
    words, scales = planes(y)
    return y, words, scales

@@ -1,0 +1,214 @@
+from contextlib import ExitStack
+
+import concourse.mybir as mybir
+from concourse.masks import make_identity
+
+F32 = mybir.dt.float32
+BF16 = mybir.dt.bfloat16
+I32 = mybir.dt.int32
+U32 = mybir.dt.uint32
+U16 = mybir.dt.uint16
+U8 = mybir.dt.uint8
+FP8X4 = mybir.dt.float8_e4m3fn_x4
+FP4X4 = mybir.dt.float4_e2m1fn_x4
+ALU = mybir.AluOpType
+ACT = mybir.ActivationFunctionType
+
+P = 128
+PACK = 4
+TOKENS = 2048
+SLOTS = 512
+ROWS = 256
+FEATURES = 512
+VECTOR_ROWS = 144
+PLANE_BYTES = TOKENS * 4
+
+FLOPS = 3 * 2 * 512 * 512 * 256
+
+
+def interleave(copy, grouped, planes):
+    copy(
+        out=grouped.rearrange("p (c i) j -> p c j i", i=PACK),
+        in_=planes.rearrange("p j (c i) -> p c j i", i=PACK),
+    )
+
+
+def tile_attend_gatedsoftmax_pl_kernel(tc, query, keys_words, keys_scales, size, vals, inp, wg, offs, out_0, out_1, out_2):
+    nc = tc.nc
+    with ExitStack() as ctx:
+        sb = ctx.enter_context(tc.tile_pool(name="sb", bufs=1))
+        vp = ctx.enter_context(tc.tile_pool(name="vp", bufs=1))
+        ps = ctx.enter_context(tc.psum_pool(name="ps", bufs=1))
+
+        def quantize(name, grouped, width, offset=None):
+            if offset is None:
+                codes = sb.tile([P, width], U32, name=name + "_codes", align_bytes=64)
+            else:
+                codes = vp.tile([P, width], U32, name=name + "_codes", align_bytes=64, offset=offset)
+            scales = sb.tile([P, width], U8, name=name + "_scales", align_bytes=64)
+            nc.vector.quantize_mx(out=codes[:].bitcast(FP8X4), scales=scales[:], in_=grouped)
+            return codes, scales
+
+        key_words = sb.tile([P, TOKENS], U16, align_bytes=64)
+        key_scales = sb.tile([P, TOKENS], U8, align_bytes=64)
+        offsets = sb.tile([P, SLOTS // 16], U16)
+        nc.gpsimd.memset(key_scales[:].bitcast(I32), 0)
+        nc.sync.dma_start(out=key_words[:].bitcast(I32), in_=keys_words[0].bitcast(I32))
+        nc.sync.dma_start(offsets[:], offs)
+        size_cols = sb.tile([P, PACK], F32)
+        nc.scalar.dma_start(out=size_cols[:], in_=size[0].rearrange("(p r) -> p r", r=PACK))
+        for quad in range(4):
+            nc.scalar.dma_start(
+                out=key_scales[32 * quad : 32 * quad + 4, :].bitcast(I32),
+                in_=keys_scales[0, 4 * quad : 4 * quad + 4, :].bitcast(I32),
+            )
+        query_raw = sb.tile([P, PACK, ROWS], F32)
+        nc.sync.dma_start(out=query_raw[:], in_=query.rearrange("(p j) q -> p j q", j=PACK))
+        inp_raw = sb.tile([P, PACK, ROWS], F32)
+        nc.sync.dma_start(out=inp_raw[:], in_=inp.rearrange("(p j) q -> p j q", j=PACK))
+        wg_raw = sb.tile([P, PACK, FEATURES], F32)
+        nc.sync.dma_start(out=wg_raw[:], in_=wg.rearrange("(p j) e -> p j e", j=PACK))
+        vals_planes = vals.rearrange("(m t) n -> t m n", t=PACK)
+        pools = []
+        for t in range(PACK):
+            pool_t = vp.tile([P, TOKENS], F32, name="vals%d" % t, align_bytes=64, offset=t * PLANE_BYTES)
+            nc.sync.dma_start(out=pool_t[:], in_=vals_planes[t])
+            pools.append(pool_t)
+
+        ident = sb.tile([P, P], F32)
+        make_identity(nc, ident[:])
+
+        got_words = sb.tile([P, SLOTS], U16, align_bytes=64)
+        got_scales = sb.tile([P, SLOTS], U8, align_bytes=64)
+        nc.vector.tensor_copy(got_words[:], key_words[:].indirect(offsets[:]))
+        nc.vector.tensor_copy(got_scales[:], key_scales[:].indirect(offsets[:]))
+
+        query_grouped = sb.tile([P, ROWS, PACK], BF16, align_bytes=64)
+        interleave(nc.scalar.copy, query_grouped[:], query_raw[:])
+        q_codes, q_scales = quantize("query", query_grouped[:].rearrange("p c j -> p (c j)"), ROWS)
+
+        size_bank = ps.tile([P, PACK, P], F32)
+        for r in range(PACK):
+            nc.tensor.transpose(size_bank[:, r, :], size_cols[:, r : r + 1].to_broadcast([P, P]), ident[:])
+
+        score_banks = []
+        for h in range(2):
+            bank = ps.tile([P, SLOTS], F32, name="acc", tag="acc", bufs=2)
+            nc.tensor.matmul_mx(
+                out=bank[:],
+                lhsT=q_codes[:, h * P : (h + 1) * P].bitcast(FP8X4),
+                lhsT_scale=q_scales[:, h * P : (h + 1) * P],
+                rhs=got_words[:].bitcast(FP4X4),
+                rhs_scale=got_scales[:],
+                start=True,
+                stop=True,
+            )
+            score_banks.append(bank)
+
+        inp_grouped = sb.tile([P, ROWS, PACK], BF16, align_bytes=64)
+        interleave(nc.scalar.copy, inp_grouped[:], inp_raw[:])
+
+        neg_max, probs, sums, weights = [], [], [], []
+        for h in range(2):
+            nm = sb.tile([P, 1], F32, name="neg_max%d" % h)
+            nc.vector.tensor_reduce(out=nm[:], in_=score_banks[h][:], axis=mybir.AxisListType.X, op=ALU.max, negate=True)
+            neg_max.append(nm)
+        i_codes, i_scales = quantize("inp", inp_grouped[:].rearrange("p c j -> p (c j)"), ROWS)
+        for h in range(2):
+            pr = sb.tile([P, SLOTS], F32, name="probs%d" % h, tag="probs%d" % h)
+            sm = sb.tile([P, 1], F32, name="sum%d" % h)
+            nc.scalar.activation(out=pr[:], in_=score_banks[h][:], func=ACT.Exp, bias=neg_max[h][:], scale=1.0, accum_out=sm[:])
+            probs.append(pr)
+            sums.append(sm)
+        inv = []
+        for h in range(2):
+            iv = sb.tile([P, 1], F32, name="inv%d" % h)
+            nc.vector.reciprocal(out=iv[:], in_=sums[h][:])
+            inv.append(iv)
+        w_bank = ps.tile([P, 2, 2, P], F32)
+        for h in range(2):
+            w = sb.tile([P, SLOTS], BF16, name="weights%d" % h)
+            nc.vector.scalar_tensor_tensor(
+                out=w[:].rearrange("p (s r) -> p s r", r=PACK),
+                in0=probs[h][:].rearrange("p (s r) -> p s r", r=PACK),
+                scalar=inv[h][:],
+                in1=size_bank[:].rearrange("p r s -> p s r"),
+                op0=ALU.mult,
+                op1=ALU.mult,
+            )
+            for u in range(2):
+                nc.tensor.transpose(w_bank[:, h, u, :], w[:].bitcast(F32)[:, u::2], ident[:])
+
+        wg_grouped = sb.tile([P, PACK, P, PACK], BF16, align_bytes=64)
+        w_grouped = sb.tile([P, ROWS * PACK], BF16, align_bytes=64)
+        nc.scalar.copy(
+            out=w_grouped[:].bitcast(F32).rearrange("p (h q u) -> p h q u", h=2, u=2),
+            in_=w_bank[:].rearrange("p h u q -> p h q u"),
+        )
+        for part in range(4):
+            ms = slice(32 * part, 32 * (part + 1))
+            nc.scalar.copy(
+                out=wg_grouped[:].rearrange("p t m j -> p m j t")[:, ms],
+                in_=wg_raw[:].rearrange("p j (m t) -> p m j t", t=PACK)[:, ms],
+            )
+        w_codes, w_scales = quantize("w", w_grouped[:], ROWS)
+        g_codes, g_scales = quantize("wg", wg_grouped[:].rearrange("p t m j -> p (t m j)"), FEATURES)
+        gate = sb.tile([P, PACK, ROWS], F32)
+        for b in range(2):
+            z_bank = ps.tile([P, 2, ROWS], F32, name="z", tag="z", bufs=2)
+            for s in range(2):
+                cols = slice((2 * b + s) * P, (2 * b + s + 1) * P)
+                nc.tensor.matmul_mx(
+                    out=z_bank[:, s, :],
+                    lhsT=g_codes[:, cols].bitcast(FP8X4),
+                    lhsT_scale=g_scales[:, cols],
+                    rhs=i_codes[:].bitcast(FP8X4),
+                    rhs_scale=i_scales[:],
+                    start=True,
+                    stop=True,
+                )
+            nc.scalar.activation(out=gate[:, 2 * b : 2 * b + 2, :], in_=z_bank[:], func=ACT.Sigmoid)
+
+        out_planes = out_0.rearrange("(p t) q -> p t q", t=PACK)
+        v_grouped = []
+        for t in range(PACK):
+            got = sb.tile([P, SLOTS], BF16, name="got%d" % t, tag="probs1" if t == 0 else "got%d" % t)
+            nc.vector.tensor_copy(got[:], pools[t][:].indirect(offsets[:]))
+            v_bank = ps.tile([P, 2, P], F32, name="vT", tag="vT", bufs=2)
+            for u in range(2):
+                nc.tensor.transpose(v_bank[:, u, :], got[:].bitcast(F32)[:, u::2], ident[:])
+            grouped = sb.tile([P, P * PACK], BF16, name="v_grouped%d" % t, align_bytes=64)
+            nc.scalar.copy(
+                out=grouped[:].bitcast(F32).rearrange("p (m u) -> p m u", u=2),
+                in_=v_bank[:].rearrange("p u m -> p m u"),
+            )
+            v_grouped.append(grouped)
+        y = vp.tile([P, PACK, ROWS], F32, align_bytes=64, offset=(PACK - 1) * PLANE_BYTES + PLANE_BYTES // 2)
+        for t in range(PACK):
+            offset = (t + 1) * PLANE_BYTES if t + 1 < PACK else None
+            v_codes, v_scales = quantize("v%d" % t, v_grouped[t][:], P, offset)
+            o_bank = ps.tile([P, ROWS], F32, name="acc", tag="acc", bufs=2)
+            nc.tensor.matmul_mx(
+                out=o_bank[:],
+                lhsT=v_codes[:].bitcast(FP8X4),
+                lhsT_scale=v_scales[:],
+                rhs=w_codes[:].bitcast(FP8X4),
+                rhs_scale=w_scales[:],
+                start=True,
+                stop=True,
+            )
+            nc.vector.tensor_tensor(out=y[:, t, :], in0=o_bank[:], in1=gate[:, t, :], op=ALU.mult)
+            if t % 2 == 1:
+                nc.sync.dma_start(out=out_planes[:, t - 1 : t + 1, :], in_=y[:, t - 1 : t + 1, :])
+
+        y_grouped = sb.tile([P, ROWS, PACK], BF16, align_bytes=64)
+        interleave(nc.vector.tensor_copy, y_grouped[:, :VECTOR_ROWS, :], y[:, :, :VECTOR_ROWS])
+        interleave(nc.scalar.copy, y_grouped[:, VECTOR_ROWS:, :], y[:, :, VECTOR_ROWS:])
+        y_codes, y_scales = quantize("y", y_grouped[:].rearrange("p c j -> p (c j)"), ROWS)
+        nc.sync.dma_start(out=out_1[0].rearrange("p n t -> p (n t)").bitcast(I32), in_=y_codes[:].bitcast(I32))
+        for quad in range(4):
+            queue = nc.scalar if quad % 2 == 0 else nc.sync
+            queue.dma_start(
+                out=out_2[0, 4 * quad : 4 * quad + 4, :].bitcast(I32),
+                in_=y_scales[32 * quad : 32 * quad + 4, :].bitcast(I32),
+            )

@@ -22,6 +22,7 @@ ROWS = 256
 FEATURES = 512
 VECTOR_ROWS = 144
 PLANE_BYTES = TOKENS * 4
+KEY_SCALES_AT = PACK * PLANE_BYTES
 
 FLOPS = 3 * 2 * 512 * 512 * 256
 
@@ -50,30 +51,28 @@ def tile_attend_gatedsoftmax_pl_kernel(tc, query, keys_words, keys_scales, size,
             return codes, scales
 
         key_words = sb.tile([P, TOKENS], U16, align_bytes=64)
-        key_scales = sb.tile([P, TOKENS], U8, align_bytes=64)
+        key_scales = vp.tile([P, TOKENS], U8, align_bytes=64, offset=KEY_SCALES_AT)
         offsets = sb.tile([P, SLOTS // 16], U16)
+        query_raw = sb.tile([P, PACK, ROWS], F32)
+        size_cols = sb.tile([P, PACK], F32)
         nc.gpsimd.memset(key_scales[:].bitcast(I32), 0)
         nc.sync.dma_start(out=key_words[:].bitcast(I32), in_=keys_words[0].bitcast(I32))
         nc.sync.dma_start(offsets[:], offs)
-        size_cols = sb.tile([P, PACK], F32)
-        nc.scalar.dma_start(out=size_cols[:], in_=size[0].rearrange("(p r) -> p r", r=PACK))
-        for quad in range(4):
-            nc.scalar.dma_start(
-                out=key_scales[32 * quad : 32 * quad + 4, :].bitcast(I32),
-                in_=keys_scales[0, 4 * quad : 4 * quad + 4, :].bitcast(I32),
-            )
-        query_raw = sb.tile([P, PACK, ROWS], F32)
         nc.sync.dma_start(out=query_raw[:], in_=query.rearrange("(p j) q -> p j q", j=PACK))
-        inp_raw = sb.tile([P, PACK, ROWS], F32)
-        nc.sync.dma_start(out=inp_raw[:], in_=inp.rearrange("(p j) q -> p j q", j=PACK))
-        wg_raw = sb.tile([P, PACK, FEATURES], F32)
-        nc.sync.dma_start(out=wg_raw[:], in_=wg.rearrange("(p j) e -> p j e", j=PACK))
+        nc.scalar.dma_start(out=size_cols[:], in_=size[0].rearrange("(p r) -> p r", r=PACK))
+        for r in range(4):
+            nc.scalar.dma_start(out=key_scales[r:P:32, :].bitcast(I32), in_=keys_scales[0, r:16:4, :].bitcast(I32))
         vals_planes = vals.rearrange("(m t) n -> t m n", t=PACK)
-        pools = []
-        for t in range(PACK):
-            pool_t = vp.tile([P, TOKENS], F32, name="vals%d" % t, align_bytes=64, offset=t * PLANE_BYTES)
-            nc.sync.dma_start(out=pool_t[:], in_=vals_planes[t])
-            pools.append(pool_t)
+        pools = [
+            vp.tile([P, TOKENS], F32, name="vals%d" % t, align_bytes=64, offset=t * PLANE_BYTES) for t in range(PACK)
+        ]
+        inp_raw = sb.tile([P, PACK, ROWS], F32)
+        wg_raw = sb.tile([P, PACK, FEATURES], F32)
+        nc.sync.dma_start(out=pools[0][:], in_=vals_planes[0])
+        nc.sync.dma_start(out=inp_raw[:], in_=inp.rearrange("(p j) q -> p j q", j=PACK))
+        nc.sync.dma_start(out=wg_raw[:], in_=wg.rearrange("(p j) e -> p j e", j=PACK))
+        for t in range(1, PACK):
+            nc.sync.dma_start(out=pools[t][:], in_=vals_planes[t])
 
         ident = sb.tile([P, P], F32)
         make_identity(nc, ident[:])
@@ -85,7 +84,7 @@ def tile_attend_gatedsoftmax_pl_kernel(tc, query, keys_words, keys_scales, size,
 
         query_grouped = sb.tile([P, ROWS, PACK], BF16, align_bytes=64)
         interleave(nc.scalar.copy, query_grouped[:], query_raw[:])
-        q_codes, q_scales = quantize("query", query_grouped[:].rearrange("p c j -> p (c j)"), ROWS)
+        q_codes, q_scales = quantize("query", query_grouped[:].rearrange("p c j -> p (c j)"), ROWS, KEY_SCALES_AT)
 
         size_bank = ps.tile([P, PACK, P], F32)
         for r in range(PACK):
@@ -105,15 +104,11 @@ def tile_attend_gatedsoftmax_pl_kernel(tc, query, keys_words, keys_scales, size,
             )
             score_banks.append(bank)
 
-        inp_grouped = sb.tile([P, ROWS, PACK], BF16, align_bytes=64)
-        interleave(nc.scalar.copy, inp_grouped[:], inp_raw[:])
-
         neg_max, probs, sums, weights = [], [], [], []
         for h in range(2):
             nm = sb.tile([P, 1], F32, name="neg_max%d" % h)
             nc.vector.tensor_reduce(out=nm[:], in_=score_banks[h][:], axis=mybir.AxisListType.X, op=ALU.max, negate=True)
             neg_max.append(nm)
-        i_codes, i_scales = quantize("inp", inp_grouped[:].rearrange("p c j -> p (c j)"), ROWS)
         for h in range(2):
             pr = sb.tile([P, SLOTS], F32, name="probs%d" % h, tag="probs%d" % h)
             sm = sb.tile([P, 1], F32, name="sum%d" % h)
@@ -140,18 +135,21 @@ def tile_attend_gatedsoftmax_pl_kernel(tc, query, keys_words, keys_scales, size,
                 nc.tensor.transpose(w_bank[:, h, u, :], w[:].bitcast(F32)[:, u::2], ident[:])
 
         wg_grouped = sb.tile([P, PACK, P, PACK], BF16, align_bytes=64)
-        w_grouped = sb.tile([P, ROWS * PACK], BF16, align_bytes=64)
-        nc.scalar.copy(
-            out=w_grouped[:].bitcast(F32).rearrange("p (h q u) -> p h q u", h=2, u=2),
-            in_=w_bank[:].rearrange("p h u q -> p h q u"),
-        )
         for part in range(4):
             ms = slice(32 * part, 32 * (part + 1))
             nc.scalar.copy(
                 out=wg_grouped[:].rearrange("p t m j -> p m j t")[:, ms],
                 in_=wg_raw[:].rearrange("p j (m t) -> p m j t", t=PACK)[:, ms],
             )
+        w_grouped = sb.tile([P, ROWS * PACK], BF16, align_bytes=64)
+        nc.scalar.copy(
+            out=w_grouped[:].bitcast(F32).rearrange("p (h q u) -> p h q u", h=2, u=2),
+            in_=w_bank[:].rearrange("p h u q -> p h q u"),
+        )
         w_codes, w_scales = quantize("w", w_grouped[:], ROWS)
+        inp_grouped = sb.tile([P, ROWS, PACK], BF16, align_bytes=64)
+        interleave(nc.scalar.copy, inp_grouped[:], inp_raw[:])
+        i_codes, i_scales = quantize("inp", inp_grouped[:].rearrange("p c j -> p (c j)"), ROWS)
         g_codes, g_scales = quantize("wg", wg_grouped[:].rearrange("p t m j -> p (t m j)"), FEATURES)
         gate = sb.tile([P, PACK, ROWS], F32)
         for b in range(2):
@@ -172,7 +170,10 @@ def tile_attend_gatedsoftmax_pl_kernel(tc, query, keys_words, keys_scales, size,
         out_planes = out_0.rearrange("(p t) q -> p t q", t=PACK)
         v_grouped = []
         for t in range(PACK):
-            got = sb.tile([P, SLOTS], BF16, name="got%d" % t, tag="probs1" if t == 0 else "got%d" % t)
+            if t == 0:
+                got = vp.tile([P, SLOTS], BF16, name="got0", align_bytes=64, offset=KEY_SCALES_AT + TOKENS // 2)
+            else:
+                got = sb.tile([P, SLOTS], BF16, name="got%d" % t)
             nc.vector.tensor_copy(got[:], pools[t][:].indirect(offsets[:]))
             v_bank = ps.tile([P, 2, P], F32, name="vT", tag="vT", bufs=2)
             for u in range(2):
@@ -185,7 +186,7 @@ def tile_attend_gatedsoftmax_pl_kernel(tc, query, keys_words, keys_scales, size,
             v_grouped.append(grouped)
         y = vp.tile([P, PACK, ROWS], F32, align_bytes=64, offset=(PACK - 1) * PLANE_BYTES + PLANE_BYTES // 2)
         for t in range(PACK):
-            offset = (t + 1) * PLANE_BYTES if t + 1 < PACK else None
+            offset = (t + 1) * PLANE_BYTES if 0 < t < PACK - 1 else None
             v_codes, v_scales = quantize("v%d" % t, v_grouped[t][:], P, offset)
             o_bank = ps.tile([P, ROWS], F32, name="acc", tag="acc", bufs=2)
             nc.tensor.matmul_mx(
@@ -206,9 +207,6 @@ def tile_attend_gatedsoftmax_pl_kernel(tc, query, keys_words, keys_scales, size,
         interleave(nc.scalar.copy, y_grouped[:, VECTOR_ROWS:, :], y[:, :, VECTOR_ROWS:])
         y_codes, y_scales = quantize("y", y_grouped[:].rearrange("p c j -> p (c j)"), ROWS)
         nc.sync.dma_start(out=out_1[0].rearrange("p n t -> p (n t)").bitcast(I32), in_=y_codes[:].bitcast(I32))
-        for quad in range(4):
-            queue = nc.scalar if quad % 2 == 0 else nc.sync
-            queue.dma_start(
-                out=out_2[0, 4 * quad : 4 * quad + 4, :].bitcast(I32),
-                in_=y_scales[32 * quad : 32 * quad + 4, :].bitcast(I32),
-            )
+        for r in range(4):
+            queue = nc.scalar if r % 2 == 0 else nc.sync
+            queue.dma_start(out=out_2[0, r:16:4, :].bitcast(I32), in_=y_scales[r:P:32, :].bitcast(I32))

@@ -22,7 +22,6 @@ ROWS = 256
 FEATURES = 512
 VECTOR_ROWS = 144
 PLANE_BYTES = TOKENS * 4
-KEY_SCALES_AT = PACK * PLANE_BYTES
 
 FLOPS = 3 * 2 * 512 * 512 * 256
 
@@ -51,28 +50,27 @@ def tile_attend_gatedsoftmax_pl_kernel(tc, query, keys_words, keys_scales, size,
             return codes, scales
 
         key_words = sb.tile([P, TOKENS], U16, align_bytes=64)
-        key_scales = vp.tile([P, TOKENS], U8, align_bytes=64, offset=KEY_SCALES_AT)
+        key_scales = sb.tile([P, TOKENS], U8, align_bytes=64)
         offsets = sb.tile([P, SLOTS // 16], U16)
-        query_raw = sb.tile([P, PACK, ROWS], F32)
-        size_cols = sb.tile([P, PACK], F32)
         nc.gpsimd.memset(key_scales[:].bitcast(I32), 0)
         nc.sync.dma_start(out=key_words[:].bitcast(I32), in_=keys_words[0].bitcast(I32))
         nc.sync.dma_start(offsets[:], offs)
-        nc.sync.dma_start(out=query_raw[:], in_=query.rearrange("(p j) q -> p j q", j=PACK))
+        size_cols = sb.tile([P, PACK], F32)
         nc.scalar.dma_start(out=size_cols[:], in_=size[0].rearrange("(p r) -> p r", r=PACK))
         for r in range(4):
             nc.scalar.dma_start(out=key_scales[r:P:32, :].bitcast(I32), in_=keys_scales[0, r:16:4, :].bitcast(I32))
-        vals_planes = vals.rearrange("(m t) n -> t m n", t=PACK)
-        pools = [
-            vp.tile([P, TOKENS], F32, name="vals%d" % t, align_bytes=64, offset=t * PLANE_BYTES) for t in range(PACK)
-        ]
+        query_raw = sb.tile([P, PACK, ROWS], F32)
+        nc.sync.dma_start(out=query_raw[:], in_=query.rearrange("(p j) q -> p j q", j=PACK))
         inp_raw = sb.tile([P, PACK, ROWS], F32)
-        wg_raw = sb.tile([P, PACK, FEATURES], F32)
-        nc.sync.dma_start(out=pools[0][:], in_=vals_planes[0])
         nc.sync.dma_start(out=inp_raw[:], in_=inp.rearrange("(p j) q -> p j q", j=PACK))
+        wg_raw = sb.tile([P, PACK, FEATURES], F32)
         nc.sync.dma_start(out=wg_raw[:], in_=wg.rearrange("(p j) e -> p j e", j=PACK))
-        for t in range(1, PACK):
-            nc.sync.dma_start(out=pools[t][:], in_=vals_planes[t])
+        vals_planes = vals.rearrange("(m t) n -> t m n", t=PACK)
+        pools = []
+        for t in range(PACK):
+            pool_t = vp.tile([P, TOKENS], F32, name="vals%d" % t, align_bytes=64, offset=t * PLANE_BYTES)
+            nc.sync.dma_start(out=pool_t[:], in_=vals_planes[t])
+            pools.append(pool_t)
 
         ident = sb.tile([P, P], F32)
         make_identity(nc, ident[:])
@@ -84,11 +82,13 @@ def tile_attend_gatedsoftmax_pl_kernel(tc, query, keys_words, keys_scales, size,
 
         query_grouped = sb.tile([P, ROWS, PACK], BF16, align_bytes=64)
         interleave(nc.scalar.copy, query_grouped[:], query_raw[:])
-        q_codes, q_scales = quantize("query", query_grouped[:].rearrange("p c j -> p (c j)"), ROWS, KEY_SCALES_AT)
+        q_codes, q_scales = quantize("query", query_grouped[:].rearrange("p c j -> p (c j)"), ROWS)
 
+        half_size = sb.tile([P, PACK], F32)
+        nc.gpsimd.tensor_scalar(out=half_size[:], in0=size_cols[:], scalar1=0.5, scalar2=0.0, op0=ALU.mult, op1=ALU.add)
         size_bank = ps.tile([P, PACK, P], F32)
         for r in range(PACK):
-            nc.tensor.transpose(size_bank[:, r, :], size_cols[:, r : r + 1].to_broadcast([P, P]), ident[:])
+            nc.tensor.transpose(size_bank[:, r, :], half_size[:, r : r + 1].to_broadcast([P, P]), ident[:])
 
         score_banks = []
         for h in range(2):
@@ -104,11 +104,15 @@ def tile_attend_gatedsoftmax_pl_kernel(tc, query, keys_words, keys_scales, size,
             )
             score_banks.append(bank)
 
+        inp_grouped = sb.tile([P, ROWS, PACK], BF16, align_bytes=64)
+        interleave(nc.scalar.copy, inp_grouped[:], inp_raw[:])
+
         neg_max, probs, sums, weights = [], [], [], []
         for h in range(2):
-            nm = sb.tile([P, 1], F32, name="neg_max%d" % h)
+            nm = sb.tile([P, 1], F32, name="neg_max%d" % h, tag="neg_max%d" % h, align_bytes=64)
             nc.vector.tensor_reduce(out=nm[:], in_=score_banks[h][:], axis=mybir.AxisListType.X, op=ALU.max, negate=True)
             neg_max.append(nm)
+        i_codes, i_scales = quantize("inp", inp_grouped[:].rearrange("p c j -> p (c j)"), ROWS)
         for h in range(2):
             pr = sb.tile([P, SLOTS], F32, name="probs%d" % h, tag="probs%d" % h)
             sm = sb.tile([P, 1], F32, name="sum%d" % h)
@@ -134,22 +138,19 @@ def tile_attend_gatedsoftmax_pl_kernel(tc, query, keys_words, keys_scales, size,
             for u in range(2):
                 nc.tensor.transpose(w_bank[:, h, u, :], w[:].bitcast(F32)[:, u::2], ident[:])
 
-        wg_grouped = sb.tile([P, PACK, P, PACK], BF16, align_bytes=64)
+        wg_grouped = sb.tile([P, PACK, P, PACK], BF16, tag="neg_max1", align_bytes=64)
+        w_grouped = sb.tile([P, ROWS * PACK], BF16, align_bytes=64)
+        nc.scalar.copy(
+            out=w_grouped[:].bitcast(F32).rearrange("p (h q u) -> p h q u", h=2, u=2),
+            in_=w_bank[:].rearrange("p h u q -> p h q u"),
+        )
         for part in range(4):
             ms = slice(32 * part, 32 * (part + 1))
             nc.scalar.copy(
                 out=wg_grouped[:].rearrange("p t m j -> p m j t")[:, ms],
                 in_=wg_raw[:].rearrange("p j (m t) -> p m j t", t=PACK)[:, ms],
             )
-        w_grouped = sb.tile([P, ROWS * PACK], BF16, align_bytes=64)
-        nc.scalar.copy(
-            out=w_grouped[:].bitcast(F32).rearrange("p (h q u) -> p h q u", h=2, u=2),
-            in_=w_bank[:].rearrange("p h u q -> p h q u"),
-        )
         w_codes, w_scales = quantize("w", w_grouped[:], ROWS)
-        inp_grouped = sb.tile([P, ROWS, PACK], BF16, align_bytes=64)
-        interleave(nc.scalar.copy, inp_grouped[:], inp_raw[:])
-        i_codes, i_scales = quantize("inp", inp_grouped[:].rearrange("p c j -> p (c j)"), ROWS)
         g_codes, g_scales = quantize("wg", wg_grouped[:].rearrange("p t m j -> p (t m j)"), FEATURES)
         gate = sb.tile([P, PACK, ROWS], F32)
         for b in range(2):
@@ -165,15 +166,17 @@ def tile_attend_gatedsoftmax_pl_kernel(tc, query, keys_words, keys_scales, size,
                     start=True,
                     stop=True,
                 )
-            nc.scalar.activation(out=gate[:, 2 * b : 2 * b + 2, :], in_=z_bank[:], func=ACT.Sigmoid)
+            nc.scalar.activation(out=gate[:, 2 * b : 2 * b + 2, :], in_=z_bank[:], func=ACT.Tanh, scale=0.5)
 
         out_planes = out_0.rearrange("(p t) q -> p t q", t=PACK)
         v_grouped = []
         for t in range(PACK):
             if t == 0:
-                got = vp.tile([P, SLOTS], BF16, name="got0", align_bytes=64, offset=KEY_SCALES_AT + TOKENS // 2)
+                got = sb.tile([P, SLOTS], BF16, name="got0", tag="probs1")
             else:
-                got = sb.tile([P, SLOTS], BF16, name="got%d" % t)
+                got = vp.tile(
+                    [P, SLOTS], BF16, name="got%d" % t, align_bytes=64, offset=(t - 1) * PLANE_BYTES + PLANE_BYTES // 2
+                )
             nc.vector.tensor_copy(got[:], pools[t][:].indirect(offsets[:]))
             v_bank = ps.tile([P, 2, P], F32, name="vT", tag="vT", bufs=2)
             for u in range(2):
@@ -186,7 +189,7 @@ def tile_attend_gatedsoftmax_pl_kernel(tc, query, keys_words, keys_scales, size,
             v_grouped.append(grouped)
         y = vp.tile([P, PACK, ROWS], F32, align_bytes=64, offset=(PACK - 1) * PLANE_BYTES + PLANE_BYTES // 2)
         for t in range(PACK):
-            offset = (t + 1) * PLANE_BYTES if 0 < t < PACK - 1 else None
+            offset = (t + 1) * PLANE_BYTES if t + 1 < PACK else None
             v_codes, v_scales = quantize("v%d" % t, v_grouped[t][:], P, offset)
             o_bank = ps.tile([P, ROWS], F32, name="acc", tag="acc", bufs=2)
             nc.tensor.matmul_mx(
@@ -198,7 +201,9 @@ def tile_attend_gatedsoftmax_pl_kernel(tc, query, keys_words, keys_scales, size,
                 start=True,
                 stop=True,
             )
-            nc.vector.tensor_tensor(out=y[:, t, :], in0=o_bank[:], in1=gate[:, t, :], op=ALU.mult)
+            nc.vector.scalar_tensor_tensor(
+                out=y[:, t, :], in0=gate[:, t, :], scalar=1.0, in1=o_bank[:], op0=ALU.add, op1=ALU.mult
+            )
             if t % 2 == 1:
                 nc.sync.dma_start(out=out_planes[:, t - 1 : t + 1, :], in_=y[:, t - 1 : t + 1, :])
 

@@ -20,7 +20,7 @@ TOKENS = 2048
 SLOTS = 512
 ROWS = 256
 FEATURES = 512
-VECTOR_ROWS = 144
+SCALAR_ROWS = 112
 PLANE_BYTES = TOKENS * 4
 
 FLOPS = 3 * 2 * 512 * 512 * 256
@@ -52,13 +52,13 @@ def tile_attend_gatedsoftmax_pl_kernel(tc, query, keys_words, keys_scales, size,
         key_words = sb.tile([P, TOKENS], U16, align_bytes=64)
         key_scales = sb.tile([P, TOKENS], U8, align_bytes=64)
         offsets = sb.tile([P, SLOTS // 16], U16)
-        nc.gpsimd.memset(key_scales[:].bitcast(I32), 0)
-        nc.sync.dma_start(out=key_words[:].bitcast(I32), in_=keys_words[0].bitcast(I32))
+        nc.vector.memset(key_scales[:].bitcast(I32), 0)
         nc.sync.dma_start(offsets[:], offs)
-        size_cols = sb.tile([P, PACK], F32)
-        nc.scalar.dma_start(out=size_cols[:], in_=size[0].rearrange("(p r) -> p r", r=PACK))
         for r in range(4):
             nc.scalar.dma_start(out=key_scales[r:P:32, :].bitcast(I32), in_=keys_scales[0, r:16:4, :].bitcast(I32))
+        size_cols = sb.tile([P, PACK], F32)
+        nc.sync.dma_start(out=size_cols[:], in_=size[0].rearrange("(p r) -> p r", r=PACK))
+        nc.sync.dma_start(out=key_words[:].bitcast(I32), in_=keys_words[0].bitcast(I32))
         query_raw = sb.tile([P, PACK, ROWS], F32)
         nc.sync.dma_start(out=query_raw[:], in_=query.rearrange("(p j) q -> p j q", j=PACK))
         inp_raw = sb.tile([P, PACK, ROWS], F32)
@@ -77,8 +77,8 @@ def tile_attend_gatedsoftmax_pl_kernel(tc, query, keys_words, keys_scales, size,
 
         got_words = sb.tile([P, SLOTS], U16, align_bytes=64)
         got_scales = sb.tile([P, SLOTS], U8, align_bytes=64)
-        nc.vector.tensor_copy(got_words[:], key_words[:].indirect(offsets[:]))
         nc.vector.tensor_copy(got_scales[:], key_scales[:].indirect(offsets[:]))
+        nc.vector.tensor_copy(got_words[:], key_words[:].indirect(offsets[:]))
 
         query_grouped = sb.tile([P, ROWS, PACK], BF16, align_bytes=64)
         interleave(nc.scalar.copy, query_grouped[:], query_raw[:])
@@ -178,7 +178,7 @@ def tile_attend_gatedsoftmax_pl_kernel(tc, query, keys_words, keys_scales, size,
                     [P, SLOTS], BF16, name="got%d" % t, align_bytes=64, offset=(t - 1) * PLANE_BYTES + PLANE_BYTES // 2
                 )
             nc.vector.tensor_copy(got[:], pools[t][:].indirect(offsets[:]))
-            v_bank = ps.tile([P, 2, P], F32, name="vT", tag="vT", bufs=2)
+            v_bank = ps.tile([P, 2, P], F32, name="vT%d" % t, tag="vT%d" % (t % 2))
             for u in range(2):
                 nc.tensor.transpose(v_bank[:, u, :], got[:].bitcast(F32)[:, u::2], ident[:])
             grouped = sb.tile([P, P * PACK], BF16, name="v_grouped%d" % t, align_bytes=64)
@@ -188,28 +188,40 @@ def tile_attend_gatedsoftmax_pl_kernel(tc, query, keys_words, keys_scales, size,
             )
             v_grouped.append(grouped)
         y = vp.tile([P, PACK, ROWS], F32, align_bytes=64, offset=(PACK - 1) * PLANE_BYTES + PLANE_BYTES // 2)
-        for t in range(PACK):
-            offset = (t + 1) * PLANE_BYTES if t + 1 < PACK else None
-            v_codes, v_scales = quantize("v%d" % t, v_grouped[t][:], P, offset)
-            o_bank = ps.tile([P, ROWS], F32, name="acc", tag="acc", bufs=2)
+
+        def gated_product(t, v_codes, v_scales, rows, tag, bufs):
+            o_bank = ps.tile([P, rows.stop - rows.start], F32, name="o", tag=tag, bufs=bufs)
             nc.tensor.matmul_mx(
                 out=o_bank[:],
                 lhsT=v_codes[:].bitcast(FP8X4),
                 lhsT_scale=v_scales[:],
-                rhs=w_codes[:].bitcast(FP8X4),
-                rhs_scale=w_scales[:],
+                rhs=w_codes[:, rows].bitcast(FP8X4),
+                rhs_scale=w_scales[:, rows],
                 start=True,
                 stop=True,
             )
             nc.vector.scalar_tensor_tensor(
-                out=y[:, t, :], in0=gate[:, t, :], scalar=1.0, in1=o_bank[:], op0=ALU.add, op1=ALU.mult
+                out=y[:, t, rows], in0=gate[:, t, rows], scalar=1.0, in1=o_bank[:], op0=ALU.add, op1=ALU.mult
             )
-            if t % 2 == 1:
-                nc.sync.dma_start(out=out_planes[:, t - 1 : t + 1, :], in_=y[:, t - 1 : t + 1, :])
+
+        for t in range(PACK):
+            offset = (t + 1) * PLANE_BYTES if t + 1 < PACK else None
+            v_codes, v_scales = quantize("v%d" % t, v_grouped[t][:], P, offset)
+            if t < 2:
+                gated_product(t, v_codes, v_scales, slice(0, ROWS), "acc", 2)
+            elif t == 2:
+                gated_product(t, v_codes, v_scales, slice(0, ROWS), "vT1", 1)
+            else:
+                for h in range(2):
+                    gated_product(t, v_codes, v_scales, slice(h * P, (h + 1) * P), "acc", 2)
+            if t == 1:
+                nc.sync.dma_start(out=out_planes[:, 0:2, :], in_=y[:, 0:2, :])
+            elif t > 1:
+                nc.sync.dma_start(out=out_planes[:, t, :], in_=y[:, t, :])
 
         y_grouped = sb.tile([P, ROWS, PACK], BF16, align_bytes=64)
-        interleave(nc.vector.tensor_copy, y_grouped[:, :VECTOR_ROWS, :], y[:, :, :VECTOR_ROWS])
-        interleave(nc.scalar.copy, y_grouped[:, VECTOR_ROWS:, :], y[:, :, VECTOR_ROWS:])
+        interleave(nc.scalar.copy, y_grouped[:, :SCALAR_ROWS, :], y[:, :, :SCALAR_ROWS])
+        interleave(nc.vector.tensor_copy, y_grouped[:, SCALAR_ROWS:, :], y[:, :, SCALAR_ROWS:])
         y_codes, y_scales = quantize("y", y_grouped[:].rearrange("p c j -> p (c j)"), ROWS)
         nc.sync.dma_start(out=out_1[0].rearrange("p n t -> p (n t)").bitcast(I32), in_=y_codes[:].bitcast(I32))
         for r in range(4):

@@ -1,7 +1,6 @@
 from contextlib import ExitStack
 
 import concourse.mybir as mybir
-from concourse.masks import make_identity
 
 F32 = mybir.dt.float32
 BF16 = mybir.dt.bfloat16
@@ -21,7 +20,12 @@ SLOTS = 512
 ROWS = 256
 FEATURES = 512
 SCALAR_ROWS = 112
+KB = 1024
 PLANE_BYTES = TOKENS * 4
+WG_AT = PACK * PLANE_BYTES
+FIRST_AT = WG_AT + 10 * KB
+LAST_AT = FIRST_AT + 4 * KB
+LATE_BYTES = LAST_AT + 2 * KB
 
 FLOPS = 3 * 2 * 512 * 512 * 256
 
@@ -40,97 +44,137 @@ def tile_attend_gatedsoftmax_pl_kernel(tc, query, keys_words, keys_scales, size,
         vp = ctx.enter_context(tc.tile_pool(name="vp", bufs=1))
         ps = ctx.enter_context(tc.psum_pool(name="ps", bufs=1))
 
-        def quantize(name, grouped, width, offset=None):
+        def tile(name, shape, dtype, offset=None):
             if offset is None:
-                codes = sb.tile([P, width], U32, name=name + "_codes", align_bytes=64)
-            else:
-                codes = vp.tile([P, width], U32, name=name + "_codes", align_bytes=64, offset=offset)
-            scales = sb.tile([P, width], U8, name=name + "_scales", align_bytes=64)
+                return sb.tile(shape, dtype, name=name, align_bytes=64)
+            return vp.tile(shape, dtype, name=name, align_bytes=64, offset=offset)
+
+        def quantize(name, grouped, width, offset=None):
+            codes = tile(name + "_codes", [P, width], U32, offset)
+            scales = tile(name + "_scales", [P, width], U8)
             nc.vector.quantize_mx(out=codes[:].bitcast(FP8X4), scales=scales[:], in_=grouped)
             return codes, scales
 
-        key_words = sb.tile([P, TOKENS], U16, align_bytes=64)
-        key_scales = sb.tile([P, TOKENS], U8, align_bytes=64)
+        def product(out, lhs, cols, rhs, rhs_dtype=FP8X4):
+            nc.tensor.matmul_mx(
+                out=out,
+                lhsT=lhs[0][:, cols].bitcast(FP8X4),
+                lhsT_scale=lhs[1][:, cols],
+                rhs=rhs[0][:].bitcast(rhs_dtype),
+                rhs_scale=rhs[1][:],
+                start=True,
+                stop=True,
+            )
+
+        halves = [slice(h * P, (h + 1) * P) for h in range(2)]
+        everything = slice(0, P)
+        all_rows = slice(0, ROWS)
+
+        key_words = tile("key_words", [P, TOKENS], U16)
+        key_scales = tile("key_scales", [P, TOKENS], U8)
         offsets = sb.tile([P, SLOTS // 16], U16)
-        nc.vector.memset(key_scales[:].bitcast(I32), 0)
+        nc.gpsimd.memset(key_scales[:].bitcast(I32), 0)
+        ident = tile("ident", [P, P], F32)
+        zeros = tile("zeros", [P, LATE_BYTES // 4], F32, 0)
+        nc.gpsimd.memset(zeros[:, :P], 0.0)
+        nc.gpsimd.affine_select(
+            out=ident[:], in_=zeros[:, :P], compare_op=ALU.not_equal, fill=1.0, base=0, pattern=[[-1, P]], channel_multiplier=1
+        )
         nc.sync.dma_start(offsets[:], offs)
+        size_cols = tile("size_cols", [P, PACK], F32)
+        nc.scalar.dma_start(out=size_cols[:], in_=size[0].rearrange("(p r) -> p r", r=PACK))
         for r in range(4):
             nc.scalar.dma_start(out=key_scales[r:P:32, :].bitcast(I32), in_=keys_scales[0, r:16:4, :].bitcast(I32))
-        size_cols = sb.tile([P, PACK], F32)
-        nc.sync.dma_start(out=size_cols[:], in_=size[0].rearrange("(p r) -> p r", r=PACK))
         nc.sync.dma_start(out=key_words[:].bitcast(I32), in_=keys_words[0].bitcast(I32))
-        query_raw = sb.tile([P, PACK, ROWS], F32)
+        query_raw = tile("query_raw", [P, PACK, ROWS], F32)
         nc.sync.dma_start(out=query_raw[:], in_=query.rearrange("(p j) q -> p j q", j=PACK))
-        inp_raw = sb.tile([P, PACK, ROWS], F32)
-        nc.sync.dma_start(out=inp_raw[:], in_=inp.rearrange("(p j) q -> p j q", j=PACK))
-        wg_raw = sb.tile([P, PACK, FEATURES], F32)
-        nc.sync.dma_start(out=wg_raw[:], in_=wg.rearrange("(p j) e -> p j e", j=PACK))
         vals_planes = vals.rearrange("(m t) n -> t m n", t=PACK)
-        pools = []
-        for t in range(PACK):
-            pool_t = vp.tile([P, TOKENS], F32, name="vals%d" % t, align_bytes=64, offset=t * PLANE_BYTES)
-            nc.sync.dma_start(out=pool_t[:], in_=vals_planes[t])
-            pools.append(pool_t)
+        inp_rows = inp.rearrange("(p j) q -> p j q", j=PACK)
 
-        ident = sb.tile([P, P], F32)
-        make_identity(nc, ident[:])
+        def load_plane(t):
+            plane = tile("vals%d" % t, [P, TOKENS], F32, t * PLANE_BYTES)
+            nc.sync.dma_start(out=plane[:], in_=vals_planes[t])
+            return plane
 
-        got_words = sb.tile([P, SLOTS], U16, align_bytes=64)
-        got_scales = sb.tile([P, SLOTS], U8, align_bytes=64)
-        nc.vector.tensor_copy(got_scales[:], key_scales[:].indirect(offsets[:]))
+        def load_inp(h, offset):
+            raw = tile("inp_raw%d" % h, [P, PACK, P], F32, offset)
+            nc.sync.dma_start(out=raw[:], in_=inp_rows[:, :, halves[h]])
+            return raw
+
+        planes = [load_plane(0)]
+        inp_first = load_inp(0, FIRST_AT)
+        wg_raw = tile("wg_raw", [P, PACK, FEATURES], F32, WG_AT)
+        nc.sync.dma_start(out=wg_raw[:], in_=wg.rearrange("(p j) e -> p j e", j=PACK))
+        for t in range(1, PACK):
+            planes.append(load_plane(t))
+        inp_last = load_inp(1, LAST_AT)
+
+        got_words = tile("got_words", [P, SLOTS], U16)
+        got_scales = tile("got_scales", [P, SLOTS], U8)
         nc.vector.tensor_copy(got_words[:], key_words[:].indirect(offsets[:]))
+        nc.vector.tensor_copy(got_scales[:], key_scales[:].indirect(offsets[:]))
 
-        query_grouped = sb.tile([P, ROWS, PACK], BF16, align_bytes=64)
+        query_grouped = tile("query_grouped", [P, ROWS, PACK], BF16)
         interleave(nc.scalar.copy, query_grouped[:], query_raw[:])
-        q_codes, q_scales = quantize("query", query_grouped[:].rearrange("p c j -> p (c j)"), ROWS)
+        q_mx = quantize("query", query_grouped[:].rearrange("p c j -> p (c j)"), ROWS)
 
-        half_size = sb.tile([P, PACK], F32)
+        half_size = tile("half_size", [P, PACK], F32)
         nc.gpsimd.tensor_scalar(out=half_size[:], in0=size_cols[:], scalar1=0.5, scalar2=0.0, op0=ALU.mult, op1=ALU.add)
-        size_bank = ps.tile([P, PACK, P], F32)
+        size_bank = ps.tile([P, PACK, P], F32, tag="size")
         for r in range(PACK):
             nc.tensor.transpose(size_bank[:, r, :], half_size[:, r : r + 1].to_broadcast([P, P]), ident[:])
 
         score_banks = []
         for h in range(2):
-            bank = ps.tile([P, SLOTS], F32, name="acc", tag="acc", bufs=2)
-            nc.tensor.matmul_mx(
-                out=bank[:],
-                lhsT=q_codes[:, h * P : (h + 1) * P].bitcast(FP8X4),
-                lhsT_scale=q_scales[:, h * P : (h + 1) * P],
-                rhs=got_words[:].bitcast(FP4X4),
-                rhs_scale=got_scales[:],
-                start=True,
-                stop=True,
-            )
+            bank = ps.tile([P, SLOTS], F32, name="scores", tag="acc", bufs=2)
+            product(bank[:], q_mx, halves[h], (got_words, got_scales), FP4X4)
             score_banks.append(bank)
 
-        inp_grouped = sb.tile([P, ROWS, PACK], BF16, align_bytes=64)
-        interleave(nc.scalar.copy, inp_grouped[:], inp_raw[:])
+        def gather_plane(t, offset=None):
+            got = tile("got%d" % t, [P, SLOTS], BF16, offset)
+            nc.vector.tensor_copy(got[:], planes[t][:].indirect(offsets[:]))
+            bank = ps.tile([P, 2, P], F32, name="vT", tag="vT%d" % (t % 2))
+            for u in range(2):
+                nc.tensor.transpose(bank[:, u, :], got[:].bitcast(F32)[:, u::2], ident[:])
+            return bank
 
-        neg_max, probs, sums, weights = [], [], [], []
+        def group_plane(t, bank, offset=None):
+            grouped = tile("v_grouped%d" % t, [P, P * PACK], BF16, offset)
+            nc.scalar.copy(
+                out=grouped[:].bitcast(F32).rearrange("p (m u) -> p m u", u=2),
+                in_=bank[:].rearrange("p u m -> p m u"),
+            )
+            return grouped
+
+        def group_inp(h, raw, offset=None):
+            grouped = tile("inp_grouped%d" % h, [P, P, PACK], BF16, offset)
+            interleave(nc.scalar.copy, grouped[:], raw[:])
+            return grouped[:].rearrange("p c j -> p (c j)")
+
+        neg_max = []
         for h in range(2):
-            nm = sb.tile([P, 1], F32, name="neg_max%d" % h, tag="neg_max%d" % h, align_bytes=64)
+            nm = tile("neg_max%d" % h, [P, 1], F32)
             nc.vector.tensor_reduce(out=nm[:], in_=score_banks[h][:], axis=mybir.AxisListType.X, op=ALU.max, negate=True)
             neg_max.append(nm)
-        i_codes, i_scales = quantize("inp", inp_grouped[:].rearrange("p c j -> p (c j)"), ROWS)
+        v_bank0 = gather_plane(0)
+        first_grouped = group_inp(0, inp_first)
+        probs, sums = [], []
         for h in range(2):
-            pr = sb.tile([P, SLOTS], F32, name="probs%d" % h, tag="probs%d" % h)
-            sm = sb.tile([P, 1], F32, name="sum%d" % h)
+            pr = tile("probs%d" % h, [P, SLOTS], F32, FIRST_AT - 2 * KB + 64 + h * 2 * KB)
+            sm = tile("sum%d" % h, [P, 1], F32)
             nc.scalar.activation(out=pr[:], in_=score_banks[h][:], func=ACT.Exp, bias=neg_max[h][:], scale=1.0, accum_out=sm[:])
             probs.append(pr)
             sums.append(sm)
-        inv = []
+        first_mx = quantize("inp0", first_grouped, P)
+        w_bank = ps.tile([P, 2, 2, P], F32, tag="w")
         for h in range(2):
-            iv = sb.tile([P, 1], F32, name="inv%d" % h)
-            nc.vector.reciprocal(out=iv[:], in_=sums[h][:])
-            inv.append(iv)
-        w_bank = ps.tile([P, 2, 2, P], F32)
-        for h in range(2):
-            w = sb.tile([P, SLOTS], BF16, name="weights%d" % h)
+            inv = tile("inv%d" % h, [P, 1], F32)
+            nc.vector.reciprocal(out=inv[:], in_=sums[h][:])
+            w = tile("weights%d" % h, [P, SLOTS], BF16)
             nc.vector.scalar_tensor_tensor(
                 out=w[:].rearrange("p (s r) -> p s r", r=PACK),
                 in0=probs[h][:].rearrange("p (s r) -> p s r", r=PACK),
-                scalar=inv[h][:],
+                scalar=inv[:],
                 in1=size_bank[:].rearrange("p r s -> p s r"),
                 op0=ALU.mult,
                 op1=ALU.mult,
@@ -138,88 +182,66 @@ def tile_attend_gatedsoftmax_pl_kernel(tc, query, keys_words, keys_scales, size,
             for u in range(2):
                 nc.tensor.transpose(w_bank[:, h, u, :], w[:].bitcast(F32)[:, u::2], ident[:])
 
-        wg_grouped = sb.tile([P, PACK, P, PACK], BF16, tag="neg_max1", align_bytes=64)
-        w_grouped = sb.tile([P, ROWS * PACK], BF16, align_bytes=64)
-        nc.scalar.copy(
-            out=w_grouped[:].bitcast(F32).rearrange("p (h q u) -> p h q u", h=2, u=2),
-            in_=w_bank[:].rearrange("p h u q -> p h q u"),
-        )
+        wg_grouped = tile("wg_grouped", [P, PACK, P, PACK], BF16)
         for part in range(4):
             ms = slice(32 * part, 32 * (part + 1))
             nc.scalar.copy(
                 out=wg_grouped[:].rearrange("p t m j -> p m j t")[:, ms],
                 in_=wg_raw[:].rearrange("p j (m t) -> p m j t", t=PACK)[:, ms],
             )
-        w_codes, w_scales = quantize("w", w_grouped[:], ROWS)
-        g_codes, g_scales = quantize("wg", wg_grouped[:].rearrange("p t m j -> p (t m j)"), FEATURES)
-        gate = sb.tile([P, PACK, ROWS], F32)
-        for b in range(2):
-            z_bank = ps.tile([P, 2, ROWS], F32, name="z", tag="z", bufs=2)
-            for s in range(2):
-                cols = slice((2 * b + s) * P, (2 * b + s + 1) * P)
-                nc.tensor.matmul_mx(
-                    out=z_bank[:, s, :],
-                    lhsT=g_codes[:, cols].bitcast(FP8X4),
-                    lhsT_scale=g_scales[:, cols],
-                    rhs=i_codes[:].bitcast(FP8X4),
-                    rhs_scale=i_scales[:],
-                    start=True,
-                    stop=True,
-                )
-            nc.scalar.activation(out=gate[:, 2 * b : 2 * b + 2, :], in_=z_bank[:], func=ACT.Tanh, scale=0.5)
+        v_grouped0 = group_plane(0, v_bank0, WG_AT)
+        w_grouped = tile("w_grouped", [P, ROWS * PACK], BF16, WG_AT + KB)
+        nc.scalar.copy(
+            out=w_grouped[:].bitcast(F32).rearrange("p (h q u) -> p h q u", h=2, u=2),
+            in_=w_bank[:].rearrange("p h u q -> p h q u"),
+        )
+        v_grouped1 = group_plane(1, gather_plane(1))
+        g_mx = quantize("wg", wg_grouped[:].rearrange("p t m j -> p (t m j)"), FEATURES, PLANE_BYTES)
+        v_mx0 = quantize("v0", v_grouped0[:], P, PLANE_BYTES + 2 * KB)
+        w_mx = quantize("w", w_grouped[:], ROWS, PLANE_BYTES + 3 * KB)
+
+        gate = tile("gate", [P, PACK, ROWS], F32)
+
+        def make_gate(h, i_mx, ts, tag):
+            z_bank = ps.tile([P, ts.stop - ts.start, P], F32, name="z", tag=tag)
+            for t in range(ts.start, ts.stop):
+                product(z_bank[:, t - ts.start, :], g_mx, slice(t * P, (t + 1) * P), i_mx)
+            nc.scalar.activation(out=gate[:, ts, halves[h]], in_=z_bank[:], func=ACT.Tanh, scale=0.5)
+
+        make_gate(0, first_mx, slice(0, PACK), "z")
+        o_01 = ps.tile([P, 2, ROWS], F32, tag="acc", bufs=2)
+        product(o_01[:, 0, :], v_mx0, everything, w_mx)
+        v_grouped2 = group_plane(2, gather_plane(2))
+        product(o_01[:, 1, :], quantize("v1", v_grouped1[:], P, 2 * PLANE_BYTES), everything, w_mx)
+
+        v_bank3 = gather_plane(3)
+        last_grouped = group_inp(1, inp_last, LATE_BYTES)
+        v_grouped3 = group_plane(3, v_bank3, LAST_AT + KB)
+        last_mx = quantize("inp1", last_grouped, P)
+        make_gate(1, last_mx, slice(0, 2), "size")
+        make_gate(1, last_mx, slice(2, 4), "w")
+        v_mx2 = quantize("v2", v_grouped2[:], P, LATE_BYTES)
 
         out_planes = out_0.rearrange("(p t) q -> p t q", t=PACK)
-        v_grouped = []
-        for t in range(PACK):
-            if t == 0:
-                got = sb.tile([P, SLOTS], BF16, name="got0", tag="probs1")
-            else:
-                got = vp.tile(
-                    [P, SLOTS], BF16, name="got%d" % t, align_bytes=64, offset=(t - 1) * PLANE_BYTES + PLANE_BYTES // 2
-                )
-            nc.vector.tensor_copy(got[:], pools[t][:].indirect(offsets[:]))
-            v_bank = ps.tile([P, 2, P], F32, name="vT%d" % t, tag="vT%d" % (t % 2))
-            for u in range(2):
-                nc.tensor.transpose(v_bank[:, u, :], got[:].bitcast(F32)[:, u::2], ident[:])
-            grouped = sb.tile([P, P * PACK], BF16, name="v_grouped%d" % t, align_bytes=64)
-            nc.scalar.copy(
-                out=grouped[:].bitcast(F32).rearrange("p (m u) -> p m u", u=2),
-                in_=v_bank[:].rearrange("p u m -> p m u"),
-            )
-            v_grouped.append(grouped)
-        y = vp.tile([P, PACK, ROWS], F32, align_bytes=64, offset=(PACK - 1) * PLANE_BYTES + PLANE_BYTES // 2)
+        y = tile("y", [P, PACK, ROWS], F32, LATE_BYTES + KB // 2)
 
-        def gated_product(t, v_codes, v_scales, rows, tag, bufs):
-            o_bank = ps.tile([P, rows.stop - rows.start], F32, name="o", tag=tag, bufs=bufs)
-            nc.tensor.matmul_mx(
-                out=o_bank[:],
-                lhsT=v_codes[:].bitcast(FP8X4),
-                lhsT_scale=v_scales[:],
-                rhs=w_codes[:, rows].bitcast(FP8X4),
-                rhs_scale=w_scales[:, rows],
-                start=True,
-                stop=True,
-            )
+        def gated(ts, rows, o_view):
             nc.vector.scalar_tensor_tensor(
-                out=y[:, t, rows], in0=gate[:, t, rows], scalar=1.0, in1=o_bank[:], op0=ALU.add, op1=ALU.mult
+                out=y[:, ts, rows], in0=gate[:, ts, rows], scalar=1.0, in1=o_view, op0=ALU.add, op1=ALU.mult
             )
 
-        for t in range(PACK):
-            offset = (t + 1) * PLANE_BYTES if t + 1 < PACK else None
-            v_codes, v_scales = quantize("v%d" % t, v_grouped[t][:], P, offset)
-            if t < 2:
-                gated_product(t, v_codes, v_scales, slice(0, ROWS), "acc", 2)
-            elif t == 2:
-                gated_product(t, v_codes, v_scales, slice(0, ROWS), "vT1", 1)
-            else:
-                for h in range(2):
-                    gated_product(t, v_codes, v_scales, slice(h * P, (h + 1) * P), "acc", 2)
-            if t == 1:
-                nc.sync.dma_start(out=out_planes[:, 0:2, :], in_=y[:, 0:2, :])
-            elif t > 1:
-                nc.sync.dma_start(out=out_planes[:, t, :], in_=y[:, t, :])
+        gated(slice(0, 2), halves[0], o_01[:, :, halves[0]])
+        o_2 = ps.tile([P, ROWS], F32, tag="vT1")
+        product(o_2[:], v_mx2, everything, w_mx)
+        o_3 = ps.tile([P, ROWS], F32, tag="acc", bufs=2)
+        product(o_3[:], quantize("v3", v_grouped3[:], P), everything, w_mx)
+        gated(slice(0, 2), halves[1], o_01[:, :, halves[1]])
+        nc.sync.dma_start(out=out_planes[:, 0:2, :], in_=y[:, 0:2, :])
+        for t, o_bank in ((2, o_2), (3, o_3)):
+            gated(t, all_rows, o_bank[:])
+            nc.sync.dma_start(out=out_planes[:, t, :], in_=y[:, t, :])
 
-        y_grouped = sb.tile([P, ROWS, PACK], BF16, align_bytes=64)
+        y_grouped = tile("y_grouped", [P, ROWS, PACK], BF16)
         interleave(nc.scalar.copy, y_grouped[:, :SCALAR_ROWS, :], y[:, :, :SCALAR_ROWS])
         interleave(nc.vector.tensor_copy, y_grouped[:, SCALAR_ROWS:, :], y[:, :, SCALAR_ROWS:])
         y_codes, y_scales = quantize("y", y_grouped[:].rearrange("p c j -> p (c j)"), ROWS)

@@ -19,13 +19,12 @@ TOKENS = 2048
 SLOTS = 512
 ROWS = 256
 FEATURES = 512
-SCALAR_ROWS = 112
 KB = 1024
 PLANE_BYTES = TOKENS * 4
 WG_AT = PACK * PLANE_BYTES
-FIRST_AT = WG_AT + 10 * KB
-LAST_AT = FIRST_AT + 4 * KB
-LATE_BYTES = LAST_AT + 2 * KB
+INP_AT = WG_AT + 10 * KB
+SIZE_AT = INP_AT + 4 * KB
+LATE_BYTES = SIZE_AT + 64
 
 FLOPS = 3 * 2 * 512 * 512 * 256
 
@@ -55,13 +54,13 @@ def tile_attend_gatedsoftmax_pl_kernel(tc, query, keys_words, keys_scales, size,
             nc.vector.quantize_mx(out=codes[:].bitcast(FP8X4), scales=scales[:], in_=grouped)
             return codes, scales
 
-        def product(out, lhs, cols, rhs, rhs_dtype=FP8X4):
+        def product(out, lhs, cols, rhs, rhs_cols, rhs_dtype=FP8X4):
             nc.tensor.matmul_mx(
                 out=out,
                 lhsT=lhs[0][:, cols].bitcast(FP8X4),
                 lhsT_scale=lhs[1][:, cols],
-                rhs=rhs[0][:].bitcast(rhs_dtype),
-                rhs_scale=rhs[1][:],
+                rhs=rhs[0][:, rhs_cols].bitcast(rhs_dtype),
+                rhs_scale=rhs[1][:, rhs_cols],
                 start=True,
                 stop=True,
             )
@@ -81,33 +80,27 @@ def tile_attend_gatedsoftmax_pl_kernel(tc, query, keys_words, keys_scales, size,
             out=ident[:], in_=zeros[:, :P], compare_op=ALU.not_equal, fill=1.0, base=0, pattern=[[-1, P]], channel_multiplier=1
         )
         nc.sync.dma_start(offsets[:], offs)
-        size_cols = tile("size_cols", [P, PACK], F32)
-        nc.scalar.dma_start(out=size_cols[:], in_=size[0].rearrange("(p r) -> p r", r=PACK))
         for r in range(4):
             nc.scalar.dma_start(out=key_scales[r:P:32, :].bitcast(I32), in_=keys_scales[0, r:16:4, :].bitcast(I32))
         nc.sync.dma_start(out=key_words[:].bitcast(I32), in_=keys_words[0].bitcast(I32))
         query_raw = tile("query_raw", [P, PACK, ROWS], F32)
         nc.sync.dma_start(out=query_raw[:], in_=query.rearrange("(p j) q -> p j q", j=PACK))
         vals_planes = vals.rearrange("(m t) n -> t m n", t=PACK)
-        inp_rows = inp.rearrange("(p j) q -> p j q", j=PACK)
 
         def load_plane(t):
             plane = tile("vals%d" % t, [P, TOKENS], F32, t * PLANE_BYTES)
             nc.sync.dma_start(out=plane[:], in_=vals_planes[t])
             return plane
 
-        def load_inp(h, offset):
-            raw = tile("inp_raw%d" % h, [P, PACK, P], F32, offset)
-            nc.sync.dma_start(out=raw[:], in_=inp_rows[:, :, halves[h]])
-            return raw
-
         planes = [load_plane(0)]
-        inp_first = load_inp(0, FIRST_AT)
+        size_cols = tile("size_cols", [P, PACK], F32, SIZE_AT)
+        nc.sync.dma_start(out=size_cols[:], in_=size[0].rearrange("(p r) -> p r", r=PACK))
+        inp_raw = tile("inp_raw", [P, PACK, ROWS], F32, INP_AT)
+        nc.sync.dma_start(out=inp_raw[:], in_=inp.rearrange("(p j) q -> p j q", j=PACK))
         wg_raw = tile("wg_raw", [P, PACK, FEATURES], F32, WG_AT)
         nc.sync.dma_start(out=wg_raw[:], in_=wg.rearrange("(p j) e -> p j e", j=PACK))
         for t in range(1, PACK):
             planes.append(load_plane(t))
-        inp_last = load_inp(1, LAST_AT)
 
         got_words = tile("got_words", [P, SLOTS], U16)
         got_scales = tile("got_scales", [P, SLOTS], U8)
@@ -120,19 +113,22 @@ def tile_attend_gatedsoftmax_pl_kernel(tc, query, keys_words, keys_scales, size,
 
         half_size = tile("half_size", [P, PACK], F32)
         nc.gpsimd.tensor_scalar(out=half_size[:], in0=size_cols[:], scalar1=0.5, scalar2=0.0, op0=ALU.mult, op1=ALU.add)
-        size_bank = ps.tile([P, PACK, P], F32, tag="size")
+        size_bank = ps.tile([P, PACK, P], F32, tag="vT0")
         for r in range(PACK):
             nc.tensor.transpose(size_bank[:, r, :], half_size[:, r : r + 1].to_broadcast([P, P]), ident[:])
 
         score_banks = []
         for h in range(2):
             bank = ps.tile([P, SLOTS], F32, name="scores", tag="acc", bufs=2)
-            product(bank[:], q_mx, halves[h], (got_words, got_scales), FP4X4)
+            product(bank[:], q_mx, halves[h], (got_words, got_scales), slice(0, SLOTS), FP4X4)
             score_banks.append(bank)
 
         def gather_plane(t, offset=None):
             got = tile("got%d" % t, [P, SLOTS], BF16, offset)
             nc.vector.tensor_copy(got[:], planes[t][:].indirect(offsets[:]))
+            return got
+
+        def turn_plane(t, got):
             bank = ps.tile([P, 2, P], F32, name="vT", tag="vT%d" % (t % 2))
             for u in range(2):
                 nc.tensor.transpose(bank[:, u, :], got[:].bitcast(F32)[:, u::2], ident[:])
@@ -146,26 +142,22 @@ def tile_attend_gatedsoftmax_pl_kernel(tc, query, keys_words, keys_scales, size,
             )
             return grouped
 
-        def group_inp(h, raw, offset=None):
-            grouped = tile("inp_grouped%d" % h, [P, P, PACK], BF16, offset)
-            interleave(nc.scalar.copy, grouped[:], raw[:])
-            return grouped[:].rearrange("p c j -> p (c j)")
-
         neg_max = []
         for h in range(2):
             nm = tile("neg_max%d" % h, [P, 1], F32)
             nc.vector.tensor_reduce(out=nm[:], in_=score_banks[h][:], axis=mybir.AxisListType.X, op=ALU.max, negate=True)
             neg_max.append(nm)
-        v_bank0 = gather_plane(0)
-        first_grouped = group_inp(0, inp_first)
+        got0 = gather_plane(0)
+        inp_grouped = tile("inp_grouped", [P, ROWS, PACK], BF16)
+        interleave(nc.scalar.copy, inp_grouped[:], inp_raw[:])
         probs, sums = [], []
         for h in range(2):
-            pr = tile("probs%d" % h, [P, SLOTS], F32, FIRST_AT - 2 * KB + 64 + h * 2 * KB)
+            pr = tile("probs%d" % h, [P, SLOTS], F32, INP_AT - 2 * KB + 64 + h * 2 * KB)
             sm = tile("sum%d" % h, [P, 1], F32)
             nc.scalar.activation(out=pr[:], in_=score_banks[h][:], func=ACT.Exp, bias=neg_max[h][:], scale=1.0, accum_out=sm[:])
             probs.append(pr)
             sums.append(sm)
-        first_mx = quantize("inp0", first_grouped, P)
+        inp_mx = quantize("inp", inp_grouped[:].rearrange("p c j -> p (c j)"), ROWS)
         w_bank = ps.tile([P, 2, 2, P], F32, tag="w")
         for h in range(2):
             inv = tile("inv%d" % h, [P, 1], F32)
@@ -189,62 +181,63 @@ def tile_attend_gatedsoftmax_pl_kernel(tc, query, keys_words, keys_scales, size,
                 out=wg_grouped[:].rearrange("p t m j -> p m j t")[:, ms],
                 in_=wg_raw[:].rearrange("p j (m t) -> p m j t", t=PACK)[:, ms],
             )
-        v_grouped0 = group_plane(0, v_bank0, WG_AT)
+        v_grouped0 = group_plane(0, turn_plane(0, got0), WG_AT)
         w_grouped = tile("w_grouped", [P, ROWS * PACK], BF16, WG_AT + KB)
         nc.scalar.copy(
             out=w_grouped[:].bitcast(F32).rearrange("p (h q u) -> p h q u", h=2, u=2),
             in_=w_bank[:].rearrange("p h u q -> p h q u"),
         )
-        v_grouped1 = group_plane(1, gather_plane(1))
+        v_grouped1 = group_plane(1, turn_plane(1, gather_plane(1)))
         g_mx = quantize("wg", wg_grouped[:].rearrange("p t m j -> p (t m j)"), FEATURES, PLANE_BYTES)
         v_mx0 = quantize("v0", v_grouped0[:], P, PLANE_BYTES + 2 * KB)
         w_mx = quantize("w", w_grouped[:], ROWS, PLANE_BYTES + 3 * KB)
 
         gate = tile("gate", [P, PACK, ROWS], F32)
+        for b in range(2):
+            z_bank = ps.tile([P, 2, ROWS], F32, name="z", tag="z", bufs=2)
+            for s in range(2):
+                product(z_bank[:, s, :], g_mx, slice((2 * b + s) * P, (2 * b + s + 1) * P), inp_mx, all_rows)
+            nc.scalar.activation(out=gate[:, 2 * b : 2 * b + 2, :], in_=z_bank[:], func=ACT.Tanh, scale=0.5)
 
-        def make_gate(h, i_mx, ts, tag):
-            z_bank = ps.tile([P, ts.stop - ts.start, P], F32, name="z", tag=tag)
-            for t in range(ts.start, ts.stop):
-                product(z_bank[:, t - ts.start, :], g_mx, slice(t * P, (t + 1) * P), i_mx)
-            nc.scalar.activation(out=gate[:, ts, halves[h]], in_=z_bank[:], func=ACT.Tanh, scale=0.5)
-
-        make_gate(0, first_mx, slice(0, PACK), "z")
         o_01 = ps.tile([P, 2, ROWS], F32, tag="acc", bufs=2)
-        product(o_01[:, 0, :], v_mx0, everything, w_mx)
-        v_grouped2 = group_plane(2, gather_plane(2))
-        product(o_01[:, 1, :], quantize("v1", v_grouped1[:], P, 2 * PLANE_BYTES), everything, w_mx)
-
-        v_bank3 = gather_plane(3)
-        last_grouped = group_inp(1, inp_last, LATE_BYTES)
-        v_grouped3 = group_plane(3, v_bank3, LAST_AT + KB)
-        last_mx = quantize("inp1", last_grouped, P)
-        make_gate(1, last_mx, slice(0, 2), "size")
-        make_gate(1, last_mx, slice(2, 4), "w")
-        v_mx2 = quantize("v2", v_grouped2[:], P, LATE_BYTES)
+        product(o_01[:, 0, :], v_mx0, everything, w_mx, all_rows)
+        v_grouped2 = group_plane(2, turn_plane(2, gather_plane(2)))
+        product(o_01[:, 1, :], quantize("v1", v_grouped1[:], P, 2 * PLANE_BYTES), everything, w_mx, all_rows)
+        v_grouped3 = group_plane(3, turn_plane(3, gather_plane(3)))
+        v_mx2 = quantize("v2", v_grouped2[:], P, 3 * PLANE_BYTES)
 
         out_planes = out_0.rearrange("(p t) q -> p t q", t=PACK)
-        y = tile("y", [P, PACK, ROWS], F32, LATE_BYTES + KB // 2)
+        y = tile("y", [P, PACK, ROWS], F32, 3 * PLANE_BYTES + KB)
 
         def gated(ts, rows, o_view):
             nc.vector.scalar_tensor_tensor(
                 out=y[:, ts, rows], in0=gate[:, ts, rows], scalar=1.0, in1=o_view, op0=ALU.add, op1=ALU.mult
             )
 
-        gated(slice(0, 2), halves[0], o_01[:, :, halves[0]])
-        o_2 = ps.tile([P, ROWS], F32, tag="vT1")
-        product(o_2[:], v_mx2, everything, w_mx)
-        o_3 = ps.tile([P, ROWS], F32, tag="acc", bufs=2)
-        product(o_3[:], quantize("v3", v_grouped3[:], P), everything, w_mx)
-        gated(slice(0, 2), halves[1], o_01[:, :, halves[1]])
+        gated(slice(0, 2), all_rows, o_01[:])
         nc.sync.dma_start(out=out_planes[:, 0:2, :], in_=y[:, 0:2, :])
-        for t, o_bank in ((2, o_2), (3, o_3)):
-            gated(t, all_rows, o_bank[:])
-            nc.sync.dma_start(out=out_planes[:, t, :], in_=y[:, t, :])
+        o_2 = ps.tile([P, ROWS], F32, tag="vT1")
+        product(o_2[:], v_mx2, everything, w_mx, all_rows)
+        v_mx3 = quantize("v3", v_grouped3[:], P)
+        gated(2, all_rows, o_2[:])
+        nc.sync.dma_start(out=out_planes[:, 2, :], in_=y[:, 2, :])
+        for h, tag in enumerate(("size", "w")):
+            o_3 = ps.tile([P, P], F32, name="o_3", tag=tag)
+            product(o_3[:], v_mx3, everything, w_mx, halves[h])
+            gated(3, halves[h], o_3[:])
+        nc.sync.dma_start(out=out_planes[:, 3, :], in_=y[:, 3, :])
 
         y_grouped = tile("y_grouped", [P, ROWS, PACK], BF16)
-        interleave(nc.scalar.copy, y_grouped[:, :SCALAR_ROWS, :], y[:, :, :SCALAR_ROWS])
-        interleave(nc.vector.tensor_copy, y_grouped[:, SCALAR_ROWS:, :], y[:, :, SCALAR_ROWS:])
-        y_codes, y_scales = quantize("y", y_grouped[:].rearrange("p c j -> p (c j)"), ROWS)
+        y_codes = tile("y_codes", [P, ROWS], U32)
+        y_scales = tile("y_scales", [P, ROWS], U8)
+        for rows, copy in zip(halves, (nc.scalar.copy, nc.vector.tensor_copy)):
+            interleave(copy, y_grouped[:, rows, :], y[:, :, rows])
+        for rows in halves:
+            nc.vector.quantize_mx(
+                out=y_codes[:, rows].bitcast(FP8X4),
+                scales=y_scales[:, rows],
+                in_=y_grouped[:, rows, :].rearrange("p c j -> p (c j)"),
+            )
         nc.sync.dma_start(out=out_1[0].rearrange("p n t -> p (n t)").bitcast(I32), in_=y_codes[:].bitcast(I32))
         for r in range(4):
             queue = nc.scalar if r % 2 == 0 else nc.sync

@@ -1,6 +1,7 @@
 from contextlib import ExitStack
 
 import concourse.mybir as mybir
+from concourse.masks import make_identity
 
 F32 = mybir.dt.float32
 BF16 = mybir.dt.bfloat16
@@ -22,7 +23,7 @@ FEATURES = 512
 KB = 1024
 PLANE_BYTES = TOKENS * 4
 WG_AT = PACK * PLANE_BYTES
-INP_AT = WG_AT + 10 * KB
+INP_AT = WG_AT + 8 * KB
 SIZE_AT = INP_AT + 4 * KB
 LATE_BYTES = SIZE_AT + 64
 
@@ -70,18 +71,18 @@ def tile_attend_gatedsoftmax_pl_kernel(tc, query, keys_words, keys_scales, size,
         all_rows = slice(0, ROWS)
 
         key_words = tile("key_words", [P, TOKENS], U16)
-        key_scales = tile("key_scales", [P, TOKENS], U8)
+        key_scales = tile("key_scales", [P, LATE_BYTES - PLANE_BYTES], U8, PLANE_BYTES)
+        scale_window = key_scales[:, :TOKENS]
         offsets = sb.tile([P, SLOTS // 16], U16)
-        nc.gpsimd.memset(key_scales[:].bitcast(I32), 0)
+        nc.gpsimd.memset(scale_window[0:16, :].bitcast(I32), 0)
+        nc.vector.memset(scale_window[32:64, :].bitcast(I32), 0)
+        nc.vector.memset(scale_window[64:P, :].bitcast(I32), 0)
+        slot_scales = tile("slot_scales", [P, SLOTS], U8)
+        nc.gpsimd.memset(slot_scales[:].bitcast(I32), 0)
         ident = tile("ident", [P, P], F32)
-        zeros = tile("zeros", [P, LATE_BYTES // 4], F32, 0)
-        nc.gpsimd.memset(zeros[:, :P], 0.0)
-        nc.gpsimd.affine_select(
-            out=ident[:], in_=zeros[:, :P], compare_op=ALU.not_equal, fill=1.0, base=0, pattern=[[-1, P]], channel_multiplier=1
-        )
+        make_identity(nc, ident[:])
         nc.sync.dma_start(offsets[:], offs)
-        for r in range(4):
-            nc.scalar.dma_start(out=key_scales[r:P:32, :].bitcast(I32), in_=keys_scales[0, r:16:4, :].bitcast(I32))
+        nc.scalar.dma_start(out=scale_window[16:32, :].bitcast(I32), in_=keys_scales[0].bitcast(I32))
         nc.sync.dma_start(out=key_words[:].bitcast(I32), in_=keys_words[0].bitcast(I32))
         query_raw = tile("query_raw", [P, PACK, ROWS], F32)
         nc.sync.dma_start(out=query_raw[:], in_=query.rearrange("(p j) q -> p j q", j=PACK))
@@ -93,6 +94,13 @@ def tile_attend_gatedsoftmax_pl_kernel(tc, query, keys_words, keys_scales, size,
             return plane
 
         planes = [load_plane(0)]
+        got_scales = tile("got_scales", [P, SLOTS], U8)
+        nc.vector.tensor_copy(got_scales[:], scale_window.indirect(offsets[:]))
+        for quad in range(4):
+            nc.sync.dma_start(
+                out=slot_scales[32 * quad : 32 * quad + 4, :].bitcast(I32),
+                in_=got_scales[16 + 4 * quad : 20 + 4 * quad, :].bitcast(I32),
+            )
         size_cols = tile("size_cols", [P, PACK], F32, SIZE_AT)
         nc.sync.dma_start(out=size_cols[:], in_=size[0].rearrange("(p r) -> p r", r=PACK))
         inp_raw = tile("inp_raw", [P, PACK, ROWS], F32, INP_AT)
@@ -103,11 +111,9 @@ def tile_attend_gatedsoftmax_pl_kernel(tc, query, keys_words, keys_scales, size,
             planes.append(load_plane(t))
 
         got_words = tile("got_words", [P, SLOTS], U16)
-        got_scales = tile("got_scales", [P, SLOTS], U8)
         nc.vector.tensor_copy(got_words[:], key_words[:].indirect(offsets[:]))
-        nc.vector.tensor_copy(got_scales[:], key_scales[:].indirect(offsets[:]))
 
-        query_grouped = tile("query_grouped", [P, ROWS, PACK], BF16)
+        query_grouped = tile("query_grouped", [P, ROWS, PACK], BF16, LATE_BYTES)
         interleave(nc.scalar.copy, query_grouped[:], query_raw[:])
         q_mx = quantize("query", query_grouped[:].rearrange("p c j -> p (c j)"), ROWS)
 
@@ -120,7 +126,7 @@ def tile_attend_gatedsoftmax_pl_kernel(tc, query, keys_words, keys_scales, size,
         score_banks = []
         for h in range(2):
             bank = ps.tile([P, SLOTS], F32, name="scores", tag="acc", bufs=2)
-            product(bank[:], q_mx, halves[h], (got_words, got_scales), slice(0, SLOTS), FP4X4)
+            product(bank[:], q_mx, halves[h], (got_words, slot_scales), slice(0, SLOTS), FP4X4)
             score_banks.append(bank)
 
         def gather_plane(t, offset=None):
@@ -147,12 +153,12 @@ def tile_attend_gatedsoftmax_pl_kernel(tc, query, keys_words, keys_scales, size,
             nm = tile("neg_max%d" % h, [P, 1], F32)
             nc.vector.tensor_reduce(out=nm[:], in_=score_banks[h][:], axis=mybir.AxisListType.X, op=ALU.max, negate=True)
             neg_max.append(nm)
-        got0 = gather_plane(0)
+        got0 = gather_plane(0, LATE_BYTES)
         inp_grouped = tile("inp_grouped", [P, ROWS, PACK], BF16)
         interleave(nc.scalar.copy, inp_grouped[:], inp_raw[:])
         probs, sums = [], []
         for h in range(2):
-            pr = tile("probs%d" % h, [P, SLOTS], F32, INP_AT - 2 * KB + 64 + h * 2 * KB)
+            pr = tile("probs%d" % h, [P, SLOTS], F32)
             sm = tile("sum%d" % h, [P, 1], F32)
             nc.scalar.activation(out=pr[:], in_=score_banks[h][:], func=ACT.Exp, bias=neg_max[h][:], scale=1.0, accum_out=sm[:])
             probs.append(pr)

@@ -236,7 +236,11 @@ def tile_attend_gatedsoftmax_pl_kernel(tc, query, keys_words, keys_scales, size,
         y_grouped = tile("y_grouped", [P, ROWS, PACK], BF16)
         y_codes = tile("y_codes", [P, ROWS], U32)
         y_scales = tile("y_scales", [P, ROWS], U8)
-        for rows, copy in zip(halves, (nc.scalar.copy, nc.vector.tensor_copy)):
+        for rows, copy in (
+            (slice(0, P // 2), nc.scalar.copy),
+            (slice(P // 2, P), nc.vector.tensor_copy),
+            (halves[1], nc.vector.tensor_copy),
+        ):
             interleave(copy, y_grouped[:, rows, :], y[:, :, rows])
         for rows in halves:
             nc.vector.quantize_mx(

@@ -23,9 +23,7 @@ FEATURES = 512
 KB = 1024
 PLANE_BYTES = TOKENS * 4
 WG_AT = PACK * PLANE_BYTES
-INP_AT = WG_AT + 8 * KB
-SIZE_AT = INP_AT + 4 * KB
-LATE_BYTES = SIZE_AT + 64
+SPARE_AT = WG_AT + 8 * KB
 
 FLOPS = 3 * 2 * 512 * 512 * 256
 
@@ -71,8 +69,8 @@ def tile_attend_gatedsoftmax_pl_kernel(tc, query, keys_words, keys_scales, size,
         all_rows = slice(0, ROWS)
 
         key_words = tile("key_words", [P, TOKENS], U16)
-        key_scales = tile("key_scales", [P, LATE_BYTES - PLANE_BYTES], U8, PLANE_BYTES)
-        scale_window = key_scales[:, :TOKENS]
+        key_scales = tile("key_scales", [P, TOKENS], U8)
+        scale_window = key_scales[:]
         offsets = sb.tile([P, SLOTS // 16], U16)
         nc.gpsimd.memset(scale_window[0:16, :].bitcast(I32), 0)
         nc.vector.memset(scale_window[32:64, :].bitcast(I32), 0)
@@ -101,9 +99,9 @@ def tile_attend_gatedsoftmax_pl_kernel(tc, query, keys_words, keys_scales, size,
                 out=slot_scales[32 * quad : 32 * quad + 4, :].bitcast(I32),
                 in_=got_scales[16 + 4 * quad : 20 + 4 * quad, :].bitcast(I32),
             )
-        size_cols = tile("size_cols", [P, PACK], F32, SIZE_AT)
+        size_cols = tile("size_cols", [P, PACK], F32)
         nc.sync.dma_start(out=size_cols[:], in_=size[0].rearrange("(p r) -> p r", r=PACK))
-        inp_raw = tile("inp_raw", [P, PACK, ROWS], F32, INP_AT)
+        inp_raw = tile("inp_raw", [P, PACK, ROWS], F32)
         nc.sync.dma_start(out=inp_raw[:], in_=inp.rearrange("(p j) q -> p j q", j=PACK))
         wg_raw = tile("wg_raw", [P, PACK, FEATURES], F32, WG_AT)
         nc.sync.dma_start(out=wg_raw[:], in_=wg.rearrange("(p j) e -> p j e", j=PACK))
@@ -113,7 +111,7 @@ def tile_attend_gatedsoftmax_pl_kernel(tc, query, keys_words, keys_scales, size,
         got_words = tile("got_words", [P, SLOTS], U16)
         nc.vector.tensor_copy(got_words[:], key_words[:].indirect(offsets[:]))
 
-        query_grouped = tile("query_grouped", [P, ROWS, PACK], BF16, LATE_BYTES)
+        query_grouped = tile("query_grouped", [P, ROWS, PACK], BF16, SPARE_AT)
         interleave(nc.scalar.copy, query_grouped[:], query_raw[:])
         q_mx = quantize("query", query_grouped[:].rearrange("p c j -> p (c j)"), ROWS)
 
@@ -135,7 +133,10 @@ def tile_attend_gatedsoftmax_pl_kernel(tc, query, keys_words, keys_scales, size,
             return got
 
         def turn_plane(t, got):
-            bank = ps.tile([P, 2, P], F32, name="vT", tag="vT%d" % (t % 2))
+            if t == 0:
+                bank = ps.tile([P, 2, P], F32, name="vT", tag="acc", bufs=2)
+            else:
+                bank = ps.tile([P, 2, P], F32, name="vT", tag="vT%d" % (t % 2))
             for u in range(2):
                 nc.tensor.transpose(bank[:, u, :], got[:].bitcast(F32)[:, u::2], ident[:])
             return bank
@@ -153,26 +154,27 @@ def tile_attend_gatedsoftmax_pl_kernel(tc, query, keys_words, keys_scales, size,
             nm = tile("neg_max%d" % h, [P, 1], F32)
             nc.vector.tensor_reduce(out=nm[:], in_=score_banks[h][:], axis=mybir.AxisListType.X, op=ALU.max, negate=True)
             neg_max.append(nm)
-        got0 = gather_plane(0, LATE_BYTES)
+        got0 = gather_plane(0, SPARE_AT)
         inp_grouped = tile("inp_grouped", [P, ROWS, PACK], BF16)
-        interleave(nc.scalar.copy, inp_grouped[:], inp_raw[:])
-        probs, sums = [], []
+        interleave(nc.vector.tensor_copy, inp_grouped[:], inp_raw[:])
+        probs = []
+        sums = tile("sums", [P, 2], F32)
         for h in range(2):
-            pr = tile("probs%d" % h, [P, SLOTS], F32)
-            sm = tile("sum%d" % h, [P, 1], F32)
-            nc.scalar.activation(out=pr[:], in_=score_banks[h][:], func=ACT.Exp, bias=neg_max[h][:], scale=1.0, accum_out=sm[:])
+            pr = tile("probs%d" % h, [P, SLOTS], F32, SPARE_AT + (2 + 2 * h) * KB)
+            nc.scalar.activation(
+                out=pr[:], in_=score_banks[h][:], func=ACT.Exp, bias=neg_max[h][:], scale=1.0, accum_out=sums[:, h : h + 1]
+            )
             probs.append(pr)
-            sums.append(sm)
-        inp_mx = quantize("inp", inp_grouped[:].rearrange("p c j -> p (c j)"), ROWS)
+        v_grouped0 = group_plane(0, turn_plane(0, got0))
+        inv = tile("inv", [P, 2], F32)
+        nc.vector.reciprocal(out=inv[:], in_=sums[:])
         w_bank = ps.tile([P, 2, 2, P], F32, tag="w")
         for h in range(2):
-            inv = tile("inv%d" % h, [P, 1], F32)
-            nc.vector.reciprocal(out=inv[:], in_=sums[h][:])
             w = tile("weights%d" % h, [P, SLOTS], BF16)
             nc.vector.scalar_tensor_tensor(
                 out=w[:].rearrange("p (s r) -> p s r", r=PACK),
                 in0=probs[h][:].rearrange("p (s r) -> p s r", r=PACK),
-                scalar=inv[:],
+                scalar=inv[:, h : h + 1],
                 in1=size_bank[:].rearrange("p r s -> p s r"),
                 op0=ALU.mult,
                 op1=ALU.mult,
@@ -180,34 +182,40 @@ def tile_attend_gatedsoftmax_pl_kernel(tc, query, keys_words, keys_scales, size,
             for u in range(2):
                 nc.tensor.transpose(w_bank[:, h, u, :], w[:].bitcast(F32)[:, u::2], ident[:])
 
-        wg_grouped = tile("wg_grouped", [P, PACK, P, PACK], BF16)
-        for part in range(4):
-            ms = slice(32 * part, 32 * (part + 1))
+        inp_mx = quantize("inp", inp_grouped[:].rearrange("p c j -> p (c j)"), ROWS, SPARE_AT + 4 * KB)
+        v_mx0 = quantize("v0", v_grouped0[:], P, SPARE_AT + 5 * KB)
+
+        def group_gate_weights(b, offset):
+            grouped = tile("wg_grouped%d" % b, [P, 2, P, PACK], BF16, offset)
             nc.scalar.copy(
-                out=wg_grouped[:].rearrange("p t m j -> p m j t")[:, ms],
-                in_=wg_raw[:].rearrange("p j (m t) -> p m j t", t=PACK)[:, ms],
+                out=grouped[:].rearrange("p t m j -> p m j t"),
+                in_=wg_raw[:].rearrange("p j (m t) -> p m j t", t=PACK)[:, :, :, 2 * b : 2 * b + 2],
             )
-        v_grouped0 = group_plane(0, turn_plane(0, got0), WG_AT)
-        w_grouped = tile("w_grouped", [P, ROWS * PACK], BF16, WG_AT + KB)
+            return grouped[:].rearrange("p t m j -> p (t m j)")
+
+        g_mx0 = quantize("wg0", group_gate_weights(0, SPARE_AT + 7 * KB), 2 * P)
+        w_grouped = tile("w_grouped", [P, ROWS * PACK], BF16, SPARE_AT + 6 * KB)
         nc.scalar.copy(
             out=w_grouped[:].bitcast(F32).rearrange("p (h q u) -> p h q u", h=2, u=2),
             in_=w_bank[:].rearrange("p h u q -> p h q u"),
         )
+        wg_grouped1 = group_gate_weights(1, SPARE_AT + 8 * KB)
         v_grouped1 = group_plane(1, turn_plane(1, gather_plane(1)))
-        g_mx = quantize("wg", wg_grouped[:].rearrange("p t m j -> p (t m j)"), FEATURES, PLANE_BYTES)
-        v_mx0 = quantize("v0", v_grouped0[:], P, PLANE_BYTES + 2 * KB)
-        w_mx = quantize("w", w_grouped[:], ROWS, PLANE_BYTES + 3 * KB)
+        w_mx = quantize("w", w_grouped[:], ROWS, PLANE_BYTES)
 
         gate = tile("gate", [P, PACK, ROWS], F32)
-        for b in range(2):
+
+        def gate_pair(b, g_mx):
             z_bank = ps.tile([P, 2, ROWS], F32, name="z", tag="z", bufs=2)
             for s in range(2):
-                product(z_bank[:, s, :], g_mx, slice((2 * b + s) * P, (2 * b + s + 1) * P), inp_mx, all_rows)
+                product(z_bank[:, s, :], g_mx, halves[s], inp_mx, all_rows)
             nc.scalar.activation(out=gate[:, 2 * b : 2 * b + 2, :], in_=z_bank[:], func=ACT.Tanh, scale=0.5)
 
+        gate_pair(0, g_mx0)
         o_01 = ps.tile([P, 2, ROWS], F32, tag="acc", bufs=2)
         product(o_01[:, 0, :], v_mx0, everything, w_mx, all_rows)
         v_grouped2 = group_plane(2, turn_plane(2, gather_plane(2)))
+        gate_pair(1, quantize("wg1", wg_grouped1, 2 * P, 2 * PLANE_BYTES + KB))
         product(o_01[:, 1, :], quantize("v1", v_grouped1[:], P, 2 * PLANE_BYTES), everything, w_mx, all_rows)
         v_grouped3 = group_plane(3, turn_plane(3, gather_plane(3)))
         v_mx2 = quantize("v2", v_grouped2[:], P, 3 * PLANE_BYTES)

@@ -217,39 +217,37 @@ def tile_attend_gatedsoftmax_pl_kernel(tc, query, keys_words, keys_scales, size,
         v_grouped2 = group_plane(2, turn_plane(2, gather_plane(2)))
         gate_pair(1, quantize("wg1", wg_grouped1, 2 * P, 2 * PLANE_BYTES + KB))
         product(o_01[:, 1, :], quantize("v1", v_grouped1[:], P, 2 * PLANE_BYTES), everything, w_mx, all_rows)
-        v_grouped3 = group_plane(3, turn_plane(3, gather_plane(3)))
+        v_grouped3 = group_plane(3, turn_plane(3, gather_plane(3)), SPARE_AT)
         v_mx2 = quantize("v2", v_grouped2[:], P, 3 * PLANE_BYTES)
 
         out_planes = out_0.rearrange("(p t) q -> p t q", t=PACK)
-        y = tile("y", [P, PACK, ROWS], F32, 3 * PLANE_BYTES + KB)
+        y01 = tile("y01", [P, 2, ROWS], F32, 3 * PLANE_BYTES + KB)
+        y23 = tile("y23", [P, 2, ROWS], F32, SPARE_AT)
 
-        def gated(ts, rows, o_view):
+        def gated(out, ts, rows, o_view):
             nc.vector.scalar_tensor_tensor(
-                out=y[:, ts, rows], in0=gate[:, ts, rows], scalar=1.0, in1=o_view, op0=ALU.add, op1=ALU.mult
+                out=out, in0=gate[:, ts, rows], scalar=1.0, in1=o_view, op0=ALU.add, op1=ALU.mult
             )
 
-        gated(slice(0, 2), all_rows, o_01[:])
-        nc.sync.dma_start(out=out_planes[:, 0:2, :], in_=y[:, 0:2, :])
-        o_2 = ps.tile([P, ROWS], F32, tag="vT1")
+        gated(y01[:], slice(0, 2), all_rows, o_01[:])
+        nc.sync.dma_start(out=out_planes[:, 0:2, :], in_=y01[:])
+        o_2 = ps.tile([P, ROWS], F32, tag="acc", bufs=2)
         product(o_2[:], v_mx2, everything, w_mx, all_rows)
         v_mx3 = quantize("v3", v_grouped3[:], P)
-        gated(2, all_rows, o_2[:])
-        nc.sync.dma_start(out=out_planes[:, 2, :], in_=y[:, 2, :])
+        gated(y23[:, 0, :], 2, all_rows, o_2[:])
+        nc.sync.dma_start(out=out_planes[:, 2, :], in_=y23[:, 0, :])
         for h, tag in enumerate(("size", "w")):
             o_3 = ps.tile([P, P], F32, name="o_3", tag=tag)
             product(o_3[:], v_mx3, everything, w_mx, halves[h])
-            gated(3, halves[h], o_3[:])
-        nc.sync.dma_start(out=out_planes[:, 3, :], in_=y[:, 3, :])
+            gated(y23[:, 1, halves[h]], 3, halves[h], o_3[:])
+        nc.sync.dma_start(out=out_planes[:, 3, :], in_=y23[:, 1, :])
 
         y_grouped = tile("y_grouped", [P, ROWS, PACK], BF16)
         y_codes = tile("y_codes", [P, ROWS], U32)
         y_scales = tile("y_scales", [P, ROWS], U8)
-        for rows, copy in (
-            (slice(0, P // 2), nc.scalar.copy),
-            (slice(P // 2, P), nc.vector.tensor_copy),
-            (halves[1], nc.vector.tensor_copy),
-        ):
-            interleave(copy, y_grouped[:, rows, :], y[:, :, rows])
+        interleave(nc.scalar.copy, y_grouped[:, :, 0:2], y01[:])
+        for rows in halves:
+            interleave(nc.vector.tensor_copy, y_grouped[:, rows, 2:4], y23[:, :, rows])
         for rows in halves:
             nc.vector.quantize_mx(
                 out=y_codes[:, rows].bitcast(FP8X4),

@@ -22,8 +22,9 @@ ROWS = 256
 FEATURES = 512
 KB = 1024
 PLANE_BYTES = TOKENS * 4
-WG_AT = PACK * PLANE_BYTES
-SPARE_AT = WG_AT + 8 * KB
+INP_AT = PACK * PLANE_BYTES
+INP_GROUPED_AT = INP_AT + 4 * KB
+QUERY_GROUPED_AT = INP_GROUPED_AT + 2 * KB
 
 FLOPS = 3 * 2 * 512 * 512 * 256
 
@@ -39,13 +40,16 @@ def tile_attend_gatedsoftmax_pl_kernel(tc, query, keys_words, keys_scales, size,
     nc = tc.nc
     with ExitStack() as ctx:
         sb = ctx.enter_context(tc.tile_pool(name="sb", bufs=1))
-        vp = ctx.enter_context(tc.tile_pool(name="vp", bufs=1))
+        placed = ctx.enter_context(tc.tile_pool(name="placed", bufs=1))
         ps = ctx.enter_context(tc.psum_pool(name="ps", bufs=1))
 
         def tile(name, shape, dtype, offset=None):
             if offset is None:
                 return sb.tile(shape, dtype, name=name, align_bytes=64)
-            return vp.tile(shape, dtype, name=name, align_bytes=64, offset=offset)
+            return placed.tile(shape, dtype, name=name, align_bytes=64, offset=offset)
+
+        def bank(number, name, shape):
+            return ps.tile(shape, F32, name=name, tag="bank%d" % number)
 
         def quantize(name, grouped, width, offset=None):
             codes = tile(name + "_codes", [P, width], U32, offset)
@@ -70,17 +74,16 @@ def tile_attend_gatedsoftmax_pl_kernel(tc, query, keys_words, keys_scales, size,
 
         key_words = tile("key_words", [P, TOKENS], U16)
         key_scales = tile("key_scales", [P, TOKENS], U8)
-        scale_window = key_scales[:]
         offsets = sb.tile([P, SLOTS // 16], U16)
-        nc.gpsimd.memset(scale_window[0:16, :].bitcast(I32), 0)
-        nc.vector.memset(scale_window[32:64, :].bitcast(I32), 0)
-        nc.vector.memset(scale_window[64:P, :].bitcast(I32), 0)
+        nc.gpsimd.memset(key_scales[0:16, :].bitcast(I32), 0)
+        nc.vector.memset(key_scales[32:64, :].bitcast(I32), 0)
+        nc.vector.memset(key_scales[64:P, :].bitcast(I32), 0)
         slot_scales = tile("slot_scales", [P, SLOTS], U8)
         nc.gpsimd.memset(slot_scales[:].bitcast(I32), 0)
         ident = tile("ident", [P, P], F32)
         make_identity(nc, ident[:])
         nc.sync.dma_start(offsets[:], offs)
-        nc.scalar.dma_start(out=scale_window[16:32, :].bitcast(I32), in_=keys_scales[0].bitcast(I32))
+        nc.scalar.dma_start(out=key_scales[16:32, :].bitcast(I32), in_=keys_scales[0].bitcast(I32))
         nc.sync.dma_start(out=key_words[:].bitcast(I32), in_=keys_words[0].bitcast(I32))
         query_raw = tile("query_raw", [P, PACK, ROWS], F32)
         nc.sync.dma_start(out=query_raw[:], in_=query.rearrange("(p j) q -> p j q", j=PACK))
@@ -93,7 +96,7 @@ def tile_attend_gatedsoftmax_pl_kernel(tc, query, keys_words, keys_scales, size,
 
         planes = [load_plane(0)]
         got_scales = tile("got_scales", [P, SLOTS], U8)
-        nc.vector.tensor_copy(got_scales[:], scale_window.indirect(offsets[:]))
+        nc.vector.tensor_copy(got_scales[:], key_scales[:].indirect(offsets[:]))
         for quad in range(4):
             nc.sync.dma_start(
                 out=slot_scales[32 * quad : 32 * quad + 4, :].bitcast(I32),
@@ -101,151 +104,159 @@ def tile_attend_gatedsoftmax_pl_kernel(tc, query, keys_words, keys_scales, size,
             )
         size_cols = tile("size_cols", [P, PACK], F32)
         nc.sync.dma_start(out=size_cols[:], in_=size[0].rearrange("(p r) -> p r", r=PACK))
-        inp_raw = tile("inp_raw", [P, PACK, ROWS], F32)
-        nc.sync.dma_start(out=inp_raw[:], in_=inp.rearrange("(p j) q -> p j q", j=PACK))
-        wg_raw = tile("wg_raw", [P, PACK, FEATURES], F32, WG_AT)
+        wg_raw = tile("wg_raw", [P, PACK, FEATURES], F32)
         nc.sync.dma_start(out=wg_raw[:], in_=wg.rearrange("(p j) e -> p j e", j=PACK))
         for t in range(1, PACK):
             planes.append(load_plane(t))
+        inp_raw = tile("inp_raw", [P, PACK, ROWS], F32, INP_AT)
+        nc.sync.dma_start(out=inp_raw[:], in_=inp.rearrange("(p j) q -> p j q", j=PACK))
 
         got_words = tile("got_words", [P, SLOTS], U16)
         nc.vector.tensor_copy(got_words[:], key_words[:].indirect(offsets[:]))
-
-        query_grouped = tile("query_grouped", [P, ROWS, PACK], BF16, SPARE_AT)
+        query_grouped = tile("query_grouped", [P, ROWS, PACK], BF16, QUERY_GROUPED_AT)
         interleave(nc.scalar.copy, query_grouped[:], query_raw[:])
         q_mx = quantize("query", query_grouped[:].rearrange("p c j -> p (c j)"), ROWS)
+        scores = []
+        for h in range(2):
+            scores.append(bank(h, "scores", [P, SLOTS]))
+            product(scores[h][:], q_mx, halves[h], (got_words, slot_scales), slice(0, SLOTS), FP4X4)
 
         half_size = tile("half_size", [P, PACK], F32)
         nc.gpsimd.tensor_scalar(out=half_size[:], in0=size_cols[:], scalar1=0.5, scalar2=0.0, op0=ALU.mult, op1=ALU.add)
-        size_bank = ps.tile([P, PACK, P], F32, tag="vT0")
+        size_row = bank(2, "size_row", [P, PACK, P])
         for r in range(PACK):
-            nc.tensor.transpose(size_bank[:, r, :], half_size[:, r : r + 1].to_broadcast([P, P]), ident[:])
-
-        score_banks = []
-        for h in range(2):
-            bank = ps.tile([P, SLOTS], F32, name="scores", tag="acc", bufs=2)
-            product(bank[:], q_mx, halves[h], (got_words, slot_scales), slice(0, SLOTS), FP4X4)
-            score_banks.append(bank)
+            nc.tensor.transpose(size_row[:, r, :], half_size[:, r : r + 1].to_broadcast([P, P]), ident[:])
 
         def gather_plane(t, offset=None):
             got = tile("got%d" % t, [P, SLOTS], BF16, offset)
             nc.vector.tensor_copy(got[:], planes[t][:].indirect(offsets[:]))
             return got
 
-        def turn_plane(t, got):
-            if t == 0:
-                bank = ps.tile([P, 2, P], F32, name="vT", tag="acc", bufs=2)
-            else:
-                bank = ps.tile([P, 2, P], F32, name="vT", tag="vT%d" % (t % 2))
+        def turn_plane(t, got, number, offset=None):
+            turned = bank(number, "turned", [P, 2, P])
             for u in range(2):
-                nc.tensor.transpose(bank[:, u, :], got[:].bitcast(F32)[:, u::2], ident[:])
-            return bank
-
-        def group_plane(t, bank, offset=None):
+                nc.tensor.transpose(turned[:, u, :], got[:].bitcast(F32)[:, u::2], ident[:])
             grouped = tile("v_grouped%d" % t, [P, P * PACK], BF16, offset)
             nc.scalar.copy(
                 out=grouped[:].bitcast(F32).rearrange("p (m u) -> p m u", u=2),
-                in_=bank[:].rearrange("p u m -> p m u"),
+                in_=turned[:].rearrange("p u m -> p m u"),
             )
             return grouped
 
-        neg_max = []
+        got0 = gather_plane(0, QUERY_GROUPED_AT)
+        neg_max, probs, sums = [], [], []
         for h in range(2):
-            nm = tile("neg_max%d" % h, [P, 1], F32)
-            nc.vector.tensor_reduce(out=nm[:], in_=score_banks[h][:], axis=mybir.AxisListType.X, op=ALU.max, negate=True)
-            neg_max.append(nm)
-        got0 = gather_plane(0, SPARE_AT)
-        inp_grouped = tile("inp_grouped", [P, ROWS, PACK], BF16)
-        interleave(nc.vector.tensor_copy, inp_grouped[:], inp_raw[:])
-        probs = []
-        sums = tile("sums", [P, 2], F32)
+            neg_max.append(tile("neg_max%d" % h, [P, 1], F32))
+            nc.vector.tensor_reduce(out=neg_max[h][:], in_=scores[h][:], axis=mybir.AxisListType.X, op=ALU.max, negate=True)
         for h in range(2):
-            pr = tile("probs%d" % h, [P, SLOTS], F32, SPARE_AT + (2 + 2 * h) * KB)
+            probs.append(tile("probs%d" % h, [P, SLOTS], F32))
+            sums.append(tile("sum%d" % h, [P, 1], F32))
             nc.scalar.activation(
-                out=pr[:], in_=score_banks[h][:], func=ACT.Exp, bias=neg_max[h][:], scale=1.0, accum_out=sums[:, h : h + 1]
+                out=probs[h][:], in_=scores[h][:], func=ACT.Exp, bias=neg_max[h][:], scale=1.0, accum_out=sums[h][:]
             )
-            probs.append(pr)
-        v_grouped0 = group_plane(0, turn_plane(0, got0))
-        inv = tile("inv", [P, 2], F32)
-        nc.vector.reciprocal(out=inv[:], in_=sums[:])
-        w_bank = ps.tile([P, 2, 2, P], F32, tag="w")
+        v_grouped0 = turn_plane(0, got0, 0)
+        w_turned = bank(3, "w_turned", [P, 2, 2, P])
         for h in range(2):
+            inv = tile("inv%d" % h, [P, 1], F32)
+            nc.vector.reciprocal(out=inv[:], in_=sums[h][:])
             w = tile("weights%d" % h, [P, SLOTS], BF16)
             nc.vector.scalar_tensor_tensor(
                 out=w[:].rearrange("p (s r) -> p s r", r=PACK),
                 in0=probs[h][:].rearrange("p (s r) -> p s r", r=PACK),
-                scalar=inv[:, h : h + 1],
-                in1=size_bank[:].rearrange("p r s -> p s r"),
+                scalar=inv[:],
+                in1=size_row[:].rearrange("p r s -> p s r"),
                 op0=ALU.mult,
                 op1=ALU.mult,
             )
             for u in range(2):
-                nc.tensor.transpose(w_bank[:, h, u, :], w[:].bitcast(F32)[:, u::2], ident[:])
+                nc.tensor.transpose(w_turned[:, h, u, :], w[:].bitcast(F32)[:, u::2], ident[:])
+        v_mx0 = quantize("v0", v_grouped0[:], P)
 
-        inp_mx = quantize("inp", inp_grouped[:].rearrange("p c j -> p (c j)"), ROWS, SPARE_AT + 4 * KB)
-        v_mx0 = quantize("v0", v_grouped0[:], P, SPARE_AT + 5 * KB)
-
-        def group_gate_weights(b, offset):
-            grouped = tile("wg_grouped%d" % b, [P, 2, P, PACK], BF16, offset)
+        def group_gate_weights(b):
+            grouped = tile("wg_grouped%d" % b, [P, 2, P, PACK], BF16)
             nc.scalar.copy(
                 out=grouped[:].rearrange("p t m j -> p m j t"),
                 in_=wg_raw[:].rearrange("p j (m t) -> p m j t", t=PACK)[:, :, :, 2 * b : 2 * b + 2],
             )
             return grouped[:].rearrange("p t m j -> p (t m j)")
 
-        g_mx0 = quantize("wg0", group_gate_weights(0, SPARE_AT + 7 * KB), 2 * P)
-        w_grouped = tile("w_grouped", [P, ROWS * PACK], BF16, SPARE_AT + 6 * KB)
+        wg_grouped0 = group_gate_weights(0)
+        w_grouped = tile("w_grouped", [P, ROWS * PACK], BF16)
         nc.scalar.copy(
             out=w_grouped[:].bitcast(F32).rearrange("p (h q u) -> p h q u", h=2, u=2),
-            in_=w_bank[:].rearrange("p h u q -> p h q u"),
+            in_=w_turned[:].rearrange("p h u q -> p h q u"),
         )
-        wg_grouped1 = group_gate_weights(1, SPARE_AT + 8 * KB)
-        v_grouped1 = group_plane(1, turn_plane(1, gather_plane(1)))
-        w_mx = quantize("w", w_grouped[:], ROWS, PLANE_BYTES)
+        wg_grouped1 = group_gate_weights(1)
 
-        gate = tile("gate", [P, PACK, ROWS], F32)
+        v_grouped1 = turn_plane(1, gather_plane(1), 4)
+        g_mx = [quantize("wg0", wg_grouped0, 2 * P, PLANE_BYTES)]
+        v_grouped2 = turn_plane(2, gather_plane(2), 2)
+        w_mx = quantize("w", w_grouped[:], ROWS, 2 * PLANE_BYTES + 2 * KB)
+        o01 = bank(1, "o01", [P, 2, ROWS])
+        outs = [o01[:, 0, :], o01[:, 1, :]]
+        product(outs[0], v_mx0, everything, w_mx, all_rows)
+        g_mx.append(quantize("wg1", wg_grouped1, 2 * P, 2 * PLANE_BYTES))
+        product(outs[1], quantize("v1", v_grouped1[:], P, 2 * PLANE_BYTES + KB), everything, w_mx, all_rows)
+        got3 = gather_plane(3)
 
-        def gate_pair(b, g_mx):
-            z_bank = ps.tile([P, 2, ROWS], F32, name="z", tag="z", bufs=2)
-            for s in range(2):
-                product(z_bank[:, s, :], g_mx, halves[s], inp_mx, all_rows)
-            nc.scalar.activation(out=gate[:, 2 * b : 2 * b + 2, :], in_=z_bank[:], func=ACT.Tanh, scale=0.5)
+        inp_mx = (tile("inp_codes", [P, ROWS], U32), tile("inp_scales", [P, ROWS], U8))
+        inp_grouped = []
+        for h, copy in enumerate((nc.scalar.copy, nc.vector.tensor_copy)):
+            inp_grouped.append(tile("inp_grouped%d" % h, [P, P, PACK], BF16, INP_GROUPED_AT + h * KB))
+            interleave(copy, inp_grouped[h][:], inp_raw[:, :, halves[h]])
+        v_grouped3 = turn_plane(3, got3, 4, INP_AT)
+        for h in range(2):
+            nc.vector.quantize_mx(
+                out=inp_mx[0][:, halves[h]].bitcast(FP8X4),
+                scales=inp_mx[1][:, halves[h]],
+                in_=inp_grouped[h][:].rearrange("p c j -> p (c j)"),
+            )
+        v_mx2 = quantize("v2", v_grouped2[:], P, INP_GROUPED_AT + KB)
+        v_mx3 = quantize("v3", v_grouped3[:], P, INP_GROUPED_AT + KB + KB // 2)
+        gates = [tile("gate%d" % t, [P, ROWS], F32) for t in range(PACK)]
 
-        gate_pair(0, g_mx0)
-        o_01 = ps.tile([P, 2, ROWS], F32, tag="acc", bufs=2)
-        product(o_01[:, 0, :], v_mx0, everything, w_mx, all_rows)
-        v_grouped2 = group_plane(2, turn_plane(2, gather_plane(2)))
-        gate_pair(1, quantize("wg1", wg_grouped1, 2 * P, 2 * PLANE_BYTES + KB))
-        product(o_01[:, 1, :], quantize("v1", v_grouped1[:], P, 2 * PLANE_BYTES), everything, w_mx, all_rows)
-        v_grouped3 = group_plane(3, turn_plane(3, gather_plane(3)), SPARE_AT)
-        v_mx2 = quantize("v2", v_grouped2[:], P, 3 * PLANE_BYTES)
+        def gate_product(t, rows, number):
+            z = bank(number, "z", [P, rows.stop - rows.start])
+            product(z[:], g_mx[t // 2], halves[t % 2], inp_mx, rows)
+            return z
+
+        def gate(t, rows, z_view):
+            nc.scalar.activation(out=gates[t][:, rows], in_=z_view, func=ACT.Tanh, scale=0.5)
+
+        for h, number in enumerate((0, 5)):
+            gate(0, halves[h], gate_product(0, halves[h], number)[:])
+        for t, number in ((1, 3), (2, 2)):
+            gate(t, all_rows, gate_product(t, all_rows, number)[:])
+        z3 = gate_product(3, all_rows, 4)
+        for rows in halves:
+            gate(3, rows, z3[:, rows])
+        for t, v_mx in ((2, v_mx2), (3, v_mx3)):
+            outs.append(bank(4 + t, "o", [P, ROWS])[:])
+            product(outs[t], v_mx, everything, w_mx, all_rows)
 
         out_planes = out_0.rearrange("(p t) q -> p t q", t=PACK)
-        y01 = tile("y01", [P, 2, ROWS], F32, 3 * PLANE_BYTES + KB)
-        y23 = tile("y23", [P, 2, ROWS], F32, SPARE_AT)
+        y01 = tile("y01", [P, 2, ROWS], F32)
+        y23 = tile("y23", [P, 2, ROWS], F32)
 
-        def gated(out, ts, rows, o_view):
+        def gated(out, t, rows):
             nc.vector.scalar_tensor_tensor(
-                out=out, in0=gate[:, ts, rows], scalar=1.0, in1=o_view, op0=ALU.add, op1=ALU.mult
+                out=out, in0=gates[t][:, rows], scalar=1.0, in1=outs[t][:, rows], op0=ALU.add, op1=ALU.mult
             )
 
-        gated(y01[:], slice(0, 2), all_rows, o_01[:])
+        for t in range(2):
+            gated(y01[:, t, :], t, all_rows)
         nc.sync.dma_start(out=out_planes[:, 0:2, :], in_=y01[:])
-        o_2 = ps.tile([P, ROWS], F32, tag="acc", bufs=2)
-        product(o_2[:], v_mx2, everything, w_mx, all_rows)
-        v_mx3 = quantize("v3", v_grouped3[:], P)
-        gated(y23[:, 0, :], 2, all_rows, o_2[:])
+        gated(y23[:, 0, :], 2, all_rows)
         nc.sync.dma_start(out=out_planes[:, 2, :], in_=y23[:, 0, :])
-        for h, tag in enumerate(("size", "w")):
-            o_3 = ps.tile([P, P], F32, name="o_3", tag=tag)
-            product(o_3[:], v_mx3, everything, w_mx, halves[h])
-            gated(y23[:, 1, halves[h]], 3, halves[h], o_3[:])
+        for rows in halves:
+            gated(y23[:, 1, rows], 3, rows)
         nc.sync.dma_start(out=out_planes[:, 3, :], in_=y23[:, 1, :])
 
         y_grouped = tile("y_grouped", [P, ROWS, PACK], BF16)
         y_codes = tile("y_codes", [P, ROWS], U32)
         y_scales = tile("y_scales", [P, ROWS], U8)
-        interleave(nc.scalar.copy, y_grouped[:, :, 0:2], y01[:])
+        for rows in halves:
+            interleave(nc.scalar.copy, y_grouped[:, rows, 0:2], y01[:, :, rows])
         for rows in halves:
             interleave(nc.vector.tensor_copy, y_grouped[:, rows, 2:4], y23[:, :, rows])
         for rows in halves:

@@ -25,6 +25,7 @@ PLANE_BYTES = TOKENS * 4
 INP_AT = PACK * PLANE_BYTES
 INP_GROUPED_AT = INP_AT + 4 * KB
 QUERY_GROUPED_AT = INP_GROUPED_AT + 2 * KB
+PROBS_AT = QUERY_GROUPED_AT + 2 * KB
 
 FLOPS = 3 * 2 * 512 * 512 * 256
 
@@ -84,6 +85,8 @@ def tile_attend_gatedsoftmax_pl_kernel(tc, query, keys_words, keys_scales, size,
         make_identity(nc, ident[:])
         nc.sync.dma_start(offsets[:], offs)
         nc.scalar.dma_start(out=key_scales[16:32, :].bitcast(I32), in_=keys_scales[0].bitcast(I32))
+        size_cols = tile("size_cols", [P, PACK], F32)
+        nc.scalar.dma_start(out=size_cols[:], in_=size[0].rearrange("(p r) -> p r", r=PACK))
         nc.sync.dma_start(out=key_words[:].bitcast(I32), in_=keys_words[0].bitcast(I32))
         query_raw = tile("query_raw", [P, PACK, ROWS], F32)
         nc.sync.dma_start(out=query_raw[:], in_=query.rearrange("(p j) q -> p j q", j=PACK))
@@ -102,11 +105,10 @@ def tile_attend_gatedsoftmax_pl_kernel(tc, query, keys_words, keys_scales, size,
                 out=slot_scales[32 * quad : 32 * quad + 4, :].bitcast(I32),
                 in_=got_scales[16 + 4 * quad : 20 + 4 * quad, :].bitcast(I32),
             )
-        size_cols = tile("size_cols", [P, PACK], F32)
-        nc.sync.dma_start(out=size_cols[:], in_=size[0].rearrange("(p r) -> p r", r=PACK))
+        planes.append(load_plane(1))
         wg_raw = tile("wg_raw", [P, PACK, FEATURES], F32)
         nc.sync.dma_start(out=wg_raw[:], in_=wg.rearrange("(p j) e -> p j e", j=PACK))
-        for t in range(1, PACK):
+        for t in range(2, PACK):
             planes.append(load_plane(t))
         inp_raw = tile("inp_raw", [P, PACK, ROWS], F32, INP_AT)
         nc.sync.dma_start(out=inp_raw[:], in_=inp.rearrange("(p j) q -> p j q", j=PACK))
@@ -149,15 +151,17 @@ def tile_attend_gatedsoftmax_pl_kernel(tc, query, keys_words, keys_scales, size,
             neg_max.append(tile("neg_max%d" % h, [P, 1], F32))
             nc.vector.tensor_reduce(out=neg_max[h][:], in_=scores[h][:], axis=mybir.AxisListType.X, op=ALU.max, negate=True)
         for h in range(2):
-            probs.append(tile("probs%d" % h, [P, SLOTS], F32))
+            probs.append(tile("probs%d" % h, [P, SLOTS], F32, PROBS_AT + 2 * h * KB))
             sums.append(tile("sum%d" % h, [P, 1], F32))
             nc.scalar.activation(
                 out=probs[h][:], in_=scores[h][:], func=ACT.Exp, bias=neg_max[h][:], scale=1.0, accum_out=sums[h][:]
             )
+        got1 = gather_plane(1)
         v_grouped0 = turn_plane(0, got0, 0)
+        v_grouped1 = turn_plane(1, got1, 4)
         w_turned = bank(3, "w_turned", [P, 2, 2, P])
         for h in range(2):
-            inv = tile("inv%d" % h, [P, 1], F32)
+            inv = tile("inv%d" % h, [P, 1], F32, PLANE_BYTES + h * KB)
             nc.vector.reciprocal(out=inv[:], in_=sums[h][:])
             w = tile("weights%d" % h, [P, SLOTS], BF16)
             nc.vector.scalar_tensor_tensor(
@@ -170,33 +174,35 @@ def tile_attend_gatedsoftmax_pl_kernel(tc, query, keys_words, keys_scales, size,
             )
             for u in range(2):
                 nc.tensor.transpose(w_turned[:, h, u, :], w[:].bitcast(F32)[:, u::2], ident[:])
-        v_mx0 = quantize("v0", v_grouped0[:], P)
+        v_mx0 = quantize("v0", v_grouped0[:], P, PROBS_AT + 2 * KB)
+        v_mx1 = quantize("v1", v_grouped1[:], P, PROBS_AT + 3 * KB)
 
-        def group_gate_weights(b):
-            grouped = tile("wg_grouped%d" % b, [P, 2, P, PACK], BF16)
-            nc.scalar.copy(
-                out=grouped[:].rearrange("p t m j -> p m j t"),
-                in_=wg_raw[:].rearrange("p j (m t) -> p m j t", t=PACK)[:, :, :, 2 * b : 2 * b + 2],
+        wg_grouped = [tile("wg_grouped%d" % b, [P, 2, P, PACK], BF16) for b in range(2)]
+
+        def group_gate_weights(copy, b, ms):
+            copy(
+                out=wg_grouped[b][:].rearrange("p t m j -> p m j t")[:, ms],
+                in_=wg_raw[:].rearrange("p j (m t) -> p m j t", t=PACK)[:, ms, :, 2 * b : 2 * b + 2],
             )
-            return grouped[:].rearrange("p t m j -> p (t m j)")
 
-        wg_grouped0 = group_gate_weights(0)
+        group_gate_weights(nc.vector.tensor_copy, 1, slice(0, P // 2))
+        group_gate_weights(nc.scalar.copy, 0, everything)
         w_grouped = tile("w_grouped", [P, ROWS * PACK], BF16)
         nc.scalar.copy(
             out=w_grouped[:].bitcast(F32).rearrange("p (h q u) -> p h q u", h=2, u=2),
             in_=w_turned[:].rearrange("p h u q -> p h q u"),
         )
-        wg_grouped1 = group_gate_weights(1)
+        group_gate_weights(nc.scalar.copy, 1, slice(P // 2, P))
+        g_mx = [quantize("wg0", wg_grouped[0][:].rearrange("p t m j -> p (t m j)"), 2 * P)]
 
-        v_grouped1 = turn_plane(1, gather_plane(1), 4)
-        g_mx = [quantize("wg0", wg_grouped0, 2 * P, PLANE_BYTES)]
-        v_grouped2 = turn_plane(2, gather_plane(2), 2)
+        got2 = gather_plane(2)
+        v_grouped2 = turn_plane(2, got2, 2)
         w_mx = quantize("w", w_grouped[:], ROWS, 2 * PLANE_BYTES + 2 * KB)
+        g_mx.append(quantize("wg1", wg_grouped[1][:].rearrange("p t m j -> p (t m j)"), 2 * P, 2 * PLANE_BYTES))
         o01 = bank(1, "o01", [P, 2, ROWS])
         outs = [o01[:, 0, :], o01[:, 1, :]]
-        product(outs[0], v_mx0, everything, w_mx, all_rows)
-        g_mx.append(quantize("wg1", wg_grouped1, 2 * P, 2 * PLANE_BYTES))
-        product(outs[1], quantize("v1", v_grouped1[:], P, 2 * PLANE_BYTES + KB), everything, w_mx, all_rows)
+        for t, v_mx in enumerate((v_mx0, v_mx1)):
+            product(outs[t], v_mx, everything, w_mx, all_rows)
         got3 = gather_plane(3)
 
         inp_mx = (tile("inp_codes", [P, ROWS], U32), tile("inp_scales", [P, ROWS], U8))

@@ -85,11 +85,11 @@ def tile_attend_gatedsoftmax_pl_kernel(tc, query, keys_words, keys_scales, size,
         make_identity(nc, ident[:])
         nc.sync.dma_start(offsets[:], offs)
         nc.scalar.dma_start(out=key_scales[16:32, :].bitcast(I32), in_=keys_scales[0].bitcast(I32))
-        size_cols = tile("size_cols", [P, PACK], F32)
-        nc.scalar.dma_start(out=size_cols[:], in_=size[0].rearrange("(p r) -> p r", r=PACK))
         nc.sync.dma_start(out=key_words[:].bitcast(I32), in_=keys_words[0].bitcast(I32))
         query_raw = tile("query_raw", [P, PACK, ROWS], F32)
         nc.sync.dma_start(out=query_raw[:], in_=query.rearrange("(p j) q -> p j q", j=PACK))
+        size_cols = tile("size_cols", [P, PACK], F32)
+        nc.sync.dma_start(out=size_cols[:], in_=size[0].rearrange("(p r) -> p r", r=PACK))
         vals_planes = vals.rearrange("(m t) n -> t m n", t=PACK)
 
         def load_plane(t):

@@ -193,12 +193,11 @@ def tile_attend_gatedsoftmax_pl_kernel(tc, query, keys_words, keys_scales, size,
             in_=w_turned[:].rearrange("p h u q -> p h q u"),
         )
         group_gate_weights(nc.scalar.copy, 1, slice(P // 2, P))
-        g_mx = [quantize("wg0", wg_grouped[0][:].rearrange("p t m j -> p (t m j)"), 2 * P)]
 
         got2 = gather_plane(2)
         v_grouped2 = turn_plane(2, got2, 2)
         w_mx = quantize("w", w_grouped[:], ROWS, 2 * PLANE_BYTES + 2 * KB)
-        g_mx.append(quantize("wg1", wg_grouped[1][:].rearrange("p t m j -> p (t m j)"), 2 * P, 2 * PLANE_BYTES))
+        g_mx = [quantize("wg0", wg_grouped[0][:].rearrange("p t m j -> p (t m j)"), 2 * P, 2 * PLANE_BYTES)]
         o01 = bank(1, "o01", [P, 2, ROWS])
         outs = [o01[:, 0, :], o01[:, 1, :]]
         for t, v_mx in enumerate((v_mx0, v_mx1)):
@@ -217,8 +216,11 @@ def tile_attend_gatedsoftmax_pl_kernel(tc, query, keys_words, keys_scales, size,
                 scales=inp_mx[1][:, halves[h]],
                 in_=inp_grouped[h][:].rearrange("p c j -> p (c j)"),
             )
-        v_mx2 = quantize("v2", v_grouped2[:], P, INP_GROUPED_AT + KB)
-        v_mx3 = quantize("v3", v_grouped3[:], P, INP_GROUPED_AT + KB + KB // 2)
+        g_mx.append(
+            quantize("wg1", wg_grouped[1][:].rearrange("p t m j -> p (t m j)"), 2 * P, INP_GROUPED_AT + 2 * KB - 64)
+        )
+        v_mx2 = quantize("v2", v_grouped2[:], P, INP_GROUPED_AT + KB - 256)
+        v_mx3 = quantize("v3", v_grouped3[:], P, INP_GROUPED_AT + KB + 256)
         gates = [tile("gate%d" % t, [P, ROWS], F32) for t in range(PACK)]
 
         def gate_product(t, rows, number):

@@ -22,10 +22,14 @@ ROWS = 256
 FEATURES = 512
 KB = 1024
 PLANE_BYTES = TOKENS * 4
-INP_AT = PACK * PLANE_BYTES
-INP_GROUPED_AT = INP_AT + 4 * KB
-QUERY_GROUPED_AT = INP_GROUPED_AT + 2 * KB
-PROBS_AT = QUERY_GROUPED_AT + 2 * KB
+PAIR_AT = 0
+PLANE2_AT = 2 * PLANE_BYTES
+PLANE3_AT = 3 * PLANE_BYTES
+INP_AT = 4 * PLANE_BYTES
+QUERY_CODES_AT = INP_AT + 4 * KB
+GROUPED_AT = QUERY_CODES_AT + 2 * KB
+SCALE_ROWS = 16
+VECTOR_SLOTS = 256
 
 FLOPS = 3 * 2 * 512 * 512 * 256
 
@@ -75,69 +79,102 @@ def tile_attend_gatedsoftmax_pl_kernel(tc, query, keys_words, keys_scales, size,
 
         key_words = tile("key_words", [P, TOKENS], U16)
         key_scales = tile("key_scales", [P, TOKENS], U8)
+        first_scale_row = P - SCALE_ROWS
         offsets = sb.tile([P, SLOTS // 16], U16)
-        nc.gpsimd.memset(key_scales[0:16, :].bitcast(I32), 0)
-        nc.vector.memset(key_scales[32:64, :].bitcast(I32), 0)
-        nc.vector.memset(key_scales[64:P, :].bitcast(I32), 0)
+        nc.vector.memset(key_scales[0:first_scale_row, :].bitcast(I32), 0)
+        size_rows = tile("size_rows", [P, P], F32, QUERY_CODES_AT + KB // 2)
+        nc.vector.memset(size_rows[0 : P - PACK, :], 0.0)
         slot_scales = tile("slot_scales", [P, SLOTS], U8)
         nc.gpsimd.memset(slot_scales[:].bitcast(I32), 0)
         ident = tile("ident", [P, P], F32)
         make_identity(nc, ident[:])
         nc.sync.dma_start(offsets[:], offs)
-        nc.scalar.dma_start(out=key_scales[16:32, :].bitcast(I32), in_=keys_scales[0].bitcast(I32))
+        nc.scalar.dma_start(out=key_scales[first_scale_row:P, :].bitcast(I32), in_=keys_scales[0].bitcast(I32))
+        nc.scalar.dma_start(out=size_rows[P - PACK : P, :], in_=size[0].rearrange("(r s) -> r s", r=PACK))
         nc.sync.dma_start(out=key_words[:].bitcast(I32), in_=keys_words[0].bitcast(I32))
         query_raw = tile("query_raw", [P, PACK, ROWS], F32)
         nc.sync.dma_start(out=query_raw[:], in_=query.rearrange("(p j) q -> p j q", j=PACK))
-        size_cols = tile("size_cols", [P, PACK], F32)
-        nc.sync.dma_start(out=size_cols[:], in_=size[0].rearrange("(p r) -> p r", r=PACK))
-        vals_planes = vals.rearrange("(m t) n -> t m n", t=PACK)
-
-        def load_plane(t):
-            plane = tile("vals%d" % t, [P, TOKENS], F32, t * PLANE_BYTES)
-            nc.sync.dma_start(out=plane[:], in_=vals_planes[t])
-            return plane
-
-        planes = [load_plane(0)]
+        wg_raw = tile("wg_raw", [P, PACK, FEATURES], F32)
+        nc.sync.dma_start(out=wg_raw[:], in_=wg.rearrange("(p j) e -> p j e", j=PACK))
         got_scales = tile("got_scales", [P, SLOTS], U8)
         nc.vector.tensor_copy(got_scales[:], key_scales[:].indirect(offsets[:]))
         for quad in range(4):
+            rows_at = first_scale_row + 4 * quad
             nc.sync.dma_start(
                 out=slot_scales[32 * quad : 32 * quad + 4, :].bitcast(I32),
-                in_=got_scales[16 + 4 * quad : 20 + 4 * quad, :].bitcast(I32),
+                in_=got_scales[rows_at : rows_at + 4, :].bitcast(I32),
             )
-        planes.append(load_plane(1))
-        wg_raw = tile("wg_raw", [P, PACK, FEATURES], F32)
-        nc.sync.dma_start(out=wg_raw[:], in_=wg.rearrange("(p j) e -> p j e", j=PACK))
-        for t in range(2, PACK):
-            planes.append(load_plane(t))
+        vals_rows = vals.rearrange("(m t) n -> m (t n)", t=PACK)
+        pair = tile("vals01", [P, 2 * TOKENS], F32, PAIR_AT)
+        nc.sync.dma_start(out=pair[:], in_=vals_rows[:, 0 : 2 * TOKENS])
+        plane2 = tile("vals2", [P, TOKENS], F32, PLANE2_AT)
+        nc.sync.dma_start(out=plane2[:], in_=vals_rows[:, 2 * TOKENS : 3 * TOKENS])
+        plane3 = tile("vals3", [P, TOKENS], F32, PLANE3_AT)
+        nc.sync.dma_start(out=plane3[:], in_=vals_rows[:, 3 * TOKENS : 4 * TOKENS])
         inp_raw = tile("inp_raw", [P, PACK, ROWS], F32, INP_AT)
         nc.sync.dma_start(out=inp_raw[:], in_=inp.rearrange("(p j) q -> p j q", j=PACK))
 
+        size_turned = bank(4, "size_turned", [P, P])
+        nc.tensor.transpose(size_turned[:], size_rows[:], ident[:])
+        half_size = tile("half_size", [P, PACK], F32)
+        nc.vector.tensor_scalar(
+            out=half_size[:], in0=size_turned[:, P - PACK : P], scalar1=0.5, scalar2=0.0, op0=ALU.mult, op1=ALU.add
+        )
+        size_row = bank(2, "size_row", [P, SLOTS])
+        for r in range(PACK):
+            nc.tensor.transpose(size_row[:, r * P : (r + 1) * P], half_size[:, r : r + 1].to_broadcast([P, P]), ident[:])
+
         got_words = tile("got_words", [P, SLOTS], U16)
         nc.vector.tensor_copy(got_words[:], key_words[:].indirect(offsets[:]))
-        query_grouped = tile("query_grouped", [P, ROWS, PACK], BF16, QUERY_GROUPED_AT)
+        query_grouped = tile("query_grouped", [P, ROWS, PACK], BF16, GROUPED_AT)
         interleave(nc.scalar.copy, query_grouped[:], query_raw[:])
-        q_mx = quantize("query", query_grouped[:].rearrange("p c j -> p (c j)"), ROWS)
+        q_mx = quantize("query", query_grouped[:].rearrange("p c j -> p (c j)"), ROWS, QUERY_CODES_AT + KB // 2)
         scores = []
         for h in range(2):
             scores.append(bank(h, "scores", [P, SLOTS]))
             product(scores[h][:], q_mx, halves[h], (got_words, slot_scales), slice(0, SLOTS), FP4X4)
 
-        half_size = tile("half_size", [P, PACK], F32)
-        nc.gpsimd.tensor_scalar(out=half_size[:], in0=size_cols[:], scalar1=0.5, scalar2=0.0, op0=ALU.mult, op1=ALU.add)
-        size_row = bank(2, "size_row", [P, PACK, P])
-        for r in range(PACK):
-            nc.tensor.transpose(size_row[:, r, :], half_size[:, r : r + 1].to_broadcast([P, P]), ident[:])
+        wg_grouped = tile("wg_grouped", [P, PACK, P, PACK], BF16, GROUPED_AT)
+        for copy, ms in ((nc.vector.tensor_copy, slice(0, P // 2)), (nc.scalar.copy, slice(P // 2, P))):
+            copy(
+                out=wg_grouped[:].rearrange("p t m j -> p m j t")[:, ms],
+                in_=wg_raw[:].rearrange("p j (m t) -> p m j t", t=PACK)[:, ms],
+            )
 
-        def gather_plane(t, offset=None):
-            got = tile("got%d" % t, [P, SLOTS], BF16, offset)
-            nc.vector.tensor_copy(got[:], planes[t][:].indirect(offsets[:]))
-            return got
+        neg_max, probs, sums = [], [], []
+        for h in range(2):
+            neg_max.append(tile("neg_max%d" % h, [P, 1], F32))
+            nc.vector.tensor_reduce(out=neg_max[h][:], in_=scores[h][:], axis=mybir.AxisListType.X, op=ALU.max, negate=True)
+        for h in range(2):
+            probs.append(tile("probs%d" % h, [P, SLOTS], F32))
+            sums.append(tile("sum%d" % h, [P, 1], F32))
+            nc.scalar.activation(
+                out=probs[h][:], in_=scores[h][:], func=ACT.Exp, bias=neg_max[h][:], scale=1.0, accum_out=sums[h][:]
+            )
+        w_turned = bank(3, "w_turned", [P, 2, 2, P])
+        g_mx = []
+        for h in range(2):
+            inv = tile("inv%d" % h, [P, 1], F32)
+            nc.vector.reciprocal(out=inv[:], in_=sums[h][:])
+            pair_of_planes = wg_grouped[:, 2 * h : 2 * h + 2].rearrange("p t m j -> p (t m j)")
+            g_mx.append(quantize("wg%d" % h, pair_of_planes, 2 * P, QUERY_CODES_AT + h * KB))
+            w = tile("weights%d" % h, [P, SLOTS], BF16)
+            nc.vector.scalar_tensor_tensor(
+                out=w[:], in0=probs[h][:], scalar=inv[:], in1=size_row[:], op0=ALU.mult, op1=ALU.mult
+            )
+            for u in range(2):
+                nc.tensor.transpose(w_turned[:, h, u, :], w[:].bitcast(F32)[:, u::2], ident[:])
 
-        def turn_plane(t, got, number, offset=None):
+        def sorted_words(got):
+            return got[:].rearrange("p (u m e) -> p m u e", u=2, e=2)
+
+        def turn(number, words_of):
             turned = bank(number, "turned", [P, 2, P])
             for u in range(2):
-                nc.tensor.transpose(turned[:, u, :], got[:].bitcast(F32)[:, u::2], ident[:])
+                nc.tensor.transpose(turned[:, u, :], words_of(u), ident[:])
+            return turned
+
+        def group_values(t, turned, offset=None):
             grouped = tile("v_grouped%d" % t, [P, P * PACK], BF16, offset)
             nc.scalar.copy(
                 out=grouped[:].bitcast(F32).rearrange("p (m u) -> p m u", u=2),
@@ -145,133 +182,88 @@ def tile_attend_gatedsoftmax_pl_kernel(tc, query, keys_words, keys_scales, size,
             )
             return grouped
 
-        got0 = gather_plane(0, QUERY_GROUPED_AT)
-        neg_max, probs, sums = [], [], []
-        for h in range(2):
-            neg_max.append(tile("neg_max%d" % h, [P, 1], F32))
-            nc.vector.tensor_reduce(out=neg_max[h][:], in_=scores[h][:], axis=mybir.AxisListType.X, op=ALU.max, negate=True)
-        for h in range(2):
-            probs.append(tile("probs%d" % h, [P, SLOTS], F32, PROBS_AT + 2 * h * KB))
-            sums.append(tile("sum%d" % h, [P, 1], F32))
-            nc.scalar.activation(
-                out=probs[h][:], in_=scores[h][:], func=ACT.Exp, bias=neg_max[h][:], scale=1.0, accum_out=sums[h][:]
-            )
-        got1 = gather_plane(1)
-        v_grouped0 = turn_plane(0, got0, 0)
-        v_grouped1 = turn_plane(1, got1, 4)
-        w_turned = bank(3, "w_turned", [P, 2, 2, P])
-        for h in range(2):
-            inv = tile("inv%d" % h, [P, 1], F32, PLANE_BYTES + h * KB)
-            nc.vector.reciprocal(out=inv[:], in_=sums[h][:])
-            w = tile("weights%d" % h, [P, SLOTS], BF16)
-            nc.vector.scalar_tensor_tensor(
-                out=w[:].rearrange("p (s r) -> p s r", r=PACK),
-                in0=probs[h][:].rearrange("p (s r) -> p s r", r=PACK),
-                scalar=inv[:],
-                in1=size_row[:].rearrange("p r s -> p s r"),
-                op0=ALU.mult,
-                op1=ALU.mult,
-            )
-            for u in range(2):
-                nc.tensor.transpose(w_turned[:, h, u, :], w[:].bitcast(F32)[:, u::2], ident[:])
-        v_mx0 = quantize("v0", v_grouped0[:], P, PROBS_AT + 2 * KB)
-        v_mx1 = quantize("v1", v_grouped1[:], P, PROBS_AT + 3 * KB)
-
-        wg_grouped = [tile("wg_grouped%d" % b, [P, 2, P, PACK], BF16) for b in range(2)]
-
-        def group_gate_weights(copy, b, ms):
-            copy(
-                out=wg_grouped[b][:].rearrange("p t m j -> p m j t")[:, ms],
-                in_=wg_raw[:].rearrange("p j (m t) -> p m j t", t=PACK)[:, ms, :, 2 * b : 2 * b + 2],
-            )
-
-        group_gate_weights(nc.vector.tensor_copy, 1, slice(0, P // 2))
-        group_gate_weights(nc.scalar.copy, 0, everything)
-        w_grouped = tile("w_grouped", [P, ROWS * PACK], BF16)
-        nc.scalar.copy(
+        got = [tile("got%d" % t, [P, SLOTS], BF16) for t in range(PACK)]
+        nc.vector.tensor_copy(sorted_words(got[1]), pair[:, TOKENS : 2 * TOKENS].indirect(offsets[:]))
+        nc.scalar.activation(got[0][:], pair[:].indirect(offsets[:]), ACT.Copy)
+        turned1 = turn(0, lambda u: got[1][:].bitcast(F32)[:, halves[u]])
+        turned0 = turn(2, lambda u: got[0][:].bitcast(F32)[:, u::2])
+        w_grouped = tile("w_grouped", [P, ROWS * PACK], BF16, PAIR_AT)
+        nc.vector.tensor_copy(
             out=w_grouped[:].bitcast(F32).rearrange("p (h q u) -> p h q u", h=2, u=2),
             in_=w_turned[:].rearrange("p h u q -> p h q u"),
         )
-        group_gate_weights(nc.scalar.copy, 1, slice(P // 2, P))
 
-        got2 = gather_plane(2)
-        v_grouped2 = turn_plane(2, got2, 2)
-        w_mx = quantize("w", w_grouped[:], ROWS, 2 * PLANE_BYTES + 2 * KB)
-        g_mx = [quantize("wg0", wg_grouped[0][:].rearrange("p t m j -> p (t m j)"), 2 * P, 2 * PLANE_BYTES)]
+        def shared_gather(t, plane):
+            cut = VECTOR_SLOTS
+            nc.vector.tensor_copy(got[t][:, 0:cut], plane[:].indirect(offsets[:, 0 : cut // 16]))
+            nc.scalar.activation(got[t][:, cut:SLOTS], plane[:].indirect(offsets[:, cut // 16 : SLOTS // 16]), ACT.Copy)
+
+        shared_gather(2, plane2)
+        turned2 = turn(3, lambda u: got[2][:].bitcast(F32)[:, u::2])
+        w_mx = quantize("w", w_grouped[:], ROWS, PLANE2_AT)
+        v_grouped1 = group_values(1, turned1, PLANE2_AT + KB)
+        v_grouped0 = group_values(0, turned0, PLANE2_AT + 2 * KB)
+        v_grouped2 = group_values(2, turned2)
+        v_mx1 = quantize("v1", v_grouped1[:], P)
+        v_mx0 = quantize("v0", v_grouped0[:], P)
+        v_mx2 = quantize("v2", v_grouped2[:], P)
         o01 = bank(1, "o01", [P, 2, ROWS])
-        outs = [o01[:, 0, :], o01[:, 1, :]]
-        for t, v_mx in enumerate((v_mx0, v_mx1)):
-            product(outs[t], v_mx, everything, w_mx, all_rows)
-        got3 = gather_plane(3)
+        product(o01[:, 1, :], v_mx1, everything, w_mx, all_rows)
+        product(o01[:, 0, :], v_mx0, everything, w_mx, all_rows)
+        o23 = [bank(5 + h, "o23", [P, 2, P]) for h in range(2)]
+        for h in range(2):
+            product(o23[h][:, 0, :], v_mx2, everything, w_mx, halves[h])
+        shared_gather(3, plane3)
+        turned3 = turn(4, lambda u: got[3][:].bitcast(F32)[:, u::2])
 
         inp_mx = (tile("inp_codes", [P, ROWS], U32), tile("inp_scales", [P, ROWS], U8))
         inp_grouped = []
-        for h, copy in enumerate((nc.scalar.copy, nc.vector.tensor_copy)):
-            inp_grouped.append(tile("inp_grouped%d" % h, [P, P, PACK], BF16, INP_GROUPED_AT + h * KB))
+        for h, copy in enumerate((nc.vector.tensor_copy, nc.scalar.copy)):
+            inp_grouped.append(tile("inp_grouped%d" % h, [P, P, PACK], BF16))
             interleave(copy, inp_grouped[h][:], inp_raw[:, :, halves[h]])
-        v_grouped3 = turn_plane(3, got3, 4, INP_AT)
+        v_grouped3 = group_values(3, turned3, INP_AT)
         for h in range(2):
             nc.vector.quantize_mx(
                 out=inp_mx[0][:, halves[h]].bitcast(FP8X4),
                 scales=inp_mx[1][:, halves[h]],
                 in_=inp_grouped[h][:].rearrange("p c j -> p (c j)"),
             )
-        g_mx.append(
-            quantize("wg1", wg_grouped[1][:].rearrange("p t m j -> p (t m j)"), 2 * P, INP_GROUPED_AT + 2 * KB - 64)
-        )
-        v_mx2 = quantize("v2", v_grouped2[:], P, INP_GROUPED_AT + KB - 256)
-        v_mx3 = quantize("v3", v_grouped3[:], P, INP_GROUPED_AT + KB + 256)
-        gates = [tile("gate%d" % t, [P, ROWS], F32) for t in range(PACK)]
-
-        def gate_product(t, rows, number):
-            z = bank(number, "z", [P, rows.stop - rows.start])
-            product(z[:], g_mx[t // 2], halves[t % 2], inp_mx, rows)
-            return z
-
-        def gate(t, rows, z_view):
-            nc.scalar.activation(out=gates[t][:, rows], in_=z_view, func=ACT.Tanh, scale=0.5)
-
-        for h, number in enumerate((0, 5)):
-            gate(0, halves[h], gate_product(0, halves[h], number)[:])
-        for t, number in ((1, 3), (2, 2)):
-            gate(t, all_rows, gate_product(t, all_rows, number)[:])
-        z3 = gate_product(3, all_rows, 4)
-        for rows in halves:
-            gate(3, rows, z3[:, rows])
-        for t, v_mx in ((2, v_mx2), (3, v_mx3)):
-            outs.append(bank(4 + t, "o", [P, ROWS])[:])
-            product(outs[t], v_mx, everything, w_mx, all_rows)
+        v_mx3 = quantize("v3", v_grouped3[:], P)
+        steps = [(b, h) for b in range(2) for h in range(2)]
+        gates = []
+        for (b, h), number in zip(steps, (0, 2, 4, 3)):
+            z = bank(number, "z", [P, 2, P])
+            for i in range(2):
+                product(z[:, i, :], g_mx[b], halves[i], inp_mx, halves[h])
+            gates.append(tile("gate%d%d" % (b, h), [P, 2, P], F32))
+            nc.scalar.activation(out=gates[-1][:], in_=z[:], func=ACT.Tanh, scale=0.5)
+        for h in range(2):
+            product(o23[h][:, 1, :], v_mx3, everything, w_mx, halves[h])
 
         out_planes = out_0.rearrange("(p t) q -> p t q", t=PACK)
-        y01 = tile("y01", [P, 2, ROWS], F32)
-        y23 = tile("y23", [P, 2, ROWS], F32)
-
-        def gated(out, t, rows):
+        y = tile("y", [P, PACK, ROWS], F32)
+        for (b, h), gate in zip(steps, gates):
+            o = o01[:, :, halves[h]] if b == 0 else o23[h][:]
             nc.vector.scalar_tensor_tensor(
-                out=out, in0=gates[t][:, rows], scalar=1.0, in1=outs[t][:, rows], op0=ALU.add, op1=ALU.mult
+                out=y[:, 2 * b : 2 * b + 2, halves[h]], in0=gate[:], scalar=1.0, in1=o, op0=ALU.add, op1=ALU.mult
             )
+            if (b, h) == (0, 1):
+                nc.sync.dma_start(out=out_planes[:, 0:2, :], in_=y[:, 0:2, :])
+        for t in (2, 3):
+            nc.sync.dma_start(out=out_planes[:, t, :], in_=y[:, t, :])
 
-        for t in range(2):
-            gated(y01[:, t, :], t, all_rows)
-        nc.sync.dma_start(out=out_planes[:, 0:2, :], in_=y01[:])
-        gated(y23[:, 0, :], 2, all_rows)
-        nc.sync.dma_start(out=out_planes[:, 2, :], in_=y23[:, 0, :])
-        for rows in halves:
-            gated(y23[:, 1, rows], 3, rows)
-        nc.sync.dma_start(out=out_planes[:, 3, :], in_=y23[:, 1, :])
-
-        y_grouped = tile("y_grouped", [P, ROWS, PACK], BF16)
+        y_grouped = [tile("y_grouped%d" % h, [P, P, PACK], BF16) for h in range(2)]
         y_codes = tile("y_codes", [P, ROWS], U32)
         y_scales = tile("y_scales", [P, ROWS], U8)
-        for rows in halves:
-            interleave(nc.scalar.copy, y_grouped[:, rows, 0:2], y01[:, :, rows])
-        for rows in halves:
-            interleave(nc.vector.tensor_copy, y_grouped[:, rows, 2:4], y23[:, :, rows])
-        for rows in halves:
+        quarter = P // 2
+        interleave(nc.scalar.copy, y_grouped[0][:, 0:quarter, :], y[:, :, 0:quarter])
+        interleave(nc.vector.tensor_copy, y_grouped[0][:, quarter:P, :], y[:, :, quarter:P])
+        interleave(nc.vector.tensor_copy, y_grouped[1][:], y[:, :, halves[1]])
+        for h in range(2):
             nc.vector.quantize_mx(
-                out=y_codes[:, rows].bitcast(FP8X4),
-                scales=y_scales[:, rows],
-                in_=y_grouped[:, rows, :].rearrange("p c j -> p (c j)"),
+                out=y_codes[:, halves[h]].bitcast(FP8X4),
+                scales=y_scales[:, halves[h]],
+                in_=y_grouped[h][:].rearrange("p c j -> p (c j)"),
             )
         nc.sync.dma_start(out=out_1[0].rearrange("p n t -> p (n t)").bitcast(I32), in_=y_codes[:].bitcast(I32))
         for r in range(4):

@@ -27,7 +27,7 @@ PLANE2_AT = 2 * PLANE_BYTES
 PLANE3_AT = 3 * PLANE_BYTES
 INP_AT = 4 * PLANE_BYTES
 QUERY_CODES_AT = INP_AT + 4 * KB
-GROUPED_AT = QUERY_CODES_AT + 2 * KB
+GROUPED_AT = QUERY_CODES_AT + 3 * KB
 SCALE_ROWS = 16
 VECTOR_SLOTS = 256
 
@@ -134,11 +134,12 @@ def tile_attend_gatedsoftmax_pl_kernel(tc, query, keys_words, keys_scales, size,
             scores.append(bank(h, "scores", [P, SLOTS]))
             product(scores[h][:], q_mx, halves[h], (got_words, slot_scales), slice(0, SLOTS), FP4X4)
 
-        wg_grouped = tile("wg_grouped", [P, PACK, P, PACK], BF16, GROUPED_AT)
-        for copy, ms in ((nc.vector.tensor_copy, slice(0, P // 2)), (nc.scalar.copy, slice(P // 2, P))):
+        wg_grouped = []
+        for b, copy in enumerate((nc.vector.tensor_copy, nc.scalar.copy)):
+            wg_grouped.append(tile("wg_grouped%d" % b, [P, 2, P, PACK], BF16, GROUPED_AT - KB + 2 * b * KB))
             copy(
-                out=wg_grouped[:].rearrange("p t m j -> p m j t")[:, ms],
-                in_=wg_raw[:].rearrange("p j (m t) -> p m j t", t=PACK)[:, ms],
+                out=wg_grouped[b][:].rearrange("p t m j -> p m j t"),
+                in_=wg_raw[:].rearrange("p j (m t) -> p m j t", t=PACK)[:, :, :, 2 * b : 2 * b + 2],
             )
 
         neg_max, probs, sums = [], [], []
@@ -156,7 +157,7 @@ def tile_attend_gatedsoftmax_pl_kernel(tc, query, keys_words, keys_scales, size,
         for h in range(2):
             inv = tile("inv%d" % h, [P, 1], F32)
             nc.vector.reciprocal(out=inv[:], in_=sums[h][:])
-            pair_of_planes = wg_grouped[:, 2 * h : 2 * h + 2].rearrange("p t m j -> p (t m j)")
+            pair_of_planes = wg_grouped[h][:].rearrange("p t m j -> p (t m j)")
             g_mx.append(quantize("wg%d" % h, pair_of_planes, 2 * P, QUERY_CODES_AT + h * KB))
             w = tile("weights%d" % h, [P, SLOTS], BF16)
             nc.vector.scalar_tensor_tensor(

@@ -27,7 +27,8 @@ PLANE2_AT = 2 * PLANE_BYTES
 PLANE3_AT = 3 * PLANE_BYTES
 INP_AT = 4 * PLANE_BYTES
 QUERY_CODES_AT = INP_AT + 4 * KB
-GROUPED_AT = QUERY_CODES_AT + 3 * KB
+FIRST_PAIR_AT = QUERY_CODES_AT + KB
+GROUPED_AT = QUERY_CODES_AT + 4 * KB
 SCALE_ROWS = 16
 VECTOR_SLOTS = 256
 
@@ -95,7 +96,8 @@ def tile_attend_gatedsoftmax_pl_kernel(tc, query, keys_words, keys_scales, size,
         query_raw = tile("query_raw", [P, PACK, ROWS], F32)
         nc.sync.dma_start(out=query_raw[:], in_=query.rearrange("(p j) q -> p j q", j=PACK))
         wg_raw = tile("wg_raw", [P, PACK, FEATURES], F32)
-        nc.sync.dma_start(out=wg_raw[:], in_=wg.rearrange("(p j) e -> p j e", j=PACK))
+        wg_rows = wg.rearrange("(p j) e -> p j e", j=PACK)
+        nc.sync.dma_start(out=wg_raw[:, 0:3, :], in_=wg_rows[:, 0:3, :])
         got_scales = tile("got_scales", [P, SLOTS], U8)
         nc.vector.tensor_copy(got_scales[:], key_scales[:].indirect(offsets[:]))
         for quad in range(4):
@@ -104,6 +106,7 @@ def tile_attend_gatedsoftmax_pl_kernel(tc, query, keys_words, keys_scales, size,
                 out=slot_scales[32 * quad : 32 * quad + 4, :].bitcast(I32),
                 in_=got_scales[rows_at : rows_at + 4, :].bitcast(I32),
             )
+        nc.sync.dma_start(out=wg_raw[:, 3, :], in_=wg_rows[:, 3, :])
         vals_rows = vals.rearrange("(m t) n -> m (t n)", t=PACK)
         pair = tile("vals01", [P, 2 * TOKENS], F32, PAIR_AT)
         nc.sync.dma_start(out=pair[:], in_=vals_rows[:, 0 : 2 * TOKENS])
@@ -127,25 +130,26 @@ def tile_attend_gatedsoftmax_pl_kernel(tc, query, keys_words, keys_scales, size,
         got_words = tile("got_words", [P, SLOTS], U16)
         nc.vector.tensor_copy(got_words[:], key_words[:].indirect(offsets[:]))
         query_grouped = tile("query_grouped", [P, ROWS, PACK], BF16, GROUPED_AT)
-        interleave(nc.scalar.copy, query_grouped[:], query_raw[:])
+        for copy, rows in zip((nc.vector.tensor_copy, nc.scalar.copy), halves):
+            interleave(copy, query_grouped[:, rows, :], query_raw[:, :, rows])
         q_mx = quantize("query", query_grouped[:].rearrange("p c j -> p (c j)"), ROWS, QUERY_CODES_AT + KB // 2)
         scores = []
         for h in range(2):
             scores.append(bank(h, "scores", [P, SLOTS]))
             product(scores[h][:], q_mx, halves[h], (got_words, slot_scales), slice(0, SLOTS), FP4X4)
 
+        neg_max, probs, sums = [], [], []
+        for h in range(2):
+            neg_max.append(tile("neg_max%d" % h, [P, 1], F32))
+            nc.vector.tensor_reduce(out=neg_max[h][:], in_=scores[h][:], axis=mybir.AxisListType.X, op=ALU.max, negate=True)
         wg_grouped = []
         for b, copy in enumerate((nc.vector.tensor_copy, nc.scalar.copy)):
-            wg_grouped.append(tile("wg_grouped%d" % b, [P, 2, P, PACK], BF16, GROUPED_AT - KB + 2 * b * KB))
+            wg_grouped.append(tile("wg_grouped%d" % b, [P, 2, P, PACK], BF16, (FIRST_PAIR_AT, GROUPED_AT)[b]))
             copy(
                 out=wg_grouped[b][:].rearrange("p t m j -> p m j t"),
                 in_=wg_raw[:].rearrange("p j (m t) -> p m j t", t=PACK)[:, :, :, 2 * b : 2 * b + 2],
             )
 
-        neg_max, probs, sums = [], [], []
-        for h in range(2):
-            neg_max.append(tile("neg_max%d" % h, [P, 1], F32))
-            nc.vector.tensor_reduce(out=neg_max[h][:], in_=scores[h][:], axis=mybir.AxisListType.X, op=ALU.max, negate=True)
         for h in range(2):
             probs.append(tile("probs%d" % h, [P, SLOTS], F32))
             sums.append(tile("sum%d" % h, [P, 1], F32))
@@ -158,7 +162,7 @@ def tile_attend_gatedsoftmax_pl_kernel(tc, query, keys_words, keys_scales, size,
             inv = tile("inv%d" % h, [P, 1], F32)
             nc.vector.reciprocal(out=inv[:], in_=sums[h][:])
             pair_of_planes = wg_grouped[h][:].rearrange("p t m j -> p (t m j)")
-            g_mx.append(quantize("wg%d" % h, pair_of_planes, 2 * P, QUERY_CODES_AT + h * KB))
+            g_mx.append(quantize("wg%d" % h, pair_of_planes, 2 * P, QUERY_CODES_AT if h == 1 else None))
             w = tile("weights%d" % h, [P, SLOTS], BF16)
             nc.vector.scalar_tensor_tensor(
                 out=w[:], in0=probs[h][:], scalar=inv[:], in1=size_row[:], op0=ALU.mult, op1=ALU.mult
@@ -219,9 +223,12 @@ def tile_attend_gatedsoftmax_pl_kernel(tc, query, keys_words, keys_scales, size,
 
         inp_mx = (tile("inp_codes", [P, ROWS], U32), tile("inp_scales", [P, ROWS], U8))
         inp_grouped = []
-        for h, copy in enumerate((nc.vector.tensor_copy, nc.scalar.copy)):
+        for h in range(2):
             inp_grouped.append(tile("inp_grouped%d" % h, [P, P, PACK], BF16))
-            interleave(copy, inp_grouped[h][:], inp_raw[:, :, halves[h]])
+        quarter = P // 2
+        interleave(nc.vector.tensor_copy, inp_grouped[0][:], inp_raw[:, :, halves[0]])
+        interleave(nc.vector.tensor_copy, inp_grouped[1][:, 0:quarter, :], inp_raw[:, :, P : P + quarter])
+        interleave(nc.scalar.copy, inp_grouped[1][:, quarter:P, :], inp_raw[:, :, P + quarter : ROWS])
         v_grouped3 = group_values(3, turned3, INP_AT)
         for h in range(2):
             nc.vector.quantize_mx(
@@ -242,29 +249,28 @@ def tile_attend_gatedsoftmax_pl_kernel(tc, query, keys_words, keys_scales, size,
             product(o23[h][:, 1, :], v_mx3, everything, w_mx, halves[h])
 
         out_planes = out_0.rearrange("(p t) q -> p t q", t=PACK)
-        y = tile("y", [P, PACK, ROWS], F32)
+        y = [tile("y%d" % b, [P, 2, ROWS], F32) for b in range(2)]
         for (b, h), gate in zip(steps, gates):
             o = o01[:, :, halves[h]] if b == 0 else o23[h][:]
             nc.vector.scalar_tensor_tensor(
-                out=y[:, 2 * b : 2 * b + 2, halves[h]], in0=gate[:], scalar=1.0, in1=o, op0=ALU.add, op1=ALU.mult
+                out=y[b][:, :, halves[h]], in0=gate[:], scalar=1.0, in1=o, op0=ALU.add, op1=ALU.mult
             )
             if (b, h) == (0, 1):
-                nc.sync.dma_start(out=out_planes[:, 0:2, :], in_=y[:, 0:2, :])
+                nc.sync.dma_start(out=out_planes[:, 0:2, :], in_=y[0][:])
         for t in (2, 3):
-            nc.sync.dma_start(out=out_planes[:, t, :], in_=y[:, t, :])
+            nc.sync.dma_start(out=out_planes[:, t, :], in_=y[1][:, t - 2, :])
 
-        y_grouped = [tile("y_grouped%d" % h, [P, P, PACK], BF16) for h in range(2)]
+        y_grouped = tile("y_grouped", [P, ROWS, PACK], BF16)
         y_codes = tile("y_codes", [P, ROWS], U32)
         y_scales = tile("y_scales", [P, ROWS], U8)
-        quarter = P // 2
-        interleave(nc.scalar.copy, y_grouped[0][:, 0:quarter, :], y[:, :, 0:quarter])
-        interleave(nc.vector.tensor_copy, y_grouped[0][:, quarter:P, :], y[:, :, quarter:P])
-        interleave(nc.vector.tensor_copy, y_grouped[1][:], y[:, :, halves[1]])
-        for h in range(2):
+        for b, copy in enumerate((nc.scalar.copy, nc.vector.tensor_copy)):
+            for rows in halves:
+                interleave(copy, y_grouped[:, rows, 2 * b : 2 * b + 2], y[b][:, :, rows])
+        for rows in halves:
             nc.vector.quantize_mx(
-                out=y_codes[:, halves[h]].bitcast(FP8X4),
-                scales=y_scales[:, halves[h]],
-                in_=y_grouped[h][:].rearrange("p c j -> p (c j)"),
+                out=y_codes[:, rows].bitcast(FP8X4),
+                scales=y_scales[:, rows],
+                in_=y_grouped[:, rows, :].rearrange("p c j -> p (c j)"),
             )
         nc.sync.dma_start(out=out_1[0].rearrange("p n t -> p (n t)").bitcast(I32), in_=y_codes[:].bitcast(I32))
         for r in range(4):

@@ -27,7 +27,6 @@ PLANE2_AT = 2 * PLANE_BYTES
 PLANE3_AT = 3 * PLANE_BYTES
 INP_AT = 4 * PLANE_BYTES
 QUERY_CODES_AT = INP_AT + 4 * KB
-FIRST_PAIR_AT = QUERY_CODES_AT + KB
 GROUPED_AT = QUERY_CODES_AT + 4 * KB
 SCALE_ROWS = 16
 VECTOR_SLOTS = 256
@@ -96,8 +95,7 @@ def tile_attend_gatedsoftmax_pl_kernel(tc, query, keys_words, keys_scales, size,
         query_raw = tile("query_raw", [P, PACK, ROWS], F32)
         nc.sync.dma_start(out=query_raw[:], in_=query.rearrange("(p j) q -> p j q", j=PACK))
         wg_raw = tile("wg_raw", [P, PACK, FEATURES], F32)
-        wg_rows = wg.rearrange("(p j) e -> p j e", j=PACK)
-        nc.sync.dma_start(out=wg_raw[:, 0:3, :], in_=wg_rows[:, 0:3, :])
+        nc.sync.dma_start(out=wg_raw[:], in_=wg.rearrange("(p j) e -> p j e", j=PACK))
         got_scales = tile("got_scales", [P, SLOTS], U8)
         nc.vector.tensor_copy(got_scales[:], key_scales[:].indirect(offsets[:]))
         for quad in range(4):
@@ -106,7 +104,6 @@ def tile_attend_gatedsoftmax_pl_kernel(tc, query, keys_words, keys_scales, size,
                 out=slot_scales[32 * quad : 32 * quad + 4, :].bitcast(I32),
                 in_=got_scales[rows_at : rows_at + 4, :].bitcast(I32),
             )
-        nc.sync.dma_start(out=wg_raw[:, 3, :], in_=wg_rows[:, 3, :])
         vals_rows = vals.rearrange("(m t) n -> m (t n)", t=PACK)
         pair = tile("vals01", [P, 2 * TOKENS], F32, PAIR_AT)
         nc.sync.dma_start(out=pair[:], in_=vals_rows[:, 0 : 2 * TOKENS])
@@ -138,18 +135,24 @@ def tile_attend_gatedsoftmax_pl_kernel(tc, query, keys_words, keys_scales, size,
             scores.append(bank(h, "scores", [P, SLOTS]))
             product(scores[h][:], q_mx, halves[h], (got_words, slot_scales), slice(0, SLOTS), FP4X4)
 
-        neg_max, probs, sums = [], [], []
-        for h in range(2):
-            neg_max.append(tile("neg_max%d" % h, [P, 1], F32))
-            nc.vector.tensor_reduce(out=neg_max[h][:], in_=scores[h][:], axis=mybir.AxisListType.X, op=ALU.max, negate=True)
         wg_grouped = []
         for b, copy in enumerate((nc.vector.tensor_copy, nc.scalar.copy)):
-            wg_grouped.append(tile("wg_grouped%d" % b, [P, 2, P, PACK], BF16, (FIRST_PAIR_AT, GROUPED_AT)[b]))
+            wg_grouped.append(tile("wg_grouped%d" % b, [P, 2, P, PACK], BF16, GROUPED_AT - KB + 2 * b * KB))
             copy(
                 out=wg_grouped[b][:].rearrange("p t m j -> p m j t"),
                 in_=wg_raw[:].rearrange("p j (m t) -> p m j t", t=PACK)[:, :, :, 2 * b : 2 * b + 2],
             )
 
+        def quantize_pair(b, offset=None):
+            return quantize("wg%d" % b, wg_grouped[b][:].rearrange("p t m j -> p (t m j)"), 2 * P, offset)
+
+        g_mx = [quantize_pair(0)]
+
+        neg_max, probs, sums = [], [], []
+        for h in range(2):
+            neg_max.append(tile("neg_max%d" % h, [P, 1], F32))
+            nc.vector.tensor_reduce(out=neg_max[h][:], in_=scores[h][:], axis=mybir.AxisListType.X, op=ALU.max, negate=True)
+        g_mx.append(quantize_pair(1, QUERY_CODES_AT))
         for h in range(2):
             probs.append(tile("probs%d" % h, [P, SLOTS], F32))
             sums.append(tile("sum%d" % h, [P, 1], F32))
@@ -157,12 +160,9 @@ def tile_attend_gatedsoftmax_pl_kernel(tc, query, keys_words, keys_scales, size,
                 out=probs[h][:], in_=scores[h][:], func=ACT.Exp, bias=neg_max[h][:], scale=1.0, accum_out=sums[h][:]
             )
         w_turned = bank(3, "w_turned", [P, 2, 2, P])
-        g_mx = []
         for h in range(2):
             inv = tile("inv%d" % h, [P, 1], F32)
             nc.vector.reciprocal(out=inv[:], in_=sums[h][:])
-            pair_of_planes = wg_grouped[h][:].rearrange("p t m j -> p (t m j)")
-            g_mx.append(quantize("wg%d" % h, pair_of_planes, 2 * P, QUERY_CODES_AT if h == 1 else None))
             w = tile("weights%d" % h, [P, SLOTS], BF16)
             nc.vector.scalar_tensor_tensor(
                 out=w[:], in0=probs[h][:], scalar=inv[:], in1=size_row[:], op0=ALU.mult, op1=ALU.mult

@@ -215,9 +215,8 @@ def tile_attend_gatedsoftmax_pl_kernel(tc, query, keys_words, keys_scales, size,
         o01 = bank(1, "o01", [P, 2, ROWS])
         product(o01[:, 1, :], v_mx1, everything, w_mx, all_rows)
         product(o01[:, 0, :], v_mx0, everything, w_mx, all_rows)
-        o23 = [bank(5 + h, "o23", [P, 2, P]) for h in range(2)]
-        for h in range(2):
-            product(o23[h][:, 0, :], v_mx2, everything, w_mx, halves[h])
+        outs = [o01[:, 0, :], o01[:, 1, :], bank(6, "o", [P, ROWS])[:], bank(7, "o", [P, ROWS])[:]]
+        product(outs[2], v_mx2, everything, w_mx, all_rows)
         shared_gather(3, plane3)
         turned3 = turn(4, lambda u: got[3][:].bitcast(F32)[:, u::2])
 
@@ -237,28 +236,41 @@ def tile_attend_gatedsoftmax_pl_kernel(tc, query, keys_words, keys_scales, size,
                 in_=inp_grouped[h][:].rearrange("p c j -> p (c j)"),
             )
         v_mx3 = quantize("v3", v_grouped3[:], P)
-        steps = [(b, h) for b in range(2) for h in range(2)]
-        gates = []
-        for (b, h), number in zip(steps, (0, 2, 4, 3)):
-            z = bank(number, "z", [P, 2, P])
-            for i in range(2):
-                product(z[:, i, :], g_mx[b], halves[i], inp_mx, halves[h])
-            gates.append(tile("gate%d%d" % (b, h), [P, 2, P], F32))
-            nc.scalar.activation(out=gates[-1][:], in_=z[:], func=ACT.Tanh, scale=0.5)
-        for h in range(2):
-            product(o23[h][:, 1, :], v_mx3, everything, w_mx, halves[h])
+        gates = [tile("gate%d" % t, [P, ROWS], F32) for t in range(PACK)]
+
+        def gate_product(t, rows, number):
+            z = bank(number, "z", [P, rows.stop - rows.start])
+            product(z[:], g_mx[t // 2], halves[t % 2], inp_mx, rows)
+            return z
+
+        def gate(t, rows, z_view):
+            nc.scalar.activation(out=gates[t][:, rows], in_=z_view, func=ACT.Tanh, scale=0.5)
+
+        for h, number in enumerate((0, 5)):
+            gate(0, halves[h], gate_product(0, halves[h], number)[:])
+        for t, number in ((1, 2), (2, 3)):
+            gate(t, all_rows, gate_product(t, all_rows, number)[:])
+        z3 = gate_product(3, all_rows, 4)
+        for rows in halves:
+            gate(3, rows, z3[:, rows])
+        product(outs[3], v_mx3, everything, w_mx, all_rows)
 
         out_planes = out_0.rearrange("(p t) q -> p t q", t=PACK)
         y = [tile("y%d" % b, [P, 2, ROWS], F32) for b in range(2)]
-        for (b, h), gate in zip(steps, gates):
-            o = o01[:, :, halves[h]] if b == 0 else o23[h][:]
+
+        def gated(t, rows):
             nc.vector.scalar_tensor_tensor(
-                out=y[b][:, :, halves[h]], in0=gate[:], scalar=1.0, in1=o, op0=ALU.add, op1=ALU.mult
+                out=y[t // 2][:, t % 2, rows], in0=gates[t][:, rows], scalar=1.0, in1=outs[t][:, rows], op0=ALU.add, op1=ALU.mult
             )
-            if (b, h) == (0, 1):
-                nc.sync.dma_start(out=out_planes[:, 0:2, :], in_=y[0][:])
-        for t in (2, 3):
-            nc.sync.dma_start(out=out_planes[:, t, :], in_=y[1][:, t - 2, :])
+
+        for t in range(2):
+            gated(t, all_rows)
+        nc.sync.dma_start(out=out_planes[:, 0:2, :], in_=y[0][:])
+        gated(2, all_rows)
+        nc.sync.dma_start(out=out_planes[:, 2, :], in_=y[1][:, 0, :])
+        for rows in halves:
+            gated(3, rows)
+        nc.sync.dma_start(out=out_planes[:, 3, :], in_=y[1][:, 1, :])
 
         y_grouped = tile("y_grouped", [P, ROWS, PACK], BF16)
         y_codes = tile("y_codes", [P, ROWS], U32)

@@ -31,6 +31,8 @@ GROUPED_AT = QUERY_CODES_AT + 4 * KB
 SCALE_ROWS = 16
 VECTOR_SLOTS = 256
 
+SCALAR_COLUMNS = 96
+
 FLOPS = 3 * 2 * 512 * 512 * 256
 
 
@@ -50,8 +52,8 @@ def tile_attend_gatedsoftmax_pl_kernel(tc, query, keys_words, keys_scales, size,
 
         def tile(name, shape, dtype, offset=None):
             if offset is None:
-                return sb.tile(shape, dtype, name=name, align_bytes=64)
-            return placed.tile(shape, dtype, name=name, align_bytes=64, offset=offset)
+                return sb.tile(shape, dtype, name=name, align_bytes=256)
+            return placed.tile(shape, dtype, name=name, align_bytes=256, offset=offset)
 
         def bank(number, name, shape):
             return ps.tile(shape, F32, name=name, tag="bank%d" % number)
@@ -135,13 +137,17 @@ def tile_attend_gatedsoftmax_pl_kernel(tc, query, keys_words, keys_scales, size,
             scores.append(bank(h, "scores", [P, SLOTS]))
             product(scores[h][:], q_mx, halves[h], (got_words, slot_scales), slice(0, SLOTS), FP4X4)
 
-        wg_grouped = []
-        for b, copy in enumerate((nc.vector.tensor_copy, nc.scalar.copy)):
-            wg_grouped.append(tile("wg_grouped%d" % b, [P, 2, P, PACK], BF16, GROUPED_AT - KB + 2 * b * KB))
+        wg_grouped = [tile("wg_grouped%d" % b, [P, 2, P, PACK], BF16, GROUPED_AT - KB + 2 * b * KB) for b in range(2)]
+
+        def group_gate_weights(copy, b, ms):
             copy(
-                out=wg_grouped[b][:].rearrange("p t m j -> p m j t"),
-                in_=wg_raw[:].rearrange("p j (m t) -> p m j t", t=PACK)[:, :, :, 2 * b : 2 * b + 2],
+                out=wg_grouped[b][:].rearrange("p t m j -> p m j t")[:, ms],
+                in_=wg_raw[:].rearrange("p j (m t) -> p m j t", t=PACK)[:, ms, :, 2 * b : 2 * b + 2],
             )
+
+        group_gate_weights(nc.vector.tensor_copy, 0, everything)
+        group_gate_weights(nc.scalar.copy, 1, slice(0, SCALAR_COLUMNS))
+        group_gate_weights(nc.vector.tensor_copy, 1, slice(SCALAR_COLUMNS, P))
 
         def quantize_pair(b, offset=None):
             return quantize("wg%d" % b, wg_grouped[b][:].rearrange("p t m j -> p (t m j)"), 2 * P, offset)
@@ -211,14 +217,14 @@ def tile_attend_gatedsoftmax_pl_kernel(tc, query, keys_words, keys_scales, size,
         v_grouped2 = group_values(2, turned2)
         v_mx1 = quantize("v1", v_grouped1[:], P)
         v_mx0 = quantize("v0", v_grouped0[:], P)
-        v_mx2 = quantize("v2", v_grouped2[:], P)
         o01 = bank(1, "o01", [P, 2, ROWS])
         product(o01[:, 1, :], v_mx1, everything, w_mx, all_rows)
         product(o01[:, 0, :], v_mx0, everything, w_mx, all_rows)
         outs = [o01[:, 0, :], o01[:, 1, :], bank(6, "o", [P, ROWS])[:], bank(7, "o", [P, ROWS])[:]]
-        product(outs[2], v_mx2, everything, w_mx, all_rows)
         shared_gather(3, plane3)
         turned3 = turn(4, lambda u: got[3][:].bitcast(F32)[:, u::2])
+        v_mx2 = quantize("v2", v_grouped2[:], P, PLANE3_AT)
+        product(outs[2], v_mx2, everything, w_mx, all_rows)
 
         inp_mx = (tile("inp_codes", [P, ROWS], U32), tile("inp_scales", [P, ROWS], U8))
         inp_grouped = []

@@ -31,7 +31,6 @@ GROUPED_AT = QUERY_CODES_AT + 4 * KB
 SCALE_ROWS = 16
 VECTOR_SLOTS = 256
 
-SCALAR_COLUMNS = 96
 
 FLOPS = 3 * 2 * 512 * 512 * 256
 
@@ -102,7 +101,8 @@ def tile_attend_gatedsoftmax_pl_kernel(tc, query, keys_words, keys_scales, size,
         nc.vector.tensor_copy(got_scales[:], key_scales[:].indirect(offsets[:]))
         for quad in range(4):
             rows_at = first_scale_row + 4 * quad
-            nc.sync.dma_start(
+            queue = nc.sync if quad % 2 == 0 else nc.scalar
+            queue.dma_start(
                 out=slot_scales[32 * quad : 32 * quad + 4, :].bitcast(I32),
                 in_=got_scales[rows_at : rows_at + 4, :].bitcast(I32),
             )
@@ -129,15 +129,14 @@ def tile_attend_gatedsoftmax_pl_kernel(tc, query, keys_words, keys_scales, size,
         got_words = tile("got_words", [P, SLOTS], U16)
         nc.vector.tensor_copy(got_words[:], key_words[:].indirect(offsets[:]))
         query_grouped = tile("query_grouped", [P, ROWS, PACK], BF16, GROUPED_AT)
-        for copy, rows in zip((nc.vector.tensor_copy, nc.scalar.copy), halves):
-            interleave(copy, query_grouped[:, rows, :], query_raw[:, :, rows])
+        interleave(nc.vector.tensor_copy, query_grouped[:], query_raw[:])
         q_mx = quantize("query", query_grouped[:].rearrange("p c j -> p (c j)"), ROWS, QUERY_CODES_AT + KB // 2)
         scores = []
         for h in range(2):
             scores.append(bank(h, "scores", [P, SLOTS]))
             product(scores[h][:], q_mx, halves[h], (got_words, slot_scales), slice(0, SLOTS), FP4X4)
 
-        wg_grouped = [tile("wg_grouped%d" % b, [P, 2, P, PACK], BF16, GROUPED_AT - KB + 2 * b * KB) for b in range(2)]
+        wg_grouped = [tile("wg_grouped%d" % b, [P, 2, P, PACK], BF16, GROUPED_AT + 2 * b * KB) for b in range(2)]
 
         def group_gate_weights(copy, b, ms):
             copy(
@@ -146,8 +145,7 @@ def tile_attend_gatedsoftmax_pl_kernel(tc, query, keys_words, keys_scales, size,
             )
 
         group_gate_weights(nc.vector.tensor_copy, 0, everything)
-        group_gate_weights(nc.scalar.copy, 1, slice(0, SCALAR_COLUMNS))
-        group_gate_weights(nc.vector.tensor_copy, 1, slice(SCALAR_COLUMNS, P))
+        group_gate_weights(nc.scalar.copy, 1, everything)
 
         def quantize_pair(b, offset=None):
             return quantize("wg%d" % b, wg_grouped[b][:].rearrange("p t m j -> p (t m j)"), 2 * P, offset)

@@ -212,7 +212,6 @@ def tile_attend_gatedsoftmax_pl_kernel(tc, query, keys_words, keys_scales, size,
         w_mx = quantize("w", w_grouped[:], ROWS, PLANE2_AT)
         v_grouped1 = group_values(1, turned1, PLANE2_AT + KB)
         v_grouped0 = group_values(0, turned0, PLANE2_AT + 2 * KB)
-        v_grouped2 = group_values(2, turned2)
         v_mx1 = quantize("v1", v_grouped1[:], P)
         v_mx0 = quantize("v0", v_grouped0[:], P)
         o01 = bank(1, "o01", [P, 2, ROWS])
@@ -221,8 +220,7 @@ def tile_attend_gatedsoftmax_pl_kernel(tc, query, keys_words, keys_scales, size,
         outs = [o01[:, 0, :], o01[:, 1, :], bank(6, "o", [P, ROWS])[:], bank(7, "o", [P, ROWS])[:]]
         shared_gather(3, plane3)
         turned3 = turn(4, lambda u: got[3][:].bitcast(F32)[:, u::2])
-        v_mx2 = quantize("v2", v_grouped2[:], P, PLANE3_AT)
-        product(outs[2], v_mx2, everything, w_mx, all_rows)
+        v_grouped2 = group_values(2, turned2, PLANE3_AT)
 
         inp_mx = (tile("inp_codes", [P, ROWS], U32), tile("inp_scales", [P, ROWS], U8))
         inp_grouped = []
@@ -239,6 +237,7 @@ def tile_attend_gatedsoftmax_pl_kernel(tc, query, keys_words, keys_scales, size,
                 scales=inp_mx[1][:, halves[h]],
                 in_=inp_grouped[h][:].rearrange("p c j -> p (c j)"),
             )
+        v_mx2 = quantize("v2", v_grouped2[:], P, INP_AT + KB)
         v_mx3 = quantize("v3", v_grouped3[:], P)
         gates = [tile("gate%d" % t, [P, ROWS], F32) for t in range(PACK)]
 
@@ -257,6 +256,7 @@ def tile_attend_gatedsoftmax_pl_kernel(tc, query, keys_words, keys_scales, size,
         z3 = gate_product(3, all_rows, 4)
         for rows in halves:
             gate(3, rows, z3[:, rows])
+        product(outs[2], v_mx2, everything, w_mx, all_rows)
         product(outs[3], v_mx3, everything, w_mx, all_rows)
 
         out_planes = out_0.rearrange("(p t) q -> p t q", t=PACK)

@@ -212,15 +212,17 @@ def tile_attend_gatedsoftmax_pl_kernel(tc, query, keys_words, keys_scales, size,
         w_mx = quantize("w", w_grouped[:], ROWS, PLANE2_AT)
         v_grouped1 = group_values(1, turned1, PLANE2_AT + KB)
         v_grouped0 = group_values(0, turned0, PLANE2_AT + 2 * KB)
+        v_grouped2 = group_values(2, turned2)
         v_mx1 = quantize("v1", v_grouped1[:], P)
         v_mx0 = quantize("v0", v_grouped0[:], P)
         o01 = bank(1, "o01", [P, 2, ROWS])
         product(o01[:, 1, :], v_mx1, everything, w_mx, all_rows)
         product(o01[:, 0, :], v_mx0, everything, w_mx, all_rows)
-        outs = [o01[:, 0, :], o01[:, 1, :], bank(6, "o", [P, ROWS])[:], bank(7, "o", [P, ROWS])[:]]
         shared_gather(3, plane3)
         turned3 = turn(4, lambda u: got[3][:].bitcast(F32)[:, u::2])
-        v_grouped2 = group_values(2, turned2, PLANE3_AT)
+        v_mx2 = quantize("v2", v_grouped2[:], P, PLANE3_AT)
+        o2 = bank(6, "o2", [P, ROWS])
+        product(o2[:], v_mx2, everything, w_mx, all_rows)
 
         inp_mx = (tile("inp_codes", [P, ROWS], U32), tile("inp_scales", [P, ROWS], U8))
         inp_grouped = []
@@ -237,43 +239,45 @@ def tile_attend_gatedsoftmax_pl_kernel(tc, query, keys_words, keys_scales, size,
                 scales=inp_mx[1][:, halves[h]],
                 in_=inp_grouped[h][:].rearrange("p c j -> p (c j)"),
             )
-        v_mx2 = quantize("v2", v_grouped2[:], P, INP_AT + KB)
         v_mx3 = quantize("v3", v_grouped3[:], P)
-        gates = [tile("gate%d" % t, [P, ROWS], F32) for t in range(PACK)]
+        gates = [tile("gate%d" % b, [P, 2, ROWS], F32) for b in range(2)]
 
-        def gate_product(t, rows, number):
-            z = bank(number, "z", [P, rows.stop - rows.start])
-            product(z[:], g_mx[t // 2], halves[t % 2], inp_mx, rows)
-            return z
+        def gate(view, z_view):
+            nc.scalar.activation(out=view, in_=z_view, func=ACT.Tanh, scale=0.5)
 
-        def gate(t, rows, z_view):
-            nc.scalar.activation(out=gates[t][:, rows], in_=z_view, func=ACT.Tanh, scale=0.5)
-
-        for h, number in enumerate((0, 5)):
-            gate(0, halves[h], gate_product(0, halves[h], number)[:])
-        for t, number in ((1, 2), (2, 3)):
-            gate(t, all_rows, gate_product(t, all_rows, number)[:])
-        z3 = gate_product(3, all_rows, 4)
+        for t, number in enumerate((0, 5)):
+            z = bank(number, "z", [P, P])
+            product(z[:], g_mx[0], halves[t], inp_mx, halves[0])
+            gate(gates[0][:, t, halves[0]], z[:])
+        z01 = bank(2, "z", [P, 2, P])
+        for t in range(2):
+            product(z01[:, t, :], g_mx[0], halves[t], inp_mx, halves[1])
+        gate(gates[0][:, :, halves[1]], z01[:])
+        z2 = bank(3, "z", [P, ROWS])
+        product(z2[:], g_mx[1], halves[0], inp_mx, all_rows)
+        gate(gates[1][:, 0, :], z2[:])
+        z3 = bank(4, "z", [P, ROWS])
+        product(z3[:], g_mx[1], halves[1], inp_mx, all_rows)
         for rows in halves:
-            gate(3, rows, z3[:, rows])
-        product(outs[2], v_mx2, everything, w_mx, all_rows)
-        product(outs[3], v_mx3, everything, w_mx, all_rows)
+            gate(gates[1][:, 1, rows], z3[:, rows])
+        o3 = [bank(number, "o3", [P, P]) for number in (7, 0)]
+        for h, rows in enumerate(halves):
+            product(o3[h][:], v_mx3, everything, w_mx, rows)
 
         out_planes = out_0.rearrange("(p t) q -> p t q", t=PACK)
         y = [tile("y%d" % b, [P, 2, ROWS], F32) for b in range(2)]
 
-        def gated(t, rows):
-            nc.vector.scalar_tensor_tensor(
-                out=y[t // 2][:, t % 2, rows], in0=gates[t][:, rows], scalar=1.0, in1=outs[t][:, rows], op0=ALU.add, op1=ALU.mult
-            )
+        def gated(y_view, gate_view, o_view):
+            nc.vector.scalar_tensor_tensor(out=y_view, in0=gate_view, scalar=1.0, in1=o_view, op0=ALU.add, op1=ALU.mult)
 
         for t in range(2):
-            gated(t, all_rows)
+            gated(y[0][:, t, halves[0]], gates[0][:, t, halves[0]], o01[:, t, halves[0]])
+        gated(y[0][:, :, halves[1]], gates[0][:, :, halves[1]], o01[:, :, halves[1]])
         nc.sync.dma_start(out=out_planes[:, 0:2, :], in_=y[0][:])
-        gated(2, all_rows)
+        gated(y[1][:, 0, :], gates[1][:, 0, :], o2[:])
         nc.sync.dma_start(out=out_planes[:, 2, :], in_=y[1][:, 0, :])
-        for rows in halves:
-            gated(3, rows)
+        for h, rows in enumerate(halves):
+            gated(y[1][:, 1, rows], gates[1][:, 1, rows], o3[h][:])
         nc.sync.dma_start(out=out_planes[:, 3, :], in_=y[1][:, 1, :])
 
         y_grouped = tile("y_grouped", [P, ROWS, PACK], BF16)

@@ -28,6 +28,7 @@ PLANE3_AT = 3 * PLANE_BYTES
 INP_AT = 4 * PLANE_BYTES
 QUERY_CODES_AT = INP_AT + 4 * KB
 GROUPED_AT = QUERY_CODES_AT + 4 * KB
+GATE_AT = GROUPED_AT + 4 * KB
 SCALE_ROWS = 16
 VECTOR_SLOTS = 256
 
@@ -240,29 +241,21 @@ def tile_attend_gatedsoftmax_pl_kernel(tc, query, keys_words, keys_scales, size,
                 in_=inp_grouped[h][:].rearrange("p c j -> p (c j)"),
             )
         v_mx3 = quantize("v3", v_grouped3[:], P)
-        gates = [tile("gate%d" % b, [P, 2, ROWS], F32) for b in range(2)]
+        gates = [tile("gate0", [P, 2, ROWS], F32, GATE_AT), tile("gate1", [P, 2, ROWS], F32)]
 
         def gate(view, z_view):
             nc.scalar.activation(out=view, in_=z_view, func=ACT.Tanh, scale=0.5)
 
-        for t, number in enumerate((0, 5)):
-            z = bank(number, "z", [P, P])
-            product(z[:], g_mx[0], halves[t], inp_mx, halves[0])
-            gate(gates[0][:, t, halves[0]], z[:])
-        z01 = bank(2, "z", [P, 2, P])
-        for t in range(2):
-            product(z01[:, t, :], g_mx[0], halves[t], inp_mx, halves[1])
-        gate(gates[0][:, :, halves[1]], z01[:])
-        z2 = bank(3, "z", [P, ROWS])
-        product(z2[:], g_mx[1], halves[0], inp_mx, all_rows)
-        gate(gates[1][:, 0, :], z2[:])
-        z3 = bank(4, "z", [P, ROWS])
-        product(z3[:], g_mx[1], halves[1], inp_mx, all_rows)
-        for rows in halves:
-            gate(gates[1][:, 1, rows], z3[:, rows])
-        o3 = [bank(number, "o3", [P, P]) for number in (7, 0)]
-        for h, rows in enumerate(halves):
-            product(o3[h][:], v_mx3, everything, w_mx, rows)
+        pieces = [(2 * b + t, h) for b in range(2) for h in range(2) for t in range(2)]
+        free_banks = (0, 5, 2, 3, 4, 7)
+        for n, (t, h) in enumerate(pieces):
+            z = bank(free_banks[n % len(free_banks)], "z", [P, P])
+            product(z[:], g_mx[t // 2], halves[t % 2], inp_mx, halves[h])
+            gate(gates[t // 2][:, t % 2, halves[h]], z[:])
+        o3 = []
+        for h in range(2):
+            o3.append(bank(free_banks[2 + h], "o3", [P, P]))
+            product(o3[h][:], v_mx3, everything, w_mx, halves[h])
 
         out_planes = out_0.rearrange("(p t) q -> p t q", t=PACK)
         y = [tile("y%d" % b, [P, 2, ROWS], F32) for b in range(2)]
@@ -270,17 +263,16 @@ def tile_attend_gatedsoftmax_pl_kernel(tc, query, keys_words, keys_scales, size,
         def gated(y_view, gate_view, o_view):
             nc.vector.scalar_tensor_tensor(out=y_view, in0=gate_view, scalar=1.0, in1=o_view, op0=ALU.add, op1=ALU.mult)
 
-        for t in range(2):
-            gated(y[0][:, t, halves[0]], gates[0][:, t, halves[0]], o01[:, t, halves[0]])
-        gated(y[0][:, :, halves[1]], gates[0][:, :, halves[1]], o01[:, :, halves[1]])
-        nc.sync.dma_start(out=out_planes[:, 0:2, :], in_=y[0][:])
-        gated(y[1][:, 0, :], gates[1][:, 0, :], o2[:])
-        nc.sync.dma_start(out=out_planes[:, 2, :], in_=y[1][:, 0, :])
-        for h, rows in enumerate(halves):
-            gated(y[1][:, 1, rows], gates[1][:, 1, rows], o3[h][:])
-        nc.sync.dma_start(out=out_planes[:, 3, :], in_=y[1][:, 1, :])
+        for t, h in pieces:
+            rows = halves[h]
+            o_view = (o01[:, 0, rows], o01[:, 1, rows], o2[:, rows], o3[h][:])[t]
+            gated(y[t // 2][:, t % 2, rows], gates[t // 2][:, t % 2, rows], o_view)
+            if (t, h) == (1, 1):
+                nc.sync.dma_start(out=out_planes[:, 0:2, :], in_=y[0][:])
+            elif t >= 2 and h == 1:
+                nc.sync.dma_start(out=out_planes[:, t, :], in_=y[1][:, t - 2, :])
 
-        y_grouped = tile("y_grouped", [P, ROWS, PACK], BF16)
+        y_grouped = tile("y_grouped", [P, ROWS, PACK], BF16, GATE_AT)
         y_codes = tile("y_codes", [P, ROWS], U32)
         y_scales = tile("y_scales", [P, ROWS], U8)
         for b, copy in enumerate((nc.scalar.copy, nc.vector.tensor_copy)):

@@ -275,10 +275,11 @@ def tile_attend_gatedsoftmax_pl_kernel(tc, query, keys_words, keys_scales, size,
         y_grouped = tile("y_grouped", [P, ROWS, PACK], BF16, GATE_AT)
         y_codes = tile("y_codes", [P, ROWS], U32)
         y_scales = tile("y_scales", [P, ROWS], U8)
-        for b, copy in enumerate((nc.scalar.copy, nc.vector.tensor_copy)):
-            for rows in halves:
+        last_runs = [halves[0], slice(P, P + quarter), slice(P + quarter, ROWS)]
+        for b, (copy, runs) in enumerate(((nc.scalar.copy, halves), (nc.vector.tensor_copy, last_runs))):
+            for rows in runs:
                 interleave(copy, y_grouped[:, rows, 2 * b : 2 * b + 2], y[b][:, :, rows])
-        for rows in halves:
+        for rows in last_runs:
             nc.vector.quantize_mx(
                 out=y_codes[:, rows].bitcast(FP8X4),
                 scales=y_scales[:, rows],

from contextlib import ExitStack

import concourse.mybir as mybir
from concourse.masks import make_identity

F32 = mybir.dt.float32
BF16 = mybir.dt.bfloat16
I32 = mybir.dt.int32
U32 = mybir.dt.uint32
U16 = mybir.dt.uint16
U8 = mybir.dt.uint8
FP8X4 = mybir.dt.float8_e4m3fn_x4
FP4X4 = mybir.dt.float4_e2m1fn_x4
ALU = mybir.AluOpType
ACT = mybir.ActivationFunctionType

P = 128
PACK = 4
TOKENS = 2048
SLOTS = 512
ROWS = 256
FEATURES = 512
KB = 1024
PLANE_BYTES = TOKENS * 4
PAIR_AT = 0
PLANE2_AT = 2 * PLANE_BYTES
PLANE3_AT = 3 * PLANE_BYTES
INP_AT = 4 * PLANE_BYTES
QUERY_CODES_AT = INP_AT + 4 * KB
GROUPED_AT = QUERY_CODES_AT + 4 * KB
GATE_AT = GROUPED_AT + 4 * KB
SCALE_ROWS = 16
VECTOR_SLOTS = 256


FLOPS = 3 * 2 * 512 * 512 * 256


def interleave(copy, grouped, planes):
    copy(
        out=grouped.rearrange("p (c i) j -> p c j i", i=PACK),
        in_=planes.rearrange("p j (c i) -> p c j i", i=PACK),
    )


def tile_attend_gatedsoftmax_pl_kernel(tc, query, keys_words, keys_scales, size, vals, inp, wg, offs, out_0, out_1, out_2):
    nc = tc.nc
    with ExitStack() as ctx:
        sb = ctx.enter_context(tc.tile_pool(name="sb", bufs=1))
        placed = ctx.enter_context(tc.tile_pool(name="placed", bufs=1))
        ps = ctx.enter_context(tc.psum_pool(name="ps", bufs=1))

        def tile(name, shape, dtype, offset=None):
            if offset is None:
                return sb.tile(shape, dtype, name=name, align_bytes=256)
            return placed.tile(shape, dtype, name=name, align_bytes=256, offset=offset)

        def bank(number, name, shape):
            return ps.tile(shape, F32, name=name, tag="bank%d" % number)

        def quantize(name, grouped, width, offset=None):
            codes = tile(name + "_codes", [P, width], U32, offset)
            scales = tile(name + "_scales", [P, width], U8)
            nc.vector.quantize_mx(out=codes[:].bitcast(FP8X4), scales=scales[:], in_=grouped)
            return codes, scales

        def product(out, lhs, cols, rhs, rhs_cols, rhs_dtype=FP8X4):
            nc.tensor.matmul_mx(
                out=out,
                lhsT=lhs[0][:, cols].bitcast(FP8X4),
                lhsT_scale=lhs[1][:, cols],
                rhs=rhs[0][:, rhs_cols].bitcast(rhs_dtype),
                rhs_scale=rhs[1][:, rhs_cols],
                start=True,
                stop=True,
            )

        halves = [slice(h * P, (h + 1) * P) for h in range(2)]
        everything = slice(0, P)
        all_rows = slice(0, ROWS)

        key_words = tile("key_words", [P, TOKENS], U16)
        key_scales = tile("key_scales", [P, TOKENS], U8)
        first_scale_row = P - SCALE_ROWS
        offsets = sb.tile([P, SLOTS // 16], U16)
        nc.vector.memset(key_scales[0:first_scale_row, :].bitcast(I32), 0)
        size_rows = tile("size_rows", [P, P], F32, QUERY_CODES_AT + KB // 2)
        nc.vector.memset(size_rows[0 : P - PACK, :], 0.0)
        slot_scales = tile("slot_scales", [P, SLOTS], U8)
        nc.gpsimd.memset(slot_scales[:].bitcast(I32), 0)
        ident = tile("ident", [P, P], F32)
        make_identity(nc, ident[:])
        nc.sync.dma_start(offsets[:], offs)
        nc.scalar.dma_start(out=key_scales[first_scale_row:P, :].bitcast(I32), in_=keys_scales[0].bitcast(I32))
        nc.scalar.dma_start(out=size_rows[P - PACK : P, :], in_=size[0].rearrange("(r s) -> r s", r=PACK))
        nc.sync.dma_start(out=key_words[:].bitcast(I32), in_=keys_words[0].bitcast(I32))
        query_raw = tile("query_raw", [P, PACK, ROWS], F32)
        nc.sync.dma_start(out=query_raw[:], in_=query.rearrange("(p j) q -> p j q", j=PACK))
        wg_raw = tile("wg_raw", [P, PACK, FEATURES], F32)
        nc.sync.dma_start(out=wg_raw[:], in_=wg.rearrange("(p j) e -> p j e", j=PACK))
        got_scales = tile("got_scales", [P, SLOTS], U8)
        nc.vector.tensor_copy(got_scales[:], key_scales[:].indirect(offsets[:]))
        for quad in range(4):
            rows_at = first_scale_row + 4 * quad
            queue = nc.sync if quad % 2 == 0 else nc.scalar
            queue.dma_start(
                out=slot_scales[32 * quad : 32 * quad + 4, :].bitcast(I32),
                in_=got_scales[rows_at : rows_at + 4, :].bitcast(I32),
            )
        vals_rows = vals.rearrange("(m t) n -> m (t n)", t=PACK)
        pair = tile("vals01", [P, 2 * TOKENS], F32, PAIR_AT)
        nc.sync.dma_start(out=pair[:], in_=vals_rows[:, 0 : 2 * TOKENS])
        plane2 = tile("vals2", [P, TOKENS], F32, PLANE2_AT)
        nc.sync.dma_start(out=plane2[:], in_=vals_rows[:, 2 * TOKENS : 3 * TOKENS])
        plane3 = tile("vals3", [P, TOKENS], F32, PLANE3_AT)
        nc.sync.dma_start(out=plane3[:], in_=vals_rows[:, 3 * TOKENS : 4 * TOKENS])
        inp_raw = tile("inp_raw", [P, PACK, ROWS], F32, INP_AT)
        nc.sync.dma_start(out=inp_raw[:], in_=inp.rearrange("(p j) q -> p j q", j=PACK))

        size_turned = bank(4, "size_turned", [P, P])
        nc.tensor.transpose(size_turned[:], size_rows[:], ident[:])
        half_size = tile("half_size", [P, PACK], F32)
        nc.vector.tensor_scalar(
            out=half_size[:], in0=size_turned[:, P - PACK : P], scalar1=0.5, scalar2=0.0, op0=ALU.mult, op1=ALU.add
        )
        size_row = bank(2, "size_row", [P, SLOTS])
        for r in range(PACK):
            nc.tensor.transpose(size_row[:, r * P : (r + 1) * P], half_size[:, r : r + 1].to_broadcast([P, P]), ident[:])

        got_words = tile("got_words", [P, SLOTS], U16)
        nc.vector.tensor_copy(got_words[:], key_words[:].indirect(offsets[:]))
        query_grouped = tile("query_grouped", [P, ROWS, PACK], BF16, GROUPED_AT)
        interleave(nc.vector.tensor_copy, query_grouped[:], query_raw[:])
        q_mx = quantize("query", query_grouped[:].rearrange("p c j -> p (c j)"), ROWS, QUERY_CODES_AT + KB // 2)
        scores = []
        for h in range(2):
            scores.append(bank(h, "scores", [P, SLOTS]))
            product(scores[h][:], q_mx, halves[h], (got_words, slot_scales), slice(0, SLOTS), FP4X4)

        wg_grouped = [tile("wg_grouped%d" % b, [P, 2, P, PACK], BF16, GROUPED_AT + 2 * b * KB) for b in range(2)]

        def group_gate_weights(copy, b, ms):
            copy(
                out=wg_grouped[b][:].rearrange("p t m j -> p m j t")[:, ms],
                in_=wg_raw[:].rearrange("p j (m t) -> p m j t", t=PACK)[:, ms, :, 2 * b : 2 * b + 2],
            )

        group_gate_weights(nc.vector.tensor_copy, 0, everything)
        group_gate_weights(nc.scalar.copy, 1, everything)

        def quantize_pair(b, offset=None):
            return quantize("wg%d" % b, wg_grouped[b][:].rearrange("p t m j -> p (t m j)"), 2 * P, offset)

        g_mx = [quantize_pair(0)]

        neg_max, probs, sums = [], [], []
        for h in range(2):
            neg_max.append(tile("neg_max%d" % h, [P, 1], F32))
            nc.vector.tensor_reduce(out=neg_max[h][:], in_=scores[h][:], axis=mybir.AxisListType.X, op=ALU.max, negate=True)
        g_mx.append(quantize_pair(1, QUERY_CODES_AT))
        for h in range(2):
            probs.append(tile("probs%d" % h, [P, SLOTS], F32))
            sums.append(tile("sum%d" % h, [P, 1], F32))
            nc.scalar.activation(
                out=probs[h][:], in_=scores[h][:], func=ACT.Exp, bias=neg_max[h][:], scale=1.0, accum_out=sums[h][:]
            )
        w_turned = bank(3, "w_turned", [P, 2, 2, P])
        for h in range(2):
            inv = tile("inv%d" % h, [P, 1], F32)
            nc.vector.reciprocal(out=inv[:], in_=sums[h][:])
            w = tile("weights%d" % h, [P, SLOTS], BF16)
            nc.vector.scalar_tensor_tensor(
                out=w[:], in0=probs[h][:], scalar=inv[:], in1=size_row[:], op0=ALU.mult, op1=ALU.mult
            )
            for u in range(2):
                nc.tensor.transpose(w_turned[:, h, u, :], w[:].bitcast(F32)[:, u::2], ident[:])

        def sorted_words(got):
            return got[:].rearrange("p (u m e) -> p m u e", u=2, e=2)

        def turn(number, words_of):
            turned = bank(number, "turned", [P, 2, P])
            for u in range(2):
                nc.tensor.transpose(turned[:, u, :], words_of(u), ident[:])
            return turned

        def group_values(t, turned, offset=None):
            grouped = tile("v_grouped%d" % t, [P, P * PACK], BF16, offset)
            nc.scalar.copy(
                out=grouped[:].bitcast(F32).rearrange("p (m u) -> p m u", u=2),
                in_=turned[:].rearrange("p u m -> p m u"),
            )
            return grouped

        got = [tile("got%d" % t, [P, SLOTS], BF16) for t in range(PACK)]
        nc.vector.tensor_copy(sorted_words(got[1]), pair[:, TOKENS : 2 * TOKENS].indirect(offsets[:]))
        nc.scalar.activation(got[0][:], pair[:].indirect(offsets[:]), ACT.Copy)
        turned1 = turn(0, lambda u: got[1][:].bitcast(F32)[:, halves[u]])
        turned0 = turn(2, lambda u: got[0][:].bitcast(F32)[:, u::2])
        w_grouped = tile("w_grouped", [P, ROWS * PACK], BF16, PAIR_AT)
        nc.vector.tensor_copy(
            out=w_grouped[:].bitcast(F32).rearrange("p (h q u) -> p h q u", h=2, u=2),
            in_=w_turned[:].rearrange("p h u q -> p h q u"),
        )

        def shared_gather(t, plane):
            cut = VECTOR_SLOTS
            nc.vector.tensor_copy(got[t][:, 0:cut], plane[:].indirect(offsets[:, 0 : cut // 16]))
            nc.scalar.activation(got[t][:, cut:SLOTS], plane[:].indirect(offsets[:, cut // 16 : SLOTS // 16]), ACT.Copy)

        shared_gather(2, plane2)
        turned2 = turn(3, lambda u: got[2][:].bitcast(F32)[:, u::2])
        w_mx = quantize("w", w_grouped[:], ROWS, PLANE2_AT)
        v_grouped1 = group_values(1, turned1, PLANE2_AT + KB)
        v_grouped0 = group_values(0, turned0, PLANE2_AT + 2 * KB)
        v_grouped2 = group_values(2, turned2)
        v_mx1 = quantize("v1", v_grouped1[:], P)
        v_mx0 = quantize("v0", v_grouped0[:], P)
        o01 = bank(1, "o01", [P, 2, ROWS])
        product(o01[:, 1, :], v_mx1, everything, w_mx, all_rows)
        product(o01[:, 0, :], v_mx0, everything, w_mx, all_rows)
        shared_gather(3, plane3)
        turned3 = turn(4, lambda u: got[3][:].bitcast(F32)[:, u::2])
        v_mx2 = quantize("v2", v_grouped2[:], P, PLANE3_AT)
        o2 = bank(6, "o2", [P, ROWS])
        product(o2[:], v_mx2, everything, w_mx, all_rows)

        inp_mx = (tile("inp_codes", [P, ROWS], U32), tile("inp_scales", [P, ROWS], U8))
        inp_grouped = []
        for h in range(2):
            inp_grouped.append(tile("inp_grouped%d" % h, [P, P, PACK], BF16))
        quarter = P // 2
        interleave(nc.vector.tensor_copy, inp_grouped[0][:], inp_raw[:, :, halves[0]])
        interleave(nc.vector.tensor_copy, inp_grouped[1][:, 0:quarter, :], inp_raw[:, :, P : P + quarter])
        interleave(nc.scalar.copy, inp_grouped[1][:, quarter:P, :], inp_raw[:, :, P + quarter : ROWS])
        v_grouped3 = group_values(3, turned3, INP_AT)
        for h in range(2):
            nc.vector.quantize_mx(
                out=inp_mx[0][:, halves[h]].bitcast(FP8X4),
                scales=inp_mx[1][:, halves[h]],
                in_=inp_grouped[h][:].rearrange("p c j -> p (c j)"),
            )
        v_mx3 = quantize("v3", v_grouped3[:], P)
        gates = [tile("gate0", [P, 2, ROWS], F32, GATE_AT), tile("gate1", [P, 2, ROWS], F32)]

        def gate(view, z_view):
            nc.scalar.activation(out=view, in_=z_view, func=ACT.Tanh, scale=0.5)

        pieces = [(2 * b + t, h) for b in range(2) for h in range(2) for t in range(2)]
        free_banks = (0, 5, 2, 3, 4, 7)
        for n, (t, h) in enumerate(pieces):
            z = bank(free_banks[n % len(free_banks)], "z", [P, P])
            product(z[:], g_mx[t // 2], halves[t % 2], inp_mx, halves[h])
            gate(gates[t // 2][:, t % 2, halves[h]], z[:])
        o3 = []
        for h in range(2):
            o3.append(bank(free_banks[2 + h], "o3", [P, P]))
            product(o3[h][:], v_mx3, everything, w_mx, halves[h])

        out_planes = out_0.rearrange("(p t) q -> p t q", t=PACK)
        y = [tile("y%d" % b, [P, 2, ROWS], F32) for b in range(2)]

        def gated(y_view, gate_view, o_view):
            nc.vector.scalar_tensor_tensor(out=y_view, in0=gate_view, scalar=1.0, in1=o_view, op0=ALU.add, op1=ALU.mult)

        for t, h in pieces:
            rows = halves[h]
            o_view = (o01[:, 0, rows], o01[:, 1, rows], o2[:, rows], o3[h][:])[t]
            gated(y[t // 2][:, t % 2, rows], gates[t // 2][:, t % 2, rows], o_view)
            if (t, h) == (1, 1):
                nc.sync.dma_start(out=out_planes[:, 0:2, :], in_=y[0][:])
            elif t >= 2 and h == 1:
                nc.sync.dma_start(out=out_planes[:, t, :], in_=y[1][:, t - 2, :])

        y_grouped = tile("y_grouped", [P, ROWS, PACK], BF16, GATE_AT)
        y_codes = tile("y_codes", [P, ROWS], U32)
        y_scales = tile("y_scales", [P, ROWS], U8)
        last_runs = [halves[0], slice(P, P + quarter), slice(P + quarter, ROWS)]
        for b, (copy, runs) in enumerate(((nc.scalar.copy, halves), (nc.vector.tensor_copy, last_runs))):
            for rows in runs:
                interleave(copy, y_grouped[:, rows, 2 * b : 2 * b + 2], y[b][:, :, rows])
        for rows in last_runs:
            nc.vector.quantize_mx(
                out=y_codes[:, rows].bitcast(FP8X4),
                scales=y_scales[:, rows],
                in_=y_grouped[:, rows, :].rearrange("p c j -> p (c j)"),
            )
        nc.sync.dma_start(out=out_1[0].rearrange("p n t -> p (n t)").bitcast(I32), in_=y_codes[:].bitcast(I32))
        for r in range(4):
            queue = nc.scalar if r % 2 == 0 else nc.sync
            queue.dma_start(out=out_2[0, r:16:4, :].bitcast(I32), in_=y_scales[r:P:32, :].bitcast(I32))
